import numpy as np
import ml_dtypes


def mxq(x, axis, fmt="e4m3"):
    dtype, down = {"e4m3": (ml_dtypes.float8_e4m3fn, 7), "e5m2": (ml_dtypes.float8_e5m2, 14)}[fmt]
    v = np.moveaxis(np.asarray(x, np.float32).astype(ml_dtypes.bfloat16).astype(np.float64), axis, -1)
    blocks = v.reshape(v.shape[:-1] + (-1, 32))
    amax = np.abs(blocks).max(-1, keepdims=True)
    byte = np.maximum(np.where(amax > 0, np.frexp(amax)[1] - 1 + 127, 0) - down, 1)
    scale = np.exp2(byte - 127.0)
    codes = (blocks / scale).astype(np.float32).astype(dtype).astype(np.float64)
    return np.moveaxis((codes * scale).reshape(v.shape), -1, axis)


WIDE = False


def mx_kscale(k):
    if not WIDE:
        return np.ones(k)
    levels = np.array([10, -10, 5, -5, 0])
    if k % 512:
        return np.exp2(np.random.permutation(np.resize(levels, k // 32))).repeat(32)
    a = np.empty((k // 512, 16))
    for p in range(k // 512):
        a[p, :8] = np.random.permutation(np.resize(levels, 8))
        for g in range(8):
            far = levels[np.abs(levels - a[p, g]) >= 10]
            a[p, g + 8] = far[np.random.randint(len(far))]
    return np.exp2(a.ravel()).repeat(32)


def f64(x):
    return np.asarray(x).astype(np.float64)


def striped(idx):
    return np.tile(idx.reshape(-1, 16).T, (8, 1)).astype(np.uint16)


def unstriped(offs):
    return offs[:16].T.reshape(-1).astype(np.int64)


E2M1 = np.array([0.0, 0.5, 1.0, 1.5, 2.0, 3.0, 4.0, 6.0, -0.0, -0.5, -1.0, -1.5, -2.0, -3.0, -4.0, -6.0])


def pack_weight(w, fmt):
    k, n = w.shape
    w = f64(np.asarray(w, np.float32).astype(ml_dtypes.bfloat16)).reshape(k // 32, 32, n)
    amax = np.abs(w).max(1)
    if fmt == "e4m3":
        byte = np.frexp(amax)[1] - 1 + 127 - 7
    else:
        mant, ex = np.frexp(amax / 6.0)
        byte = np.where(mant > 0.5, ex, ex - 1) + 127
    byte = np.clip(np.where(amax > 0, byte, 1), 1, 254)
    scaled = (w * np.exp2(127.0 - byte)[:, None, :]).reshape(k, n).astype(np.float32)
    by_word = np.ascontiguousarray(scaled.reshape(k // 512, 128, 4, n).transpose(0, 1, 3, 2))
    if fmt == "e4m3":
        words = by_word.astype(ml_dtypes.float8_e4m3fn).view(np.uint8)
    else:
        c = by_word.astype(ml_dtypes.float4_e2m1fn).view(np.uint8) & 0xF
        words = (c[..., 0::2] | (c[..., 1::2] << 4)).reshape(k // 512, 128, 2 * n)
    return np.ascontiguousarray(words), np.ascontiguousarray(byte.astype(np.uint8).reshape(k // 512, 16, n))


def unpack_weight(words, scales, fmt):
    g, _, n = scales.shape
    words = np.ascontiguousarray(words).reshape(g, 128, n, -1)
    if fmt == "e4m3":
        vals = words.view(ml_dtypes.float8_e4m3fn).astype(np.float64)
    else:
        nib = np.empty((g, 128, n, 4), np.uint8)
        nib[..., 0::2] = words & 0xF
        nib[..., 1::2] = words >> 4
        vals = E2M1[nib]
    vals = vals * np.repeat(np.exp2(scales.astype(np.float64) - 127.0), 8, axis=1)[..., None]
    return vals.transpose(0, 1, 3, 2).reshape(g * 512, n)


K, T, E, C, N = 1536, 640, 4, 128, 512
K8 = 512


def by_expert(wq, xq):
    return np.concatenate([wq[e].T @ xq[:, e * C:(e + 1) * C] for e in range(E)], axis=1)


def setup_inputs():
    n = np.random.standard_normal
    s = mx_kscale(K)[:, None]
    w = n((E, K, N)) / np.sqrt(K) / s[None]
    w8 = [pack_weight(m[:K8], "e4m3") for m in w]
    w4 = [pack_weight(m[K8:], "e2m1") for m in w]
    return {
        "xT": (n((K, T)) * s).astype(np.float32),
        "xr": n((N, T)).astype(np.float32),
        "w8_words": np.stack([m[0] for m in w8]),
        "w8_scales": np.stack([m[1] for m in w8]),
        "w4_words": np.stack([m[0] for m in w4]),
        "w4_scales": np.stack([m[1] for m in w4]),
        "gate": np.tile(np.random.uniform(0.2, 1.0, E * C), (N, 1)).astype(np.float32),
        "offs": striped(np.random.permutation(T)[:E * C]),
    }


def reference(xT, xr, w8_words, w8_scales, w4_words, w4_scales, gate, offs):
    idx = unstriped(offs)
    w = np.stack([np.concatenate([unpack_weight(w8_words[e], w8_scales[e], "e4m3"), unpack_weight(w4_words[e], w4_scales[e], "e2m1")]) for e in range(E)])
    xq = mxq(f64(xT)[:, idx], 0, "e4m3")
    y = by_expert(w, xq)
    out = f64(xr).copy()
    out[:, idx] += f64(gate) * y
    return out

@@ -1,0 +1,219 @@
+from contextlib import ExitStack
+
+import concourse.mybir as mybir
+from concourse.masks import make_identity
+
+K, T, E, C, N = 1536, 640, 4, 128, 512
+P = 128
+S = E * C
+PASSES = 3
+NB = N // P
+WIDE = 704
+
+F32 = mybir.dt.float32
+BF16 = mybir.dt.bfloat16
+I32 = mybir.dt.int32
+U32 = mybir.dt.uint32
+U16 = mybir.dt.uint16
+U8 = mybir.dt.uint8
+FP8X4 = mybir.dt.float8_e4m3fn_x4
+FP4X4 = mybir.dt.float4_e2m1fn_x4
+COPY = mybir.ActivationFunctionType.Copy
+ADD = mybir.AluOpType.add
+
+FLOPS = 2 * K * N * S
+BYTES = 4 * K * T + 2 * 4 * N * T + E * 512 * N * 4 + E * 1024 * N // 2 + E * 48 * N + 4 * S + 2 * 128 * S // 16
+
+LOADS = (
+    ((0, 256, ((256, "v"),), (256,)), (256, 384, ((256, "v"), (128, "s")), (256, 128))),
+    ((0, 384, ((256, "s"), (128, "v")), (256, 128)), (384, 256, ((128, "s"), (128, "v")), (256,))),
+    ((0, 256, ((256, "s"),), (256,)), (256, 256, ((192, "v"), (64, "s")), (256,)), (512, 128, ((128, "s"),), (128,))),
+)
+
+
+def tile_moe_res_lin_none_kernel(tc, xT, xr, w8_words, w8_scales, w4_words, w4_scales, gate, offs, out):
+    nc = tc.nc
+    with ExitStack() as ctx:
+        keep = ctx.enter_context(tc.tile_pool(name="keep", bufs=1))
+        psum = ctx.enter_context(tc.psum_pool(name="psum", bufs=1))
+
+        offsets = keep.tile([P, S // 16], U16, name="offsets")
+        w8 = keep.tile([P, E, 4 * N], U8, name="w8", align_bytes=64)
+        w4 = keep.tile([P, 2 * E, 2 * N], U8, name="w4", align_bytes=64)
+        w8s = keep.tile([P, E, N], U8, name="w8s", align_bytes=64)
+        w4s = keep.tile([P, 2 * E, N], U8, name="w4s", align_bytes=64)
+        residual = keep.tile([P, NB, T], F32, name="residual")
+        gate_rows = keep.tile([P, P], F32, name="gate_rows")
+        gate_cols = keep.tile([P, E], F32, name="gate_cols")
+        ident = keep.tile([P, P], F32, name="ident")
+        windows = [keep.tile([P, T if b < 2 else WIDE], F32, name=f"window{b}") for b in range(NB)]
+        slot_y = [keep.tile([P, S], F32, name=f"slot_y{b}") for b in range(NB)]
+        results = [keep.tile([P, T], F32, name=f"result{b}") for b in range(NB)]
+        words = [keep.tile([P, T], U32, name=f"words{a}", align_bytes=64) for a in range(PASSES)]
+        scales = [keep.tile([P, T], U8, name=f"scales{a}", align_bytes=64) for a in range(2)]
+        slot_words = [keep.tile([P, S], U32, name=f"slot_words{a}", align_bytes=64) for a in range(PASSES)]
+        slot_scales = [keep.tile([P, S], U8, name=f"slot_scales{a}", align_bytes=64) for a in range(2)]
+        planes = ((0, 4), (0, 0), (1, 0))
+        warm = keep.tile([P, 1], F32, name="warm")
+
+        nc.vector.memset(warm[:], 0.0)
+        nc.scalar.copy(warm[:], warm[:])
+        for plane in scales:
+            nc.gpsimd.memset(plane[:].bitcast(I32), 0)
+        nc.gpsimd.memset(gate_rows[:], 0.0)
+        make_identity(nc, ident[:])
+        nc.vector.memset(w8s[:].rearrange("p e n -> p (e n)").bitcast(I32), 0)
+        nc.vector.memset(w4s[:].rearrange("p e n -> p (e n)").bitcast(I32), 0)
+        for b in range(NB):
+            nc.gpsimd.memset(windows[b][:], 0.0)
+
+        x_src = xT.rearrange("(a p j) t -> a p j t", a=PASSES, j=4)
+        raw = {}
+
+        def load_tokens(a, i):
+            t0, width, casts, pieces = LOADS[a][i]
+            tile = keep.tile([P, 4, width], F32, name=f"raw{a}_{i}")
+            nc.sync.dma_start(tile[:], x_src[a, :, :, t0 : t0 + width])
+            raw[a, i] = tile
+
+        def load_scales(src, dst):
+            rows = src.rearrange("e a q n -> q (e a) n").bitcast(I32)
+            for q in range(4):
+                nc.sync.dma_start(dst[32 * q : 32 * q + 4, :, :].bitcast(I32), rows[4 * q : 4 * q + 4])
+
+        load_tokens(0, 0)
+        nc.sync.dma_start(offsets[:], offs)
+        load_tokens(0, 1)
+        load_scales(w8_scales, w8s)
+        load_tokens(1, 0)
+        load_tokens(1, 1)
+        nc.sync.dma_start(gate_rows[0:E, :], gate[0:1, :].rearrange("o (e c) -> (o e) c", c=C))
+        load_scales(w4_scales, w4s)
+        load_tokens(2, 0)
+        load_tokens(2, 1)
+        load_tokens(2, 2)
+        w8_src = w8_words.rearrange("e a p n r -> p (e a) (n r)").bitcast(I32)
+        w4_src = w4_words.rearrange("e a p b -> p (e a) b").bitcast(I32)
+        for h in range(2):
+            nc.sync.dma_start(w8[:, 2 * h : 2 * h + 2, :].bitcast(I32), w8_src[:, 2 * h : 2 * h + 2, :])
+            nc.sync.dma_start(w4[:, 4 * h : 4 * h + 4, :].bitcast(I32), w4_src[:, 4 * h : 4 * h + 4, :])
+        xr_src = xr.rearrange("(b p) t -> p b t", p=P)
+        for h in range(2):
+            nc.sync.dma_start(residual[:, 2 * h : 2 * h + 2, :], xr_src[:, 2 * h : 2 * h + 2, :])
+
+        turned_gate = psum.tile([P, 2, 2 * C], F32, name="turned_gate", tag="turned", bufs=4)
+        nc.tensor.transpose(turned_gate[:, 0, 0:P], gate_rows[:], ident[:])
+        nc.scalar.copy(gate_cols[:], turned_gate[:, 0, 0:E])
+
+        def quantise_pass(a):
+            plane, row = planes[a]
+            staged = []
+            for i, (t0, width, casts, pieces) in enumerate(LOADS[a]):
+                grouped = keep.tile([P, width, 4], BF16, name=f"grouped{a}_{i}", align_bytes=64)
+                u0 = 0
+                for n, engine in casts:
+                    src = raw[a, i][:, :, u0 : u0 + n].rearrange("p j (c i) -> p c j i", i=4)
+                    dst = grouped[:, u0 : u0 + n, :].rearrange("p (c i) j -> p c j i", i=4)
+                    if engine == "v":
+                        nc.vector.tensor_copy(dst, src)
+                    else:
+                        nc.scalar.copy(dst, src)
+                    u0 += n
+                staged.append(grouped)
+            for grouped, (t0, width, casts, pieces) in zip(staged, LOADS[a]):
+                u0 = 0
+                for n in pieces:
+                    cols = slice(t0 + u0, t0 + u0 + n)
+                    nc.vector.quantize_mx(
+                        out=words[a][:, cols].bitcast(FP8X4),
+                        scales=scales[plane][row:P, cols],
+                        in_=grouped[:, u0 : u0 + n, :].rearrange("p t j -> p (t j)"),
+                    )
+                    u0 += n
+
+        def gather(table, slots, h):
+            cols = slice(h * S // 2, (h + 1) * S // 2)
+            part = offsets[:, h * S // 32 : (h + 1) * S // 32]
+            nc.vector.tensor_copy(slots[:, cols], table[:].indirect(part))
+
+        def gather_words(a, h):
+            gather(words[a], slot_words[a], h)
+
+        def gather_scales(i, h):
+            gather(scales[i], slot_scales[i], h)
+
+        banks = [psum.tile([P, N], F32, name=f"bank{e}") for e in range(E)]
+
+        def multiply(a, e):
+            cols = slice(e * C, (e + 1) * C)
+            if a == 0:
+                rhs, rhs_scale = w8[:, e, :].bitcast(FP8X4), w8s[:, e, :]
+            else:
+                rhs, rhs_scale = w4[:, 2 * e + a - 1, :].bitcast(FP4X4), w4s[:, 2 * e + a - 1, :]
+            nc.tensor.matmul_mx(
+                out=banks[e][:],
+                lhsT=slot_words[a][:, cols].bitcast(FP8X4),
+                lhsT_scale=slot_scales[planes[a][0]][planes[a][1] : P, cols],
+                rhs=rhs,
+                rhs_scale=rhs_scale,
+                start=(a == 0),
+                stop=(a == PASSES - 1),
+            )
+
+        def turn(h):
+            for half in range(2):
+                turned = psum.tile([P, 2, 2 * C], F32, name=f"turned{h}{half}", tag="turned", bufs=4)
+                for i in range(2):
+                    e = 2 * h + i
+                    gated = keep.tile([P, 2 * P], F32, name=f"gated{e}{half}")
+                    nc.scalar.activation(gated[:], banks[e][:, half * 2 * P : (half + 1) * 2 * P], COPY, scale=gate_cols[:, e : e + 1])
+                    for b in range(2):
+                        nc.tensor.transpose(turned[:, b, i * C : (i + 1) * C], gated[:, b * P : (b + 1) * P], ident[:])
+                for b in range(2):
+                    nc.scalar.copy(slot_y[2 * half + b][:, 2 * h * C : 2 * (h + 1) * C], turned[:, b, :])
+
+        def scatter(b, h):
+            part = offsets[:, h * S // 32 : (h + 1) * S // 32]
+            nc.vector.tensor_copy(windows[b][:].indirect(part), slot_y[b][:, 2 * h * C : 2 * (h + 1) * C])
+
+        def scatter_all(b):
+            nc.vector.tensor_copy(windows[b][:].indirect(offsets[:]), slot_y[b][:])
+
+        def finish(b, engine, parts):
+            for i in range(parts):
+                cols = slice(i * T // parts, (i + 1) * T // parts)
+                engine.tensor_tensor(results[b][:, cols], windows[b][:, cols], residual[:, b, cols], ADD)
+                nc.sync.dma_start(out[b * P : (b + 1) * P, cols], results[b][:, cols])
+
+        quantise_pass(0)
+        gather_words(0, 0)
+        gather_words(0, 1)
+        quantise_pass(1)
+        gather_words(1, 0)
+        gather_scales(0, 0)
+        quantise_pass(2)
+        gather_words(2, 0)
+        gather_scales(1, 0)
+        for e in (0, 1):
+            for a in range(PASSES):
+                multiply(a, e)
+        gather_words(1, 1)
+        gather_scales(0, 1)
+        turn(0)
+        gather_words(2, 1)
+        gather_scales(1, 1)
+        for e in (2, 3):
+            for a in range(PASSES):
+                multiply(a, e)
+        turn(1)
+
+        scatter(0, 0)
+        scatter(1, 0)
+        scatter(0, 1)
+        finish(0, nc.gpsimd, 1)
+        scatter(1, 1)
+        finish(1, nc.gpsimd, 1)
+        scatter_all(2)
+        finish(2, nc.gpsimd, 1)
+        scatter_all(3)
+        finish(3, nc.vector, 2)

@@ -24,11 +24,15 @@ ADD = mybir.AluOpType.add
 FLOPS = 2 * K * N * S
 BYTES = 4 * K * T + 2 * 4 * N * T + E * 512 * N * 4 + E * 1024 * N // 2 + E * 48 * N + 4 * S + 2 * 128 * S // 16
 
-LOADS = (
-    ((0, 256, ((256, "v"),), (256,)), (256, 384, ((256, "v"), (128, "s")), (256, 128))),
-    ((0, 384, ((256, "s"), (128, "v")), (256, 128)), (384, 256, ((128, "s"), (128, "v")), (256,))),
-    ((0, 256, ((256, "s"),), (256,)), (256, 256, ((192, "v"), (64, "s")), (256,)), (512, 128, ((128, "s"),), (128,))),
-)
+ORDER = (1, 0, 2)
+PIECES = ((0, 256), (256, 256), (512, 128))
+CASTS = {
+    1: ((0, 2, 0, "s"), (0, 2, 1, "v"), (0, 2, 2, "s"), (2, 4, 0, "s"), (2, 4, 1, "v"), (2, 4, 2, "v")),
+    0: ((0, 2, 0, "s"), (0, 2, 1, "s"), (0, 2, 2, "s"), (2, 4, 0, "v"), (2, 4, 1, "s"), (2, 4, 2, "s")),
+    2: ((0, 2, 1, "s"), (0, 2, 2, "s"), (0, 4, 0, "v"), (2, 4, 1, "s"), (2, 4, 2, "v")),
+}
+QUANT = {1: (1, 2, 0), 0: (0, 1, 2), 2: (0, 2, 1)}
+PLANES = {1: (0, 0), 0: (1, 4), 2: (1, 0)}
 
 
 def tile_moe_res_lin_none_kernel(tc, xT, xr, w8_words, w8_scales, w4_words, w4_scales, gate, offs, out):
@@ -40,180 +44,195 @@ def tile_moe_res_lin_none_kernel(tc, xT, xr, w8_words, w8_scales, w4_words, w4_s
         offsets = keep.tile([P, S // 16], U16, name="offsets")
         w8 = keep.tile([P, E, 4 * N], U8, name="w8", align_bytes=64)
         w4 = keep.tile([P, 2 * E, 2 * N], U8, name="w4", align_bytes=64)
-        w8s = keep.tile([P, E, N], U8, name="w8s", align_bytes=64)
-        w4s = keep.tile([P, 2 * E, N], U8, name="w4s", align_bytes=64)
+        w_scales = [keep.tile([P, 2, 2, N], U8, name=f"w_scales{h}", align_bytes=64) for h in range(2)]
         residual = keep.tile([P, NB, T], F32, name="residual")
         gate_rows = keep.tile([P, P], F32, name="gate_rows")
         gate_cols = keep.tile([P, E], F32, name="gate_cols")
         ident = keep.tile([P, P], F32, name="ident")
-        windows = [keep.tile([P, T if b < 2 else WIDE], F32, name=f"window{b}") for b in range(NB)]
+        windows = [keep.tile([P, WIDE], F32, name=f"window{b}") for b in range(3)]
         slot_y = [keep.tile([P, S], F32, name=f"slot_y{b}") for b in range(NB)]
         results = [keep.tile([P, T], F32, name=f"result{b}") for b in range(NB)]
         words = [keep.tile([P, T], U32, name=f"words{a}", align_bytes=64) for a in range(PASSES)]
         scales = [keep.tile([P, T], U8, name=f"scales{a}", align_bytes=64) for a in range(2)]
         slot_words = [keep.tile([P, S], U32, name=f"slot_words{a}", align_bytes=64) for a in range(PASSES)]
         slot_scales = [keep.tile([P, S], U8, name=f"slot_scales{a}", align_bytes=64) for a in range(2)]
-        planes = ((0, 4), (0, 0), (1, 0))
         warm = keep.tile([P, 1], F32, name="warm")
 
         nc.vector.memset(warm[:], 0.0)
         nc.scalar.copy(warm[:], warm[:])
-        for plane in scales:
-            nc.gpsimd.memset(plane[:].bitcast(I32), 0)
         nc.gpsimd.memset(gate_rows[:], 0.0)
         make_identity(nc, ident[:])
-        nc.vector.memset(w8s[:].rearrange("p e n -> p (e n)").bitcast(I32), 0)
-        nc.vector.memset(w4s[:].rearrange("p e n -> p (e n)").bitcast(I32), 0)
-        for b in range(NB):
-            nc.gpsimd.memset(windows[b][:], 0.0)
+        for plane in scales:
+            nc.vector.memset(plane[:].bitcast(I32), 0)
+        for plane in w_scales:
+            nc.vector.memset(plane[:].rearrange("p e a n -> p (e a n)").bitcast(I32), 0)
+        for window in windows:
+            nc.gpsimd.memset(window[:], 0.0)
 
-        x_src = xT.rearrange("(a p j) t -> a p j t", a=PASSES, j=4)
-        raw = {}
+        x_src = xT.rearrange("(a p u j) t -> a u p (j t)", a=PASSES, u=2, j=2)
+        raw = [keep.tile([P, 4 * T], F32, name=f"raw{a}") for a in range(PASSES)]
 
-        def load_tokens(a, i):
-            t0, width, casts, pieces = LOADS[a][i]
-            tile = keep.tile([P, 4, width], F32, name=f"raw{a}_{i}")
-            nc.sync.dma_start(tile[:], x_src[a, :, :, t0 : t0 + width])
-            raw[a, i] = tile
+        def load_tokens(a, u):
+            nc.sync.dma_start(raw[a][:, 2 * T * u : 2 * T * (u + 1)], x_src[a, u])
 
-        def load_scales(src, dst):
-            rows = src.rearrange("e a q n -> q (e a) n").bitcast(I32)
-            for q in range(4):
-                nc.sync.dma_start(dst[32 * q : 32 * q + 4, :, :].bitcast(I32), rows[4 * q : 4 * q + 4])
-
-        load_tokens(0, 0)
-        nc.sync.dma_start(offsets[:], offs)
-        load_tokens(0, 1)
-        load_scales(w8_scales, w8s)
-        load_tokens(1, 0)
-        load_tokens(1, 1)
-        nc.sync.dma_start(gate_rows[0:E, :], gate[0:1, :].rearrange("o (e c) -> (o e) c", c=C))
-        load_scales(w4_scales, w4s)
-        load_tokens(2, 0)
-        load_tokens(2, 1)
-        load_tokens(2, 2)
         w8_src = w8_words.rearrange("e a p n r -> p (e a) (n r)").bitcast(I32)
         w4_src = w4_words.rearrange("e a p b -> p (e a) b").bitcast(I32)
-        for h in range(2):
-            nc.sync.dma_start(w8[:, 2 * h : 2 * h + 2, :].bitcast(I32), w8_src[:, 2 * h : 2 * h + 2, :])
-            nc.sync.dma_start(w4[:, 4 * h : 4 * h + 4, :].bitcast(I32), w4_src[:, 4 * h : 4 * h + 4, :])
+        w8s_src = w8_scales.rearrange("e a (q r) n -> r q (e a) n", r=4).bitcast(I32)
+        w4s_src = w4_scales.rearrange("e a (q r) n -> r q (e a) n", r=4).bitcast(I32)
+
+        def load_w8(e0, e1):
+            nc.sync.dma_start(w8[:, e0:e1, :].bitcast(I32), w8_src[:, e0:e1, :])
+
+        def load_w4(e0, e1):
+            nc.sync.dma_start(w4[:, 2 * e0 : 2 * e1, :].bitcast(I32), w4_src[:, 2 * e0 : 2 * e1, :])
+
+        def load_w8_scales(e0, e1):
+            for r in range(4):
+                nc.sync.dma_start(w_scales[e0 // 2][4 + r : P : 32, :, 0, :].bitcast(I32), w8s_src[r, :, e0:e1, :])
+
+        def load_w4_scales(e0, e1):
+            for r in range(4):
+                dst = w_scales[e0 // 2][r:P:32, :, :, :].rearrange("q e a n -> q (e a) n")
+                nc.sync.dma_start(dst.bitcast(I32), w4s_src[r, :, 2 * e0 : 2 * e1, :])
+
+        load_tokens(ORDER[0], 0)
+        load_tokens(ORDER[0], 1)
+        nc.sync.dma_start(offsets[:], offs)
+        nc.sync.dma_start(gate_rows[0:E, :], gate[0:1, :].rearrange("o (e c) -> (o e) c", c=C))
+        for a in ORDER[1:]:
+            for u in range(2):
+                load_tokens(a, u)
+        load_w8_scales(0, 2)
+        load_w4(0, 1)
+        load_w8(0, 1)
+        load_w4_scales(0, 2)
+        load_w4(1, 2)
+        load_w8(1, 2)
+        load_w8_scales(2, 4)
+        load_w4(2, 4)
+        load_w8(2, 4)
+        load_w4_scales(2, 4)
         xr_src = xr.rearrange("(b p) t -> p b t", p=P)
         for h in range(2):
             nc.sync.dma_start(residual[:, 2 * h : 2 * h + 2, :], xr_src[:, 2 * h : 2 * h + 2, :])
 
-        turned_gate = psum.tile([P, 2, 2 * C], F32, name="turned_gate", tag="turned", bufs=4)
-        nc.tensor.transpose(turned_gate[:, 0, 0:P], gate_rows[:], ident[:])
-        nc.scalar.copy(gate_cols[:], turned_gate[:, 0, 0:E])
+        turned_gate = psum.tile([P, N], F32, name="turned_gate", tag="turned", bufs=3)
+        nc.tensor.transpose(turned_gate[:, 0:P], gate_rows[:], ident[:])
+        nc.scalar.copy(gate_cols[:], turned_gate[:, 0:E])
 
         def quantise_pass(a):
-            plane, row = planes[a]
-            staged = []
-            for i, (t0, width, casts, pieces) in enumerate(LOADS[a]):
-                grouped = keep.tile([P, width, 4], BF16, name=f"grouped{a}_{i}", align_bytes=64)
-                u0 = 0
-                for n, engine in casts:
-                    src = raw[a, i][:, :, u0 : u0 + n].rearrange("p j (c i) -> p c j i", i=4)
-                    dst = grouped[:, u0 : u0 + n, :].rearrange("p (c i) j -> p c j i", i=4)
-                    if engine == "v":
-                        nc.vector.tensor_copy(dst, src)
-                    else:
-                        nc.scalar.copy(dst, src)
-                    u0 += n
-                staged.append(grouped)
-            for grouped, (t0, width, casts, pieces) in zip(staged, LOADS[a]):
-                u0 = 0
-                for n in pieces:
-                    cols = slice(t0 + u0, t0 + u0 + n)
-                    nc.vector.quantize_mx(
-                        out=words[a][:, cols].bitcast(FP8X4),
-                        scales=scales[plane][row:P, cols],
-                        in_=grouped[:, u0 : u0 + n, :].rearrange("p t j -> p (t j)"),
-                    )
-                    u0 += n
+            plane, row = PLANES[a]
+            grouped = [keep.tile([P, n, 4], BF16, name=f"grouped{a}_{t0}", align_bytes=64) for t0, n in PIECES]
+            rows = raw[a][:].rearrange("p (j t) -> p j t", j=4)
+            for j0, j1, piece, engine in CASTS[a]:
+                t0, n = PIECES[piece]
+                src = rows[:, j0:j1, t0 : t0 + n].rearrange("p j (c i) -> p c j i", i=4)
+                dst = grouped[piece][:, :, j0:j1].rearrange("p (c i) j -> p c j i", i=4)
+                if engine == "v":
+                    nc.vector.tensor_copy(dst, src)
+                else:
+                    nc.scalar.copy(dst, src)
+            for piece in QUANT[a]:
+                tile, (t0, n) = grouped[piece], PIECES[piece]
+                nc.vector.quantize_mx(
+                    out=words[a][:, t0 : t0 + n].bitcast(FP8X4),
+                    scales=scales[plane][row:P, t0 : t0 + n],
+                    in_=tile[:].rearrange("p t j -> p (t j)"),
+                )
 
-        def gather(table, slots, h):
-            cols = slice(h * S // 2, (h + 1) * S // 2)
-            part = offsets[:, h * S // 32 : (h + 1) * S // 32]
-            nc.vector.tensor_copy(slots[:, cols], table[:].indirect(part))
+        def listed(e0, e1):
+            return offsets[:, e0 * C // 16 : e1 * C // 16]
 
-        def gather_words(a, h):
-            gather(words[a], slot_words[a], h)
+        def gather(table, slots, e0, e1):
+            nc.vector.tensor_copy(slots[:, e0 * C : e1 * C], table[:].indirect(listed(e0, e1)))
 
-        def gather_scales(i, h):
-            gather(scales[i], slot_scales[i], h)
-
+        first_bank = psum.tile([P, N], F32, name="first_bank")
         banks = [psum.tile([P, N], F32, name=f"bank{e}") for e in range(E)]
+        gated = {}
 
-        def multiply(a, e):
+        def sums(e, b0, b1):
+            return first_bank[:, 0:P] if (e, b0) == (0, 0) else banks[e][:, b0 * P : b1 * P]
+
+        def multiply(e, b0, b1):
             cols = slice(e * C, (e + 1) * C)
-            if a == 0:
-                rhs, rhs_scale = w8[:, e, :].bitcast(FP8X4), w8s[:, e, :]
-            else:
-                rhs, rhs_scale = w4[:, 2 * e + a - 1, :].bitcast(FP4X4), w4s[:, 2 * e + a - 1, :]
-            nc.tensor.matmul_mx(
-                out=banks[e][:],
-                lhsT=slot_words[a][:, cols].bitcast(FP8X4),
-                lhsT_scale=slot_scales[planes[a][0]][planes[a][1] : P, cols],
-                rhs=rhs,
-                rhs_scale=rhs_scale,
-                start=(a == 0),
-                stop=(a == PASSES - 1),
-            )
+            n0, n1 = b0 * P, b1 * P
+            for a in ORDER:
+                plane, row = PLANES[a]
+                if a == 0:
+                    rhs, rhs_scale = w8[:, e, 4 * n0 : 4 * n1].bitcast(FP8X4), w_scales[e // 2][4:P, e % 2, 0, n0:n1]
+                else:
+                    rhs, rhs_scale = w4[:, 2 * e + a - 1, 2 * n0 : 2 * n1].bitcast(FP4X4), w_scales[e // 2][:, e % 2, a - 1, n0:n1]
+                nc.tensor.matmul_mx(
+                    out=sums(e, b0, b1),
+                    lhsT=slot_words[a][:, cols].bitcast(FP8X4),
+                    lhsT_scale=slot_scales[plane][row:P, cols],
+                    rhs=rhs,
+                    rhs_scale=rhs_scale,
+                    start=(a == ORDER[0]),
+                    stop=(a == ORDER[-1]),
+                )
 
-        def turn(h):
-            for half in range(2):
-                turned = psum.tile([P, 2, 2 * C], F32, name=f"turned{h}{half}", tag="turned", bufs=4)
-                for i in range(2):
-                    e = 2 * h + i
-                    gated = keep.tile([P, 2 * P], F32, name=f"gated{e}{half}")
-                    nc.scalar.activation(gated[:], banks[e][:, half * 2 * P : (half + 1) * 2 * P], COPY, scale=gate_cols[:, e : e + 1])
-                    for b in range(2):
-                        nc.tensor.transpose(turned[:, b, i * C : (i + 1) * C], gated[:, b * P : (b + 1) * P], ident[:])
-                for b in range(2):
-                    nc.scalar.copy(slot_y[2 * half + b][:, 2 * h * C : 2 * (h + 1) * C], turned[:, b, :])
+        def weigh(e, b0, b1):
+            tile = keep.tile([P, (b1 - b0) * P], F32, name=f"gated{e}{b0}")
+            nc.scalar.activation(tile[:], sums(e, b0, b1), COPY, scale=gate_cols[:, e : e + 1])
+            for b in range(b0, b1):
+                gated[e, b] = tile[:, (b - b0) * P : (b - b0 + 1) * P]
 
-        def scatter(b, h):
-            part = offsets[:, h * S // 32 : (h + 1) * S // 32]
-            nc.vector.tensor_copy(windows[b][:].indirect(part), slot_y[b][:, 2 * h * C : 2 * (h + 1) * C])
+        def turn(b, e0, e1):
+            turned = psum.tile([P, N], F32, name=f"turned{b}{e0}", tag="turned", bufs=3)
+            for e in range(e0, e1):
+                nc.tensor.transpose(turned[:, (e - e0) * C : (e - e0 + 1) * C], gated[e, b], ident[:])
+            nc.scalar.copy(slot_y[b][:, e0 * C : e1 * C], turned[:, 0 : (e1 - e0) * C])
 
-        def scatter_all(b):
-            nc.vector.tensor_copy(windows[b][:].indirect(offsets[:]), slot_y[b][:])
+        def scatter(b, e0, e1):
+            nc.vector.tensor_copy(windows[b % 3][:].indirect(listed(e0, e1)), slot_y[b][:, e0 * C : e1 * C])
 
         def finish(b, engine, parts):
             for i in range(parts):
                 cols = slice(i * T // parts, (i + 1) * T // parts)
-                engine.tensor_tensor(results[b][:, cols], windows[b][:, cols], residual[:, b, cols], ADD)
+                engine.tensor_tensor(results[b][:, cols], windows[b % 3][:, cols], residual[:, b, cols], ADD)
                 nc.sync.dma_start(out[b * P : (b + 1) * P, cols], results[b][:, cols])
 
-        quantise_pass(0)
-        gather_words(0, 0)
-        gather_words(0, 1)
         quantise_pass(1)
-        gather_words(1, 0)
-        gather_scales(0, 0)
+        for h in range(2):
+            gather(words[1], slot_words[1], 2 * h, 2 * h + 2)
+            gather(scales[0], slot_scales[0], 2 * h, 2 * h + 2)
+        quantise_pass(0)
+        for h in range(2):
+            gather(words[0], slot_words[0], 2 * h, 2 * h + 2)
         quantise_pass(2)
-        gather_words(2, 0)
-        gather_scales(1, 0)
-        for e in (0, 1):
-            for a in range(PASSES):
-                multiply(a, e)
-        gather_words(1, 1)
-        gather_scales(0, 1)
-        turn(0)
-        gather_words(2, 1)
-        gather_scales(1, 1)
+        for e0, e1 in ((0, 1), (1, 2), (2, 4)):
+            gather(scales[1], slot_scales[1], e0, e1)
+            gather(words[2], slot_words[2], e0, e1)
+        for b in range(3):
+            multiply(0, b, b + 1)
+            weigh(0, b, b + 1)
+            turn(b, 0, 1)
+        multiply(1, 0, NB)
+        weigh(1, 0, 2)
+        turn(0, 1, 2)
+        turn(1, 1, 2)
+        multiply(0, 3, 4)
         for e in (2, 3):
-            for a in range(PASSES):
-                multiply(a, e)
-        turn(1)
+            multiply(e, 0, NB)
+            weigh(e, 0, 2)
+        turn(0, 2, 4)
+        turn(1, 2, 4)
+        for e in (1, 2, 3):
+            weigh(e, 2, 4)
+        weigh(0, 3, 4)
+        turn(2, 1, 4)
+        turn(3, 0, 4)
 
-        scatter(0, 0)
-        scatter(1, 0)
-        scatter(0, 1)
+        for b in range(3):
+            scatter(b, 0, 1)
+        scatter(0, 1, 2)
+        scatter(1, 1, 2)
+        scatter(0, 2, 4)
         finish(0, nc.gpsimd, 1)
-        scatter(1, 1)
+        scatter(1, 2, 4)
         finish(1, nc.gpsimd, 1)
-        scatter_all(2)
+        scatter(2, 1, 4)
         finish(2, nc.gpsimd, 1)
-        scatter_all(3)
+        scatter(3, 0, 4)
         finish(3, nc.vector, 2)

@@ -25,13 +25,15 @@ FLOPS = 2 * K * N * S
 BYTES = 4 * K * T + 2 * 4 * N * T + E * 512 * N * 4 + E * 1024 * N // 2 + E * 48 * N + 4 * S + 2 * 128 * S // 16
 
 ORDER = (1, 0, 2)
-PIECES = ((0, 256), (256, 256), (512, 128))
+PIECES = ((0, 256), (256, 128), (384, 256))
 CASTS = {
-    1: ((0, 2, 0, "s"), (0, 2, 1, "v"), (0, 2, 2, "s"), (2, 4, 0, "s"), (2, 4, 1, "v"), (2, 4, 2, "v")),
-    0: ((0, 2, 0, "s"), (0, 2, 1, "s"), (0, 2, 2, "s"), (2, 4, 0, "v"), (2, 4, 1, "s"), (2, 4, 2, "s")),
-    2: ((0, 2, 1, "s"), (0, 2, 2, "s"), (0, 4, 0, "v"), (2, 4, 1, "s"), (2, 4, 2, "v")),
+    1: ((0, 2, 0, 0, 256, "v"), (0, 2, 2, 0, 256, "s"), (0, 2, 1, 0, 128, "v"), (2, 4, 0, 0, 256, "v"), (2, 4, 1, 0, 128, "s"),
+        (2, 4, 2, 0, 128, "s"), (2, 4, 2, 128, 256, "v")),
+    0: ((0, 2, 0, 0, 256, "s"), (0, 2, 1, 0, 128, "s"), (2, 4, 0, 0, 256, "s"), (2, 4, 1, 0, 128, "s"), (0, 4, 2, 0, 256, "v")),
+    2: ((0, 2, 0, 0, 256, "s"), (0, 2, 2, 0, 256, "s"), (2, 4, 0, 0, 256, "s"), (0, 4, 1, 0, 128, "v"),
+        (2, 4, 2, 0, 128, "s"), (2, 4, 2, 128, 256, "v")),
 }
-QUANT = {1: (1, 2, 0), 0: (0, 1, 2), 2: (0, 2, 1)}
+QUANT = {1: (0, 1, 2), 0: (0, 1, 2), 2: (1, 0, 2)}
 PLANES = {1: (0, 0), 0: (1, 4), 2: (1, 0)}
 
 
@@ -49,12 +51,12 @@ def tile_moe_res_lin_none_kernel(tc, xT, xr, w8_words, w8_scales, w4_words, w4_s
         gate_rows = keep.tile([P, P], F32, name="gate_rows")
         gate_cols = keep.tile([P, E], F32, name="gate_cols")
         ident = keep.tile([P, P], F32, name="ident")
-        windows = [keep.tile([P, WIDE], F32, name=f"window{b}") for b in range(3)]
+        windows = [keep.tile([P, T], F32, name=f"window{b}") for b in range(2)]
         slot_y = [keep.tile([P, S], F32, name=f"slot_y{b}") for b in range(NB)]
         results = [keep.tile([P, T], F32, name=f"result{b}") for b in range(NB)]
-        words = [keep.tile([P, T], U32, name=f"words{a}", align_bytes=64) for a in range(PASSES)]
-        scales = [keep.tile([P, T], U8, name=f"scales{a}", align_bytes=64) for a in range(2)]
-        slot_words = [keep.tile([P, S], U32, name=f"slot_words{a}", align_bytes=64) for a in range(PASSES)]
+        words = [keep.tile([P, WIDE if a == 1 else T], U32, name=f"words{a}", align_bytes=64) for a in range(PASSES)]
+        scales = [keep.tile([P, WIDE if a == 0 else T], U8, name=f"scales{a}", align_bytes=64) for a in range(2)]
+        slot_words = [keep.tile([P, S if a else S // 2], U32, name=f"slot_words{a}", align_bytes=64) for a in range(PASSES)]
         slot_scales = [keep.tile([P, S], U8, name=f"slot_scales{a}", align_bytes=64) for a in range(2)]
         warm = keep.tile([P, 1], F32, name="warm")
 
@@ -64,10 +66,12 @@ def tile_moe_res_lin_none_kernel(tc, xT, xr, w8_words, w8_scales, w4_words, w4_s
         make_identity(nc, ident[:])
         for plane in scales:
             nc.vector.memset(plane[:].bitcast(I32), 0)
+        for table in words[1:2]:
+            nc.vector.memset(table[:, T:WIDE].bitcast(I32), 0)
         for plane in w_scales:
             nc.vector.memset(plane[:].rearrange("p e a n -> p (e a n)").bitcast(I32), 0)
         for window in windows:
-            nc.gpsimd.memset(window[:], 0.0)
+            nc.vector.memset(window[:], 0.0)
 
         x_src = xT.rearrange("(a p u j) t -> a u p (j t)", a=PASSES, u=2, j=2)
         raw = [keep.tile([P, 4 * T], F32, name=f"raw{a}") for a in range(PASSES)]
@@ -96,7 +100,9 @@ def tile_moe_res_lin_none_kernel(tc, xT, xr, w8_words, w8_scales, w4_words, w4_s
                 nc.sync.dma_start(dst.bitcast(I32), w4s_src[r, :, 2 * e0 : 2 * e1, :])
 
         load_tokens(ORDER[0], 0)
-        load_tokens(ORDER[0], 1)
+        for t0, t1 in ((0, 384), (384, T)):
+            dst = raw[ORDER[0]][:, 2 * T : 4 * T].rearrange("p (j t) -> p j t", j=2)
+            nc.sync.dma_start(dst[:, :, t0:t1], x_src[ORDER[0], 1].rearrange("p (j t) -> p j t", j=2)[:, :, t0:t1])
         nc.sync.dma_start(offsets[:], offs)
         nc.sync.dma_start(gate_rows[0:E, :], gate[0:1, :].rearrange("o (e c) -> (o e) c", c=C))
         for a in ORDER[1:]:
@@ -124,10 +130,10 @@ def tile_moe_res_lin_none_kernel(tc, xT, xr, w8_words, w8_scales, w4_words, w4_s
             plane, row = PLANES[a]
             grouped = [keep.tile([P, n, 4], BF16, name=f"grouped{a}_{t0}", align_bytes=64) for t0, n in PIECES]
             rows = raw[a][:].rearrange("p (j t) -> p j t", j=4)
-            for j0, j1, piece, engine in CASTS[a]:
-                t0, n = PIECES[piece]
-                src = rows[:, j0:j1, t0 : t0 + n].rearrange("p j (c i) -> p c j i", i=4)
-                dst = grouped[piece][:, :, j0:j1].rearrange("p (c i) j -> p c j i", i=4)
+            for j0, j1, piece, u0, u1, engine in CASTS[a]:
+                t0 = PIECES[piece][0]
+                src = rows[:, j0:j1, t0 + u0 : t0 + u1].rearrange("p j (c i) -> p c j i", i=4)
+                dst = grouped[piece][:, u0:u1, j0:j1].rearrange("p (c i) j -> p c j i", i=4)
                 if engine == "v":
                     nc.vector.tensor_copy(dst, src)
                 else:
@@ -149,6 +155,7 @@ def tile_moe_res_lin_none_kernel(tc, xT, xr, w8_words, w8_scales, w4_words, w4_s
         first_bank = psum.tile([P, N], F32, name="first_bank")
         banks = [psum.tile([P, N], F32, name=f"bank{e}") for e in range(E)]
         gated = {}
+        late = []
 
         def sums(e, b0, b1):
             return first_bank[:, 0:P] if (e, b0) == (0, 0) else banks[e][:, b0 * P : b1 * P]
@@ -164,7 +171,7 @@ def tile_moe_res_lin_none_kernel(tc, xT, xr, w8_words, w8_scales, w4_words, w4_s
                     rhs, rhs_scale = w4[:, 2 * e + a - 1, 2 * n0 : 2 * n1].bitcast(FP4X4), w_scales[e // 2][:, e % 2, a - 1, n0:n1]
                 nc.tensor.matmul_mx(
                     out=sums(e, b0, b1),
-                    lhsT=slot_words[a][:, cols].bitcast(FP8X4),
+                    lhsT=(late[0][:, (e - 2) * C : (e - 1) * C] if a == 0 and e >= 2 else slot_words[a][:, cols]).bitcast(FP8X4),
                     lhsT_scale=slot_scales[plane][row:P, cols],
                     rhs=rhs,
                     rhs_scale=rhs_scale,
@@ -185,26 +192,33 @@ def tile_moe_res_lin_none_kernel(tc, xT, xr, w8_words, w8_scales, w4_words, w4_s
             nc.scalar.copy(slot_y[b][:, e0 * C : e1 * C], turned[:, 0 : (e1 - e0) * C])
 
         def scatter(b, e0, e1):
-            nc.vector.tensor_copy(windows[b % 3][:].indirect(listed(e0, e1)), slot_y[b][:, e0 * C : e1 * C])
+            nc.vector.tensor_copy(windows[b][:].indirect(listed(e0, e1)), slot_y[b][:, e0 * C : e1 * C])
 
         def finish(b, engine, parts):
             for i in range(parts):
                 cols = slice(i * T // parts, (i + 1) * T // parts)
-                engine.tensor_tensor(results[b][:, cols], windows[b % 3][:, cols], residual[:, b, cols], ADD)
+                engine.tensor_tensor(results[b][:, cols], windows[b][:, cols], residual[:, b, cols], ADD)
                 nc.sync.dma_start(out[b * P : (b + 1) * P, cols], results[b][:, cols])
 
         quantise_pass(1)
-        for h in range(2):
-            gather(words[1], slot_words[1], 2 * h, 2 * h + 2)
-            gather(scales[0], slot_scales[0], 2 * h, 2 * h + 2)
+        gather(words[1], slot_words[1], 0, E)
+        gather(scales[0], slot_scales[0], 0, E)
         quantise_pass(0)
-        for h in range(2):
-            gather(words[0], slot_words[0], 2 * h, 2 * h + 2)
+        gather(words[0], slot_words[0], 0, 2)
         quantise_pass(2)
-        for e0, e1 in ((0, 1), (1, 2), (2, 4)):
-            gather(scales[1], slot_scales[1], e0, e1)
-            gather(words[2], slot_words[2], e0, e1)
-        for b in range(3):
+        for e in range(2):
+            gather(scales[1], slot_scales[1], e, e + 1)
+            gather(words[2], slot_words[2], e, e + 1)
+        late_words = keep.tile([P, S // 2], U32, name="late_words", tag="grouped2_384", align_bytes=64)
+        late.append(late_words)
+        nc.vector.tensor_copy(late_words[:], words[0][:].indirect(listed(2, 4)))
+        gather(scales[1], slot_scales[1], 2, 4)
+        gather(words[2], slot_words[2], 2, 4)
+        for b, tag in ((2, "scales1"), (3, "words2")):
+            window = keep.tile([P, T], F32, name=f"window{b}", tag=tag, align_bytes=64)
+            nc.gpsimd.memset(window[:], 0.0)
+            windows.append(window)
+        for b in range(2):
             multiply(0, b, b + 1)
             weigh(0, b, b + 1)
             turn(b, 0, 1)
@@ -212,27 +226,29 @@ def tile_moe_res_lin_none_kernel(tc, xT, xr, w8_words, w8_scales, w4_words, w4_s
         weigh(1, 0, 2)
         turn(0, 1, 2)
         turn(1, 1, 2)
+        multiply(0, 2, 3)
         multiply(0, 3, 4)
+        weigh(0, 2, 4)
+        weigh(1, 2, 4)
+        turn(2, 0, 2)
+        turn(3, 0, 2)
         for e in (2, 3):
             multiply(e, 0, NB)
             weigh(e, 0, 2)
         turn(0, 2, 4)
         turn(1, 2, 4)
-        for e in (1, 2, 3):
+        for e in (2, 3):
             weigh(e, 2, 4)
-        weigh(0, 3, 4)
-        turn(2, 1, 4)
-        turn(3, 0, 4)
+        turn(2, 2, 4)
+        turn(3, 2, 4)
 
-        for b in range(3):
-            scatter(b, 0, 1)
-        scatter(0, 1, 2)
-        scatter(1, 1, 2)
-        scatter(0, 2, 4)
-        finish(0, nc.gpsimd, 1)
-        scatter(1, 2, 4)
-        finish(1, nc.gpsimd, 1)
-        scatter(2, 1, 4)
-        finish(2, nc.gpsimd, 1)
-        scatter(3, 0, 4)
+        for e in range(2):
+            for b in range(2):
+                scatter(b, e, e + 1)
+        scatter(2, 0, 2)
+        scatter(3, 0, 2)
+        for b in range(NB - 1):
+            scatter(b, 2, 4)
+            finish(b, nc.gpsimd, 1)
+        scatter(3, 2, 4)
         finish(3, nc.vector, 2)

@@ -20,6 +20,7 @@ FP8X4 = mybir.dt.float8_e4m3fn_x4
 FP4X4 = mybir.dt.float4_e2m1fn_x4
 COPY = mybir.ActivationFunctionType.Copy
 ADD = mybir.AluOpType.add
+MULT = mybir.AluOpType.mult
 
 FLOPS = 2 * K * N * S
 BYTES = 4 * K * T + 2 * 4 * N * T + E * 512 * N * 4 + E * 1024 * N // 2 + E * 48 * N + 4 * S + 2 * 128 * S // 16
@@ -27,8 +28,8 @@ BYTES = 4 * K * T + 2 * 4 * N * T + E * 512 * N * 4 + E * 1024 * N // 2 + E * 48
 ORDER = (1, 0, 2)
 PIECES = ((0, 256), (256, 128), (384, 256))
 CASTS = {
-    1: ((0, 2, 0, 0, 256, "v"), (0, 2, 2, 0, 256, "s"), (0, 2, 1, 0, 128, "v"), (2, 4, 0, 0, 256, "v"), (2, 4, 1, 0, 128, "s"),
-        (2, 4, 2, 0, 128, "s"), (2, 4, 2, 128, 256, "v")),
+    1: ((0, 2, 0, 0, 256, "v"), (0, 2, 2, 0, 256, "s"), (0, 2, 1, 0, 128, "v"), (2, 4, 0, 0, 192, "v"), (2, 4, 0, 192, 256, "s"),
+        (2, 4, 1, 0, 128, "s"), (2, 4, 2, 0, 192, "s"), (2, 4, 2, 192, 256, "v")),
     0: ((0, 2, 0, 0, 256, "s"), (0, 2, 1, 0, 128, "s"), (2, 4, 0, 0, 256, "s"), (2, 4, 1, 0, 128, "s"), (0, 4, 2, 0, 256, "v")),
     2: ((0, 2, 0, 0, 256, "s"), (0, 2, 2, 0, 256, "s"), (2, 4, 0, 0, 256, "s"), (0, 4, 1, 0, 128, "v"),
         (2, 4, 2, 0, 128, "s"), (2, 4, 2, 128, 256, "v")),
@@ -44,20 +45,18 @@ def tile_moe_res_lin_none_kernel(tc, xT, xr, w8_words, w8_scales, w4_words, w4_s
         psum = ctx.enter_context(tc.psum_pool(name="psum", bufs=1))
 
         offsets = keep.tile([P, S // 16], U16, name="offsets")
-        w8 = keep.tile([P, E, 4 * N], U8, name="w8", align_bytes=64)
-        w4 = keep.tile([P, 2 * E, 2 * N], U8, name="w4", align_bytes=64)
         w_scales = [keep.tile([P, 2, 2, N], U8, name=f"w_scales{h}", align_bytes=64) for h in range(2)]
+        w8s = w_scales[0][:].rearrange("p e a n -> p (e a) n")
         residual = keep.tile([P, NB, T], F32, name="residual")
         gate_rows = keep.tile([P, P], F32, name="gate_rows")
         gate_cols = keep.tile([P, E], F32, name="gate_cols")
+        gate_wide = keep.tile([P, 2 * C], F32, name="gate_wide")
         ident = keep.tile([P, P], F32, name="ident")
         windows = [keep.tile([P, T], F32, name=f"window{b}") for b in range(2)]
         slot_y = [keep.tile([P, S], F32, name=f"slot_y{b}") for b in range(NB)]
         results = [keep.tile([P, T], F32, name=f"result{b}") for b in range(NB)]
         words = [keep.tile([P, WIDE if a == 1 else T], U32, name=f"words{a}", align_bytes=64) for a in range(PASSES)]
-        scales = [keep.tile([P, WIDE if a == 0 else T], U8, name=f"scales{a}", align_bytes=64) for a in range(2)]
-        slot_words = [keep.tile([P, S if a else S // 2], U32, name=f"slot_words{a}", align_bytes=64) for a in range(PASSES)]
-        slot_scales = [keep.tile([P, S], U8, name=f"slot_scales{a}", align_bytes=64) for a in range(2)]
+        scales = [keep.tile([P, T], U8, name=f"scales{a}", align_bytes=64) for a in range(2)]
         warm = keep.tile([P, 1], F32, name="warm")
 
         nc.vector.memset(warm[:], 0.0)
@@ -84,15 +83,21 @@ def tile_moe_res_lin_none_kernel(tc, xT, xr, w8_words, w8_scales, w4_words, w4_s
         w8s_src = w8_scales.rearrange("e a (q r) n -> r q (e a) n", r=4).bitcast(I32)
         w4s_src = w4_scales.rearrange("e a (q r) n -> r q (e a) n", r=4).bitcast(I32)
 
-        def load_w8(e0, e1):
-            nc.sync.dma_start(w8[:, e0:e1, :].bitcast(I32), w8_src[:, e0:e1, :])
+        weights = {}
 
-        def load_w4(e0, e1):
-            nc.sync.dma_start(w4[:, 2 * e0 : 2 * e1, :].bitcast(I32), w4_src[:, 2 * e0 : 2 * e1, :])
+        def load_weights(e0, e1, b0, b1):
+            width = (b1 - b0) * P
+            w4 = keep.tile([P, 2 * (e1 - e0), 2 * width], U8, name=f"w4_{e0}{b0}", align_bytes=64)
+            nc.sync.dma_start(w4[:].bitcast(I32), w4_src[:, 2 * e0 : 2 * e1, b0 * P // 2 : b1 * P // 2])
+            w8 = keep.tile([P, e1 - e0, 4 * width], U8, name=f"w8_{e0}{b0}", align_bytes=64)
+            nc.sync.dma_start(w8[:].bitcast(I32), w8_src[:, e0:e1, b0 * P : b1 * P])
+            for e in range(e0, e1):
+                for b in range(b0, b1):
+                    weights[e, b] = (w8[:, e - e0, :], w4[:, 2 * (e - e0) : 2 * (e - e0) + 2, :], b0)
 
-        def load_w8_scales(e0, e1):
+        def load_w8_scales():
             for r in range(4):
-                nc.sync.dma_start(w_scales[e0 // 2][4 + r : P : 32, :, 0, :].bitcast(I32), w8s_src[r, :, e0:e1, :])
+                nc.sync.dma_start(w8s[4 + r : P : 32, :, :].bitcast(I32), w8s_src[r])
 
         def load_w4_scales(e0, e1):
             for r in range(4):
@@ -105,19 +110,17 @@ def tile_moe_res_lin_none_kernel(tc, xT, xr, w8_words, w8_scales, w4_words, w4_s
             nc.sync.dma_start(dst[:, :, t0:t1], x_src[ORDER[0], 1].rearrange("p (j t) -> p j t", j=2)[:, :, t0:t1])
         nc.sync.dma_start(offsets[:], offs)
         nc.sync.dma_start(gate_rows[0:E, :], gate[0:1, :].rearrange("o (e c) -> (o e) c", c=C))
-        for a in ORDER[1:]:
-            for u in range(2):
-                load_tokens(a, u)
-        load_w8_scales(0, 2)
-        load_w4(0, 1)
-        load_w8(0, 1)
+        load_tokens(ORDER[1], 0)
+        load_tokens(ORDER[1], 1)
+        load_tokens(ORDER[2], 0)
+        load_w8_scales()
+        load_tokens(ORDER[2], 1)
         load_w4_scales(0, 2)
-        load_w4(1, 2)
-        load_w8(1, 2)
-        load_w8_scales(2, 4)
-        load_w4(2, 4)
-        load_w8(2, 4)
+        load_weights(0, 2, 0, 2)
+        nc.sync.dma_start(gate_wide[:], gate[0:P, 0 : 2 * C])
+        load_weights(0, 2, 2, NB)
         load_w4_scales(2, 4)
+        load_weights(2, 4, 0, NB)
         xr_src = xr.rearrange("(b p) t -> p b t", p=P)
         for h in range(2):
             nc.sync.dma_start(residual[:, 2 * h : 2 * h + 2, :], xr_src[:, 2 * h : 2 * h + 2, :])
@@ -149,39 +152,50 @@ def tile_moe_res_lin_none_kernel(tc, xT, xr, w8_words, w8_scales, w4_words, w4_s
         def listed(e0, e1):
             return offsets[:, e0 * C // 16 : e1 * C // 16]
 
-        def gather(table, slots, e0, e1):
-            nc.vector.tensor_copy(slots[:, e0 * C : e1 * C], table[:].indirect(listed(e0, e1)))
+        slot_words, slot_scales = {}, {}
 
-        first_bank = psum.tile([P, N], F32, name="first_bank")
-        banks = [psum.tile([P, N], F32, name=f"bank{e}") for e in range(E)]
+        def gather(table, dtype, name, e0, e1, tag):
+            tile = keep.tile([P, (e1 - e0) * C], dtype, name=name, tag=tag or name, align_bytes=64)
+            nc.vector.tensor_copy(tile[:], table[:].indirect(listed(e0, e1)))
+            return {e: (tile, slice((e - e0) * C, (e - e0 + 1) * C)) for e in range(e0, e1)}
+
+        def gather_words(a, e0, e1, tag=None):
+            for e, place in gather(words[a], U32, f"slot_words{a}{e0}", e0, e1, tag).items():
+                slot_words[a, e] = place
+
+        def gather_scales(plane, e0, e1, tag=None):
+            for e, place in gather(scales[plane], U8, f"slot_scales{plane}{e0}", e0, e1, tag).items():
+                slot_scales[plane, e] = place
+
         gated = {}
-        late = []
 
-        def sums(e, b0, b1):
-            return first_bank[:, 0:P] if (e, b0) == (0, 0) else banks[e][:, b0 * P : b1 * P]
-
-        def multiply(e, b0, b1):
-            cols = slice(e * C, (e + 1) * C)
+        def multiply(e, b0, b1, sums, tokens_move):
             n0, n1 = b0 * P, b1 * P
+            w8, w4, first = weights[e, b0]
+            m0, m1 = (b0 - first) * P, (b1 - first) * P
             for a in ORDER:
                 plane, row = PLANES[a]
                 if a == 0:
-                    rhs, rhs_scale = w8[:, e, 4 * n0 : 4 * n1].bitcast(FP8X4), w_scales[e // 2][4:P, e % 2, 0, n0:n1]
+                    matrix = w8[:, 4 * m0 : 4 * m1].bitcast(FP8X4), w8s[4:P, e, n0:n1]
                 else:
-                    rhs, rhs_scale = w4[:, 2 * e + a - 1, 2 * n0 : 2 * n1].bitcast(FP4X4), w_scales[e // 2][:, e % 2, a - 1, n0:n1]
+                    matrix = w4[:, a - 1, 2 * m0 : 2 * m1].bitcast(FP4X4), w_scales[e // 2][:, e % 2, a - 1, n0:n1]
+                codes, code_cols = slot_words[a, e]
+                plane_tile, plane_cols = slot_scales[plane, e]
+                tokens = codes[:, code_cols].bitcast(FP8X4), plane_tile[row:P, plane_cols]
+                still, moving = (matrix, tokens) if tokens_move else (tokens, matrix)
                 nc.tensor.matmul_mx(
-                    out=sums(e, b0, b1),
-                    lhsT=(late[0][:, (e - 2) * C : (e - 1) * C] if a == 0 and e >= 2 else slot_words[a][:, cols]).bitcast(FP8X4),
-                    lhsT_scale=slot_scales[plane][row:P, cols],
-                    rhs=rhs,
-                    rhs_scale=rhs_scale,
+                    out=sums,
+                    lhsT=still[0],
+                    lhsT_scale=still[1],
+                    rhs=moving[0],
+                    rhs_scale=moving[1],
                     start=(a == ORDER[0]),
                     stop=(a == ORDER[-1]),
                 )
 
-        def weigh(e, b0, b1):
+        def weigh(e, bank, b0, b1):
             tile = keep.tile([P, (b1 - b0) * P], F32, name=f"gated{e}{b0}")
-            nc.scalar.activation(tile[:], sums(e, b0, b1), COPY, scale=gate_cols[:, e : e + 1])
+            nc.scalar.activation(tile[:], bank[:, b0 * P : b1 * P], COPY, scale=gate_cols[:, e : e + 1])
             for b in range(b0, b1):
                 gated[e, b] = tile[:, (b - b0) * P : (b - b0 + 1) * P]
 
@@ -190,6 +204,9 @@ def tile_moe_res_lin_none_kernel(tc, xT, xr, w8_words, w8_scales, w4_words, w4_s
             for e in range(e0, e1):
                 nc.tensor.transpose(turned[:, (e - e0) * C : (e - e0 + 1) * C], gated[e, b], ident[:])
             nc.scalar.copy(slot_y[b][:, e0 * C : e1 * C], turned[:, 0 : (e1 - e0) * C])
+
+        def scatter_times_gate(b):
+            nc.vector.tensor_tensor(windows[b][:].indirect(listed(0, 2)), slot_y[b][:, 0 : 2 * C], gate_wide[:], MULT)
 
         def scatter(b, e0, e1):
             nc.vector.tensor_copy(windows[b][:].indirect(listed(e0, e1)), slot_y[b][:, e0 * C : e1 * C])
@@ -201,52 +218,44 @@ def tile_moe_res_lin_none_kernel(tc, xT, xr, w8_words, w8_scales, w4_words, w4_s
                 nc.sync.dma_start(out[b * P : (b + 1) * P, cols], results[b][:, cols])
 
         quantise_pass(1)
-        gather(words[1], slot_words[1], 0, E)
-        gather(scales[0], slot_scales[0], 0, E)
+        gather_words(1, 0, E)
+        gather_scales(0, 0, 2)
         quantise_pass(0)
-        gather(words[0], slot_words[0], 0, 2)
+        gather_scales(0, 2, 4, tag="grouped0_256")
+        gather_words(0, 0, 2)
         quantise_pass(2)
-        for e in range(2):
-            gather(scales[1], slot_scales[1], e, e + 1)
-            gather(words[2], slot_words[2], e, e + 1)
-        late_words = keep.tile([P, S // 2], U32, name="late_words", tag="grouped2_384", align_bytes=64)
-        late.append(late_words)
-        nc.vector.tensor_copy(late_words[:], words[0][:].indirect(listed(2, 4)))
-        gather(scales[1], slot_scales[1], 2, 4)
-        gather(words[2], slot_words[2], 2, 4)
+        gather_scales(1, 0, 2)
+        gather_words(2, 0, 2)
+        gather_words(0, 2, 4, tag="grouped2_384")
+        gather_scales(1, 2, 4)
+        gather_words(2, 2, 4)
         for b, tag in ((2, "scales1"), (3, "words2")):
             window = keep.tile([P, T], F32, name=f"window{b}", tag=tag, align_bytes=64)
             nc.gpsimd.memset(window[:], 0.0)
             windows.append(window)
-        for b in range(2):
-            multiply(0, b, b + 1)
-            weigh(0, b, b + 1)
-            turn(b, 0, 1)
-        multiply(1, 0, NB)
-        weigh(1, 0, 2)
-        turn(0, 1, 2)
-        turn(1, 1, 2)
-        multiply(0, 2, 3)
-        multiply(0, 3, 4)
-        weigh(0, 2, 4)
-        weigh(1, 2, 4)
-        turn(2, 0, 2)
-        turn(3, 0, 2)
+        for e in range(2):
+            bank = psum.tile([P, N], F32, name=f"first{e}", tag=f"bank{2 + e}")
+            multiply(e, 0, 1, bank[:, 0:C], True)
+            nc.scalar.copy(slot_y[0][:, e * C : (e + 1) * C], bank[:, 0:C])
+        for b in range(1, NB):
+            bank = psum.tile([P, N], F32, name=f"pair{b}")
+            for e in range(2):
+                multiply(e, b, b + 1, bank[:, e * C : (e + 1) * C], True)
+            nc.scalar.copy(slot_y[b][:, 0 : 2 * C], bank[:, 0 : 2 * C])
+        banks = {}
         for e in (2, 3):
-            multiply(e, 0, NB)
-            weigh(e, 0, 2)
+            banks[e] = psum.tile([P, N], F32, name=f"bank{e}", tag=f"bank{e}")
+            multiply(e, 0, NB, banks[e][:], False)
+            weigh(e, banks[e], 0, 2)
         turn(0, 2, 4)
         turn(1, 2, 4)
         for e in (2, 3):
-            weigh(e, 2, 4)
+            weigh(e, banks[e], 2, 4)
         turn(2, 2, 4)
         turn(3, 2, 4)
 
-        for e in range(2):
-            for b in range(2):
-                scatter(b, e, e + 1)
-        scatter(2, 0, 2)
-        scatter(3, 0, 2)
+        for b in range(NB):
+            scatter_times_gate(b)
         for b in range(NB - 1):
             scatter(b, 2, 4)
             finish(b, nc.gpsimd, 1)

@@ -46,7 +46,6 @@ def tile_moe_res_lin_none_kernel(tc, xT, xr, w8_words, w8_scales, w4_words, w4_s
 
         offsets = keep.tile([P, S // 16], U16, name="offsets")
         w_scales = [keep.tile([P, 2, 2, N], U8, name=f"w_scales{h}", align_bytes=64) for h in range(2)]
-        w8s = w_scales[0][:].rearrange("p e a n -> p (e a) n")
         residual = keep.tile([P, NB, T], F32, name="residual")
         gate_rows = keep.tile([P, P], F32, name="gate_rows")
         gate_cols = keep.tile([P, E], F32, name="gate_cols")
@@ -55,7 +54,7 @@ def tile_moe_res_lin_none_kernel(tc, xT, xr, w8_words, w8_scales, w4_words, w4_s
         windows = [keep.tile([P, T], F32, name=f"window{b}") for b in range(2)]
         slot_y = [keep.tile([P, S], F32, name=f"slot_y{b}") for b in range(NB)]
         results = [keep.tile([P, T], F32, name=f"result{b}") for b in range(NB)]
-        words = [keep.tile([P, WIDE if a == 1 else T], U32, name=f"words{a}", align_bytes=64) for a in range(PASSES)]
+        words = [keep.tile([P, WIDE if a < 2 else T], U32, name=f"words{a}", align_bytes=64) for a in range(PASSES)]
         scales = [keep.tile([P, T], U8, name=f"scales{a}", align_bytes=64) for a in range(2)]
         warm = keep.tile([P, 1], F32, name="warm")
 
@@ -65,7 +64,7 @@ def tile_moe_res_lin_none_kernel(tc, xT, xr, w8_words, w8_scales, w4_words, w4_s
         make_identity(nc, ident[:])
         for plane in scales:
             nc.vector.memset(plane[:].bitcast(I32), 0)
-        for table in words[1:2]:
+        for table in words[:2]:
             nc.vector.memset(table[:, T:WIDE].bitcast(I32), 0)
         for plane in w_scales:
             nc.vector.memset(plane[:].rearrange("p e a n -> p (e a n)").bitcast(I32), 0)
@@ -95,9 +94,9 @@ def tile_moe_res_lin_none_kernel(tc, xT, xr, w8_words, w8_scales, w4_words, w4_s
                 for b in range(b0, b1):
                     weights[e, b] = (w8[:, e - e0, :], w4[:, 2 * (e - e0) : 2 * (e - e0) + 2, :], b0)
 
-        def load_w8_scales():
+        def load_w8_scales(e0, e1):
             for r in range(4):
-                nc.sync.dma_start(w8s[4 + r : P : 32, :, :].bitcast(I32), w8s_src[r])
+                nc.sync.dma_start(w_scales[e0 // 2][4 + r : P : 32, :, 0, :].bitcast(I32), w8s_src[r, :, e0:e1, :])
 
         def load_w4_scales(e0, e1):
             for r in range(4):
@@ -109,23 +108,24 @@ def tile_moe_res_lin_none_kernel(tc, xT, xr, w8_words, w8_scales, w4_words, w4_s
             dst = raw[ORDER[0]][:, 2 * T : 4 * T].rearrange("p (j t) -> p j t", j=2)
             nc.sync.dma_start(dst[:, :, t0:t1], x_src[ORDER[0], 1].rearrange("p (j t) -> p j t", j=2)[:, :, t0:t1])
         nc.sync.dma_start(offsets[:], offs)
-        nc.sync.dma_start(gate_rows[0:E, :], gate[0:1, :].rearrange("o (e c) -> (o e) c", c=C))
-        load_tokens(ORDER[1], 0)
-        load_tokens(ORDER[1], 1)
-        load_tokens(ORDER[2], 0)
-        load_w8_scales()
-        load_tokens(ORDER[2], 1)
+        for a in ORDER[1:]:
+            load_tokens(a, 0)
+            load_tokens(a, 1)
         load_w4_scales(0, 2)
-        load_weights(0, 2, 0, 2)
+        load_weights(0, 1, 0, NB)
+        load_w8_scales(0, 2)
         nc.sync.dma_start(gate_wide[:], gate[0:P, 0 : 2 * C])
-        load_weights(0, 2, 2, NB)
+        load_weights(1, 2, 0, NB)
         load_w4_scales(2, 4)
-        load_weights(2, 4, 0, NB)
+        load_weights(2, 3, 0, NB)
+        load_w8_scales(2, 4)
+        load_weights(3, 4, 0, NB)
+        nc.sync.dma_start(gate_rows[0:E, :], gate[0:1, :].rearrange("o (e c) -> (o e) c", c=C))
         xr_src = xr.rearrange("(b p) t -> p b t", p=P)
         for h in range(2):
             nc.sync.dma_start(residual[:, 2 * h : 2 * h + 2, :], xr_src[:, 2 * h : 2 * h + 2, :])
 
-        turned_gate = psum.tile([P, N], F32, name="turned_gate", tag="turned", bufs=3)
+        turned_gate = psum.tile([P, N], F32, name="turned_gate", tag="turned", bufs=4)
         nc.tensor.transpose(turned_gate[:, 0:P], gate_rows[:], ident[:])
         nc.scalar.copy(gate_cols[:], turned_gate[:, 0:E])
 
@@ -176,7 +176,7 @@ def tile_moe_res_lin_none_kernel(tc, xT, xr, w8_words, w8_scales, w4_words, w4_s
             for a in ORDER:
                 plane, row = PLANES[a]
                 if a == 0:
-                    matrix = w8[:, 4 * m0 : 4 * m1].bitcast(FP8X4), w8s[4:P, e, n0:n1]
+                    matrix = w8[:, 4 * m0 : 4 * m1].bitcast(FP8X4), w_scales[e // 2][4:P, e % 2, 0, n0:n1]
                 else:
                     matrix = w4[:, a - 1, 2 * m0 : 2 * m1].bitcast(FP4X4), w_scales[e // 2][:, e % 2, a - 1, n0:n1]
                 codes, code_cols = slot_words[a, e]
@@ -200,13 +200,14 @@ def tile_moe_res_lin_none_kernel(tc, xT, xr, w8_words, w8_scales, w4_words, w4_s
                 gated[e, b] = tile[:, (b - b0) * P : (b - b0 + 1) * P]
 
         def turn(b, e0, e1):
-            turned = psum.tile([P, N], F32, name=f"turned{b}{e0}", tag="turned", bufs=3)
+            turned = psum.tile([P, N], F32, name=f"turned{b}{e0}", tag="turned", bufs=4)
             for e in range(e0, e1):
                 nc.tensor.transpose(turned[:, (e - e0) * C : (e - e0 + 1) * C], gated[e, b], ident[:])
             nc.scalar.copy(slot_y[b][:, e0 * C : e1 * C], turned[:, 0 : (e1 - e0) * C])
 
-        def scatter_times_gate(b):
-            nc.vector.tensor_tensor(windows[b][:].indirect(listed(0, 2)), slot_y[b][:, 0 : 2 * C], gate_wide[:], MULT)
+        def scatter_times_gate(b, e0, e1):
+            cols = slice(e0 * C, e1 * C)
+            nc.vector.tensor_tensor(windows[b][:].indirect(listed(e0, e1)), slot_y[b][:, cols], gate_wide[:, cols], MULT)
 
         def scatter(b, e0, e1):
             nc.vector.tensor_copy(windows[b][:].indirect(listed(e0, e1)), slot_y[b][:, e0 * C : e1 * C])
@@ -222,26 +223,23 @@ def tile_moe_res_lin_none_kernel(tc, xT, xr, w8_words, w8_scales, w4_words, w4_s
         gather_scales(0, 0, 2)
         quantise_pass(0)
         gather_scales(0, 2, 4, tag="grouped0_256")
-        gather_words(0, 0, 2)
+        gather_words(0, 0, E)
         quantise_pass(2)
-        gather_scales(1, 0, 2)
-        gather_words(2, 0, 2)
-        gather_words(0, 2, 4, tag="grouped2_384")
+        for e in range(2):
+            gather_scales(1, e, e + 1)
+            gather_words(2, e, e + 1)
         gather_scales(1, 2, 4)
         gather_words(2, 2, 4)
         for b, tag in ((2, "scales1"), (3, "words2")):
             window = keep.tile([P, T], F32, name=f"window{b}", tag=tag, align_bytes=64)
             nc.gpsimd.memset(window[:], 0.0)
             windows.append(window)
-        for e in range(2):
-            bank = psum.tile([P, N], F32, name=f"first{e}", tag=f"bank{2 + e}")
-            multiply(e, 0, 1, bank[:, 0:C], True)
-            nc.scalar.copy(slot_y[0][:, e * C : (e + 1) * C], bank[:, 0:C])
-        for b in range(1, NB):
-            bank = psum.tile([P, N], F32, name=f"pair{b}")
-            for e in range(2):
-                multiply(e, b, b + 1, bank[:, e * C : (e + 1) * C], True)
-            nc.scalar.copy(slot_y[b][:, 0 : 2 * C], bank[:, 0 : 2 * C])
+        first_units = [(b, e, e + 1) for e in range(2) for b in range(2)] + [(b, 0, 2) for b in range(2, NB)]
+        for i, (b, e0, e1) in enumerate(first_units):
+            bank = psum.tile([P, N], F32, name=f"direct{i}", tag=f"bank{i % 4}")
+            for e in range(e0, e1):
+                multiply(e, b, b + 1, bank[:, (e - e0) * C : (e - e0 + 1) * C], True)
+            nc.scalar.copy(slot_y[b][:, e0 * C : e1 * C], bank[:, 0 : (e1 - e0) * C])
         banks = {}
         for e in (2, 3):
             banks[e] = psum.tile([P, N], F32, name=f"bank{e}", tag=f"bank{e}")
@@ -254,8 +252,8 @@ def tile_moe_res_lin_none_kernel(tc, xT, xr, w8_words, w8_scales, w4_words, w4_s
         turn(2, 2, 4)
         turn(3, 2, 4)
 
-        for b in range(NB):
-            scatter_times_gate(b)
+        for unit in first_units:
+            scatter_times_gate(*unit)
         for b in range(NB - 1):
             scatter(b, 2, 4)
             finish(b, nc.gpsimd, 1)

@@ -28,8 +28,8 @@ BYTES = 4 * K * T + 2 * 4 * N * T + E * 512 * N * 4 + E * 1024 * N // 2 + E * 48
 ORDER = (1, 0, 2)
 PIECES = ((0, 256), (256, 128), (384, 256))
 CASTS = {
-    1: ((0, 2, 0, 0, 256, "v"), (0, 2, 2, 0, 256, "s"), (0, 2, 1, 0, 128, "v"), (2, 4, 0, 0, 192, "v"), (2, 4, 0, 192, 256, "s"),
-        (2, 4, 1, 0, 128, "s"), (2, 4, 2, 0, 192, "s"), (2, 4, 2, 192, 256, "v")),
+    1: ((0, 2, 0, 0, 256, "v"), (0, 2, 2, 0, 256, "s"), (0, 2, 1, 0, 128, "v"), (2, 4, 0, 0, 256, "v"), (2, 4, 2, 0, 256, "s"),
+        (2, 4, 1, 0, 128, "v")),
     0: ((0, 2, 0, 0, 256, "s"), (0, 2, 1, 0, 128, "s"), (2, 4, 0, 0, 256, "s"), (2, 4, 1, 0, 128, "s"), (0, 4, 2, 0, 256, "v")),
     2: ((0, 2, 0, 0, 256, "s"), (0, 2, 2, 0, 256, "s"), (2, 4, 0, 0, 256, "s"), (0, 4, 1, 0, 128, "v"),
         (2, 4, 2, 0, 128, "s"), (2, 4, 2, 128, 256, "v")),
@@ -48,14 +48,13 @@ def tile_moe_res_lin_none_kernel(tc, xT, xr, w8_words, w8_scales, w4_words, w4_s
         w_scales = [keep.tile([P, 2, 2, N], U8, name=f"w_scales{h}", align_bytes=64) for h in range(2)]
         residual = keep.tile([P, NB, T], F32, name="residual")
         gate_rows = keep.tile([P, P], F32, name="gate_rows")
-        gate_cols = keep.tile([P, E], F32, name="gate_cols")
-        gate_wide = keep.tile([P, 2 * C], F32, name="gate_wide")
+        gate_wide = keep.tile([P, S], F32, name="gate_wide")
         ident = keep.tile([P, P], F32, name="ident")
         windows = [keep.tile([P, T], F32, name=f"window{b}") for b in range(2)]
         slot_y = [keep.tile([P, S], F32, name=f"slot_y{b}") for b in range(NB)]
         results = [keep.tile([P, T], F32, name=f"result{b}") for b in range(NB)]
         words = [keep.tile([P, WIDE if a < 2 else T], U32, name=f"words{a}", align_bytes=64) for a in range(PASSES)]
-        scales = [keep.tile([P, T], U8, name=f"scales{a}", align_bytes=64) for a in range(2)]
+        scales = [keep.tile([P, WIDE if a == 0 else T], U8, name=f"scales{a}", align_bytes=64) for a in range(2)]
         warm = keep.tile([P, 1], F32, name="warm")
 
         nc.vector.memset(warm[:], 0.0)
@@ -104,30 +103,35 @@ def tile_moe_res_lin_none_kernel(tc, xT, xr, w8_words, w8_scales, w4_words, w4_s
                 nc.sync.dma_start(dst.bitcast(I32), w4s_src[r, :, 2 * e0 : 2 * e1, :])
 
         load_tokens(ORDER[0], 0)
-        for t0, t1 in ((0, 384), (384, T)):
-            dst = raw[ORDER[0]][:, 2 * T : 4 * T].rearrange("p (j t) -> p j t", j=2)
-            nc.sync.dma_start(dst[:, :, t0:t1], x_src[ORDER[0], 1].rearrange("p (j t) -> p j t", j=2)[:, :, t0:t1])
+        load_tokens(ORDER[0], 1)
         nc.sync.dma_start(offsets[:], offs)
         for a in ORDER[1:]:
             load_tokens(a, 0)
             load_tokens(a, 1)
+        nc.sync.dma_start(gate_rows[0:E, :], gate[0:1, :].rearrange("o (e c) -> (o e) c", c=C))
         load_w4_scales(0, 2)
         load_weights(0, 1, 0, NB)
         load_w8_scales(0, 2)
-        nc.sync.dma_start(gate_wide[:], gate[0:P, 0 : 2 * C])
         load_weights(1, 2, 0, NB)
         load_w4_scales(2, 4)
         load_weights(2, 3, 0, NB)
         load_w8_scales(2, 4)
         load_weights(3, 4, 0, NB)
-        nc.sync.dma_start(gate_rows[0:E, :], gate[0:1, :].rearrange("o (e c) -> (o e) c", c=C))
         xr_src = xr.rearrange("(b p) t -> p b t", p=P)
         for h in range(2):
             nc.sync.dma_start(residual[:, 2 * h : 2 * h + 2, :], xr_src[:, 2 * h : 2 * h + 2, :])
 
-        turned_gate = psum.tile([P, N], F32, name="turned_gate", tag="turned", bufs=4)
-        nc.tensor.transpose(turned_gate[:, 0:P], gate_rows[:], ident[:])
-        nc.scalar.copy(gate_cols[:], turned_gate[:, 0:E])
+        gate_cols = []
+
+        def spread_gate():
+            turned_gate = psum.tile([P, N], F32, name="turned_gate", tag="turned", bufs=2)
+            nc.tensor.transpose(turned_gate[:, 0:P], gate_rows[:], ident[:])
+            gate_cols.append(keep.tile([P, E], F32, name="gate_cols", tag="raw2"))
+            nc.scalar.copy(gate_cols[0][:], turned_gate[:, 0:E])
+            spread = psum.tile([P, S], F32, name="spread", tag="turned", bufs=2)
+            for e in range(E):
+                nc.tensor.transpose(spread[:, e * C : (e + 1) * C], gate_cols[0][:, e : e + 1].to_broadcast([P, P]), ident[:])
+            nc.scalar.copy(gate_wide[:], spread[:])
 
         def quantise_pass(a):
             plane, row = PLANES[a]
@@ -195,12 +199,12 @@ def tile_moe_res_lin_none_kernel(tc, xT, xr, w8_words, w8_scales, w4_words, w4_s
 
         def weigh(e, bank, b0, b1):
             tile = keep.tile([P, (b1 - b0) * P], F32, name=f"gated{e}{b0}")
-            nc.scalar.activation(tile[:], bank[:, b0 * P : b1 * P], COPY, scale=gate_cols[:, e : e + 1])
+            nc.scalar.activation(tile[:], bank[:, b0 * P : b1 * P], COPY, scale=gate_cols[0][:, e : e + 1])
             for b in range(b0, b1):
                 gated[e, b] = tile[:, (b - b0) * P : (b - b0 + 1) * P]
 
         def turn(b, e0, e1):
-            turned = psum.tile([P, N], F32, name=f"turned{b}{e0}", tag="turned", bufs=4)
+            turned = psum.tile([P, N], F32, name=f"turned{b}{e0}", tag="turned", bufs=2)
             for e in range(e0, e1):
                 nc.tensor.transpose(turned[:, (e - e0) * C : (e - e0 + 1) * C], gated[e, b], ident[:])
             nc.scalar.copy(slot_y[b][:, e0 * C : e1 * C], turned[:, 0 : (e1 - e0) * C])
@@ -220,42 +224,39 @@ def tile_moe_res_lin_none_kernel(tc, xT, xr, w8_words, w8_scales, w4_words, w4_s
 
         quantise_pass(1)
         gather_words(1, 0, E)
-        gather_scales(0, 0, 2)
+        gather_scales(0, 0, E)
         quantise_pass(0)
-        gather_scales(0, 2, 4, tag="grouped0_256")
         gather_words(0, 0, E)
         quantise_pass(2)
-        for e in range(2):
-            gather_scales(1, e, e + 1)
-            gather_words(2, e, e + 1)
-        gather_scales(1, 2, 4)
-        gather_words(2, 2, 4)
+        spread_gate()
+        for e0, e1 in ((0, 1), (1, E)):
+            gather_scales(1, e0, e1)
+            gather_words(2, e0, e1)
         for b, tag in ((2, "scales1"), (3, "words2")):
             window = keep.tile([P, T], F32, name=f"window{b}", tag=tag, align_bytes=64)
             nc.gpsimd.memset(window[:], 0.0)
             windows.append(window)
-        first_units = [(b, e, e + 1) for e in range(2) for b in range(2)] + [(b, 0, 2) for b in range(2, NB)]
+        first_units = [(b, 0, 1) for b in range(NB)] + [(b, 1, 2) for b in range(3)] + [(0, 2, 4)]
         for i, (b, e0, e1) in enumerate(first_units):
             bank = psum.tile([P, N], F32, name=f"direct{i}", tag=f"bank{i % 4}")
             for e in range(e0, e1):
                 multiply(e, b, b + 1, bank[:, (e - e0) * C : (e - e0 + 1) * C], True)
             nc.scalar.copy(slot_y[b][:, e0 * C : e1 * C], bank[:, 0 : (e1 - e0) * C])
         banks = {}
-        for e in (2, 3):
-            banks[e] = psum.tile([P, N], F32, name=f"bank{e}", tag=f"bank{e}")
-            multiply(e, 0, NB, banks[e][:], False)
-            weigh(e, banks[e], 0, 2)
-        turn(0, 2, 4)
+        for e, b0 in ((1, 3), (2, 1), (3, 1)):
+            banks[e] = psum.tile([P, N], F32, name=f"late{e}", tag=f"late{e % 2}")
+            for b in range(b0, NB):
+                multiply(e, b, b + 1, banks[e][:, b * P : (b + 1) * P], False)
+            weigh(e, banks[e], b0, NB)
         turn(1, 2, 4)
-        for e in (2, 3):
-            weigh(e, banks[e], 2, 4)
         turn(2, 2, 4)
-        turn(3, 2, 4)
+        turn(3, 1, 4)
 
         for unit in first_units:
             scatter_times_gate(*unit)
-        for b in range(NB - 1):
+        finish(0, nc.gpsimd, 1)
+        for b in range(1, NB - 1):
             scatter(b, 2, 4)
             finish(b, nc.gpsimd, 1)
-        scatter(3, 2, 4)
+        scatter(3, 1, 4)
         finish(3, nc.vector, 2)

@@ -25,17 +25,12 @@ MULT = mybir.AluOpType.mult
 FLOPS = 2 * K * N * S
 BYTES = 4 * K * T + 2 * 4 * N * T + E * 512 * N * 4 + E * 1024 * N // 2 + E * 48 * N + 4 * S + 2 * 128 * S // 16
 
-ORDER = (1, 0, 2)
-PIECES = ((0, 256), (256, 128), (384, 256))
-CASTS = {
-    1: ((0, 2, 0, 0, 256, "v"), (0, 2, 2, 0, 256, "s"), (0, 2, 1, 0, 128, "v"), (2, 4, 0, 0, 256, "v"), (2, 4, 2, 0, 256, "s"),
-        (2, 4, 1, 0, 128, "v")),
-    0: ((0, 2, 0, 0, 256, "s"), (0, 2, 1, 0, 128, "s"), (2, 4, 0, 0, 256, "s"), (2, 4, 1, 0, 128, "s"), (0, 4, 2, 0, 256, "v")),
-    2: ((0, 2, 0, 0, 256, "s"), (0, 2, 2, 0, 256, "s"), (2, 4, 0, 0, 256, "s"), (0, 4, 1, 0, 128, "v"),
-        (2, 4, 2, 0, 128, "s"), (2, 4, 2, 128, 256, "v")),
-}
-QUANT = {1: (0, 1, 2), 0: (0, 1, 2), 2: (1, 0, 2)}
-PLANES = {1: (0, 0), 0: (1, 4), 2: (1, 0)}
+FIRST, SECOND, LAST = 1, 0, 2
+ORDER = (FIRST, SECOND, LAST)
+SCALE_PLACE = {FIRST: (0, 0), SECOND: (1, 4), LAST: (1, 0)}
+
+RUNS = ((0, 256), (256, 128), (384, 256))
+LOW, HIGH, BOTH = (0, 2), (2, 4), (0, 4)
 
 
 def tile_moe_res_lin_none_kernel(tc, xT, xr, w8_words, w8_scales, w4_words, w4_scales, gate, offs, out):
@@ -45,7 +40,7 @@ def tile_moe_res_lin_none_kernel(tc, xT, xr, w8_words, w8_scales, w4_words, w4_s
         psum = ctx.enter_context(tc.psum_pool(name="psum", bufs=1))
 
         offsets = keep.tile([P, S // 16], U16, name="offsets")
-        w_scales = [keep.tile([P, 2, 2, N], U8, name=f"w_scales{h}", align_bytes=64) for h in range(2)]
+        w_scales = [keep.tile([P, n, 2, N], U8, name=f"w_scales{n}", align_bytes=64) for n in (1, E - 1)]
         residual = keep.tile([P, NB, T], F32, name="residual")
         gate_rows = keep.tile([P, P], F32, name="gate_rows")
         gate_wide = keep.tile([P, S], F32, name="gate_wide")
@@ -53,139 +48,157 @@ def tile_moe_res_lin_none_kernel(tc, xT, xr, w8_words, w8_scales, w4_words, w4_s
         windows = [keep.tile([P, T], F32, name=f"window{b}") for b in range(2)]
         slot_y = [keep.tile([P, S], F32, name=f"slot_y{b}") for b in range(NB)]
         results = [keep.tile([P, T], F32, name=f"result{b}") for b in range(NB)]
-        words = [keep.tile([P, WIDE if a < 2 else T], U32, name=f"words{a}", align_bytes=64) for a in range(PASSES)]
-        scales = [keep.tile([P, WIDE if a == 0 else T], U8, name=f"scales{a}", align_bytes=64) for a in range(2)]
-        warm = keep.tile([P, 1], F32, name="warm")
+        words = [keep.tile([P, T if a == LAST else WIDE], U32, name=f"words{a}", align_bytes=64) for a in range(PASSES)]
+        scales = [keep.tile([P, width], U8, name=f"scales{i}", align_bytes=64) for i, width in enumerate((WIDE, T))]
 
-        nc.vector.memset(warm[:], 0.0)
-        nc.scalar.copy(warm[:], warm[:])
+        nc.vector.memset(windows[0][:], 0.0)
+        nc.scalar.copy(windows[1][:], windows[0][:])
         nc.gpsimd.memset(gate_rows[:], 0.0)
         make_identity(nc, ident[:])
-        for plane in scales:
-            nc.vector.memset(plane[:].bitcast(I32), 0)
-        for table in words[:2]:
-            nc.vector.memset(table[:, T:WIDE].bitcast(I32), 0)
-        for plane in w_scales:
-            nc.vector.memset(plane[:].rearrange("p e a n -> p (e a n)").bitcast(I32), 0)
-        for window in windows:
-            nc.vector.memset(window[:], 0.0)
+        for tile in scales:
+            nc.vector.memset(tile[:].bitcast(I32), 0)
+        for a in (SECOND, FIRST):
+            nc.vector.memset(words[a][:, T:WIDE].bitcast(I32), 0)
+        for tile in w_scales:
+            nc.vector.memset(tile[:].rearrange("p e a n -> p (e a n)").bitcast(I32), 0)
 
         x_src = xT.rearrange("(a p u j) t -> a u p (j t)", a=PASSES, u=2, j=2)
-        raw = [keep.tile([P, 4 * T], F32, name=f"raw{a}") for a in range(PASSES)]
-
-        def load_tokens(a, u):
-            nc.sync.dma_start(raw[a][:, 2 * T * u : 2 * T * (u + 1)], x_src[a, u])
-
         w8_src = w8_words.rearrange("e a p n r -> p (e a) (n r)").bitcast(I32)
         w4_src = w4_words.rearrange("e a p b -> p (e a) b").bitcast(I32)
         w8s_src = w8_scales.rearrange("e a (q r) n -> r q (e a) n", r=4).bitcast(I32)
         w4s_src = w4_scales.rearrange("e a (q r) n -> r q (e a) n", r=4).bitcast(I32)
+        xr_src = xr.rearrange("(b p) t -> p b t", p=P)
+        raw = [keep.tile([P, 4 * T], F32, name=f"raw{a}") for a in range(PASSES)]
+        w8, w4 = {}, {}
 
-        weights = {}
+        def load_tokens(a):
+            for u in range(2):
+                nc.sync.dma_start(raw[a][:, 2 * T * u : 2 * T * (u + 1)], x_src[a, u])
 
-        def load_weights(e0, e1, b0, b1):
-            width = (b1 - b0) * P
-            w4 = keep.tile([P, 2 * (e1 - e0), 2 * width], U8, name=f"w4_{e0}{b0}", align_bytes=64)
-            nc.sync.dma_start(w4[:].bitcast(I32), w4_src[:, 2 * e0 : 2 * e1, b0 * P // 2 : b1 * P // 2])
-            w8 = keep.tile([P, e1 - e0, 4 * width], U8, name=f"w8_{e0}{b0}", align_bytes=64)
-            nc.sync.dma_start(w8[:].bitcast(I32), w8_src[:, e0:e1, b0 * P : b1 * P])
-            for e in range(e0, e1):
-                for b in range(b0, b1):
-                    weights[e, b] = (w8[:, e - e0, :], w4[:, 2 * (e - e0) : 2 * (e - e0) + 2, :], b0)
+        def load_weights(e):
+            w4[e] = keep.tile([P, 2, 2 * N], U8, name=f"w4_{e}", align_bytes=64)
+            nc.sync.dma_start(w4[e][:].bitcast(I32), w4_src[:, 2 * e : 2 * e + 2, :])
+            w8[e] = keep.tile([P, 1, 4 * N], U8, name=f"w8_{e}", align_bytes=64)
+            nc.sync.dma_start(w8[e][:].bitcast(I32), w8_src[:, e : e + 1, :])
 
-        def load_w8_scales(e0, e1):
+        def load_w8_scales(tile, e0, e1):
             for r in range(4):
-                nc.sync.dma_start(w_scales[e0 // 2][4 + r : P : 32, :, 0, :].bitcast(I32), w8s_src[r, :, e0:e1, :])
+                nc.sync.dma_start(tile[4 + r : P : 32, :, 0, :].bitcast(I32), w8s_src[r, :, e0:e1, :])
 
-        def load_w4_scales(e0, e1):
+        def load_w4_scales(tile, e0, e1):
             for r in range(4):
-                dst = w_scales[e0 // 2][r:P:32, :, :, :].rearrange("q e a n -> q (e a) n")
+                dst = tile[r:P:32, :, :, :].rearrange("q e a n -> q (e a) n")
                 nc.sync.dma_start(dst.bitcast(I32), w4s_src[r, :, 2 * e0 : 2 * e1, :])
 
-        load_tokens(ORDER[0], 0)
-        load_tokens(ORDER[0], 1)
+        load_tokens(FIRST)
         nc.sync.dma_start(offsets[:], offs)
-        for a in ORDER[1:]:
-            load_tokens(a, 0)
-            load_tokens(a, 1)
+        load_tokens(SECOND)
+        load_tokens(LAST)
         nc.sync.dma_start(gate_rows[0:E, :], gate[0:1, :].rearrange("o (e c) -> (o e) c", c=C))
-        load_w4_scales(0, 2)
-        load_weights(0, 1, 0, NB)
-        load_w8_scales(0, 2)
-        load_weights(1, 2, 0, NB)
-        load_w4_scales(2, 4)
-        load_weights(2, 3, 0, NB)
-        load_w8_scales(2, 4)
-        load_weights(3, 4, 0, NB)
-        xr_src = xr.rearrange("(b p) t -> p b t", p=P)
-        for h in range(2):
-            nc.sync.dma_start(residual[:, 2 * h : 2 * h + 2, :], xr_src[:, 2 * h : 2 * h + 2, :])
+        load_w4_scales(w_scales[0], 0, 1)
+        load_weights(0)
+        load_w8_scales(w_scales[0], 0, 1)
+        load_w4_scales(w_scales[1], 1, E)
+        load_weights(1)
+        load_w8_scales(w_scales[1], 1, E)
+        load_weights(2)
+        load_weights(3)
+        for b0 in (0, 2):
+            nc.sync.dma_start(residual[:, b0 : b0 + 2, :], xr_src[:, b0 : b0 + 2, :])
 
-        gate_cols = []
+        grouped = {
+            (a, run): keep.tile([P, count, 4], BF16, name=f"grouped{a}_{run}", align_bytes=64)
+            for a in ORDER
+            for run, (first, count) in enumerate(RUNS)
+        }
 
-        def spread_gate():
-            turned_gate = psum.tile([P, N], F32, name="turned_gate", tag="turned", bufs=2)
-            nc.tensor.transpose(turned_gate[:, 0:P], gate_rows[:], ident[:])
-            gate_cols.append(keep.tile([P, E], F32, name="gate_cols", tag="raw2"))
-            nc.scalar.copy(gate_cols[0][:], turned_gate[:, 0:E])
-            spread = psum.tile([P, S], F32, name="spread", tag="turned", bufs=2)
-            for e in range(E):
-                nc.tensor.transpose(spread[:, e * C : (e + 1) * C], gate_cols[0][:, e : e + 1].to_broadcast([P, P]), ident[:])
-            nc.scalar.copy(gate_wide[:], spread[:])
-
-        def quantise_pass(a):
-            plane, row = PLANES[a]
-            grouped = [keep.tile([P, n, 4], BF16, name=f"grouped{a}_{t0}", align_bytes=64) for t0, n in PIECES]
+        def cast(copy, a, pair, run, part=None):
+            first, count = RUNS[run]
+            u0, u1 = part or (0, count)
             rows = raw[a][:].rearrange("p (j t) -> p j t", j=4)
-            for j0, j1, piece, u0, u1, engine in CASTS[a]:
-                t0 = PIECES[piece][0]
-                src = rows[:, j0:j1, t0 + u0 : t0 + u1].rearrange("p j (c i) -> p c j i", i=4)
-                dst = grouped[piece][:, u0:u1, j0:j1].rearrange("p (c i) j -> p c j i", i=4)
-                if engine == "v":
-                    nc.vector.tensor_copy(dst, src)
-                else:
-                    nc.scalar.copy(dst, src)
-            for piece in QUANT[a]:
-                tile, (t0, n) = grouped[piece], PIECES[piece]
-                nc.vector.quantize_mx(
-                    out=words[a][:, t0 : t0 + n].bitcast(FP8X4),
-                    scales=scales[plane][row:P, t0 : t0 + n],
-                    in_=tile[:].rearrange("p t j -> p (t j)"),
-                )
+            src = rows[:, pair[0] : pair[1], first + u0 : first + u1].rearrange("p j (c i) -> p c j i", i=4)
+            dst = grouped[a, run][:, u0:u1, pair[0] : pair[1]].rearrange("p (c i) j -> p c j i", i=4)
+            copy(dst, src)
+
+        def quantise(a, run):
+            i, row = SCALE_PLACE[a]
+            first, count = RUNS[run]
+            nc.vector.quantize_mx(
+                out=words[a][:, first : first + count].bitcast(FP8X4),
+                scales=scales[i][row:P, first : first + count],
+                in_=grouped[a, run][:].rearrange("p t j -> p (t j)"),
+            )
 
         def listed(e0, e1):
             return offsets[:, e0 * C // 16 : e1 * C // 16]
 
         slot_words, slot_scales = {}, {}
 
-        def gather(table, dtype, name, e0, e1, tag):
-            tile = keep.tile([P, (e1 - e0) * C], dtype, name=name, tag=tag or name, align_bytes=64)
+        def gather(into, key, table, dtype, e0, e1):
+            sort = "words" if into is slot_words else "scales"
+            tile = keep.tile([P, (e1 - e0) * C], dtype, name=f"slot_{sort}{key}_{e0}", align_bytes=64)
             nc.vector.tensor_copy(tile[:], table[:].indirect(listed(e0, e1)))
-            return {e: (tile, slice((e - e0) * C, (e - e0 + 1) * C)) for e in range(e0, e1)}
+            for e in range(e0, e1):
+                into[key, e] = (tile, slice((e - e0) * C, (e - e0 + 1) * C))
 
-        def gather_words(a, e0, e1, tag=None):
-            for e, place in gather(words[a], U32, f"slot_words{a}{e0}", e0, e1, tag).items():
-                slot_words[a, e] = place
+        on_vector, on_scalar = nc.vector.tensor_copy, nc.scalar.copy
 
-        def gather_scales(plane, e0, e1, tag=None):
-            for e, place in gather(scales[plane], U8, f"slot_scales{plane}{e0}", e0, e1, tag).items():
-                slot_scales[plane, e] = place
+        for pair in (LOW, HIGH):
+            cast(on_vector, FIRST, pair, 0)
+            cast(on_scalar, FIRST, pair, 2)
+            cast(on_vector, FIRST, pair, 1)
+        for run in range(3):
+            quantise(FIRST, run)
+        gather(slot_words, FIRST, words[FIRST], U32, 0, E)
+        gather(slot_scales, 0, scales[0], U8, 0, E)
 
-        gated = {}
+        for pair in (LOW, HIGH):
+            cast(on_scalar, SECOND, pair, 0)
+            cast(on_scalar, SECOND, pair, 1)
+        cast(on_vector, SECOND, BOTH, 2)
+        for run in range(3):
+            quantise(SECOND, run)
+        gather(slot_words, SECOND, words[SECOND], U32, 0, E)
 
-        def multiply(e, b0, b1, sums, tokens_move):
-            n0, n1 = b0 * P, b1 * P
-            w8, w4, first = weights[e, b0]
-            m0, m1 = (b0 - first) * P, (b1 - first) * P
+        cast(on_scalar, LAST, LOW, 0)
+        cast(on_scalar, LAST, LOW, 2)
+        cast(on_scalar, LAST, HIGH, 0)
+        cast(on_vector, LAST, BOTH, 1)
+        cast(on_scalar, LAST, HIGH, 2, (0, 128))
+        cast(on_vector, LAST, HIGH, 2, (128, 256))
+        for run in (1, 0, 2):
+            quantise(LAST, run)
+
+        turned_gate = psum.tile([P, N], F32, name="turned_gate", tag="turned", bufs=2)
+        nc.tensor.transpose(turned_gate[:, 0:P], gate_rows[:], ident[:])
+        gate_cols = keep.tile([P, E], F32, name="gate_cols", tag=f"raw{LAST}")
+        nc.scalar.copy(gate_cols[:], turned_gate[:, 0:E])
+        spread_gate = psum.tile([P, S], F32, name="spread_gate", tag="turned", bufs=2)
+        for e in range(E):
+            nc.tensor.transpose(spread_gate[:, e * C : (e + 1) * C], gate_cols[:, e : e + 1].to_broadcast([P, P]), ident[:])
+        nc.scalar.copy(gate_wide[:], spread_gate[:])
+
+        for e0, e1 in ((0, 1), (1, E)):
+            gather(slot_scales, 1, scales[1], U8, e0, e1)
+            gather(slot_words, LAST, words[LAST], U32, e0, e1)
+
+        for b, tag in ((2, "scales1"), (3, f"words{LAST}")):
+            window = keep.tile([P, T], F32, name=f"window{b}", tag=tag, align_bytes=64)
+            nc.gpsimd.memset(window[:], 0.0)
+            windows.append(window)
+
+        def multiply(e, b, sums, tokens_move):
+            n0, n1 = b * P, (b + 1) * P
+            scale_tile, place = (w_scales[0], 0) if e == 0 else (w_scales[1], e - 1)
             for a in ORDER:
-                plane, row = PLANES[a]
-                if a == 0:
-                    matrix = w8[:, 4 * m0 : 4 * m1].bitcast(FP8X4), w_scales[e // 2][4:P, e % 2, 0, n0:n1]
+                i, row = SCALE_PLACE[a]
+                if a == SECOND:
+                    matrix = w8[e][:, 0, 4 * n0 : 4 * n1].bitcast(FP8X4), scale_tile[row:P, place, 0, n0:n1]
                 else:
-                    matrix = w4[:, a - 1, 2 * m0 : 2 * m1].bitcast(FP4X4), w_scales[e // 2][:, e % 2, a - 1, n0:n1]
-                codes, code_cols = slot_words[a, e]
-                plane_tile, plane_cols = slot_scales[plane, e]
-                tokens = codes[:, code_cols].bitcast(FP8X4), plane_tile[row:P, plane_cols]
+                    matrix = w4[e][:, a - 1, 2 * n0 : 2 * n1].bitcast(FP4X4), scale_tile[row:P, place, a - 1, n0:n1]
+                word_tile, word_cols = slot_words[a, e]
+                byte_tile, byte_cols = slot_scales[i, e]
+                tokens = word_tile[:, word_cols].bitcast(FP8X4), byte_tile[row:P, byte_cols]
                 still, moving = (matrix, tokens) if tokens_move else (tokens, matrix)
                 nc.tensor.matmul_mx(
                     out=sums,
@@ -193,28 +206,33 @@ def tile_moe_res_lin_none_kernel(tc, xT, xr, w8_words, w8_scales, w4_words, w4_s
                     lhsT_scale=still[1],
                     rhs=moving[0],
                     rhs_scale=moving[1],
-                    start=(a == ORDER[0]),
-                    stop=(a == ORDER[-1]),
+                    start=(a == FIRST),
+                    stop=(a == LAST),
                 )
 
-        def weigh(e, bank, b0, b1):
-            tile = keep.tile([P, (b1 - b0) * P], F32, name=f"gated{e}{b0}")
-            nc.scalar.activation(tile[:], bank[:, b0 * P : b1 * P], COPY, scale=gate_cols[0][:, e : e + 1])
-            for b in range(b0, b1):
-                gated[e, b] = tile[:, (b - b0) * P : (b - b0 + 1) * P]
+        early = [(b, 0, 1) for b in range(NB)] + [(b, 1, 2) for b in range(NB - 1)] + [(0, 2, E)]
+        for i, (b, e0, e1) in enumerate(early):
+            bank = psum.tile([P, N], F32, name=f"early{i}", tag=f"early{i % 4}")
+            for e in range(e0, e1):
+                multiply(e, b, bank[:, (e - e0) * C : (e - e0 + 1) * C], True)
+            nc.scalar.copy(slot_y[b][:, e0 * C : e1 * C], bank[:, 0 : (e1 - e0) * C])
 
-        def turn(b, e0, e1):
-            turned = psum.tile([P, N], F32, name=f"turned{b}{e0}", tag="turned", bufs=2)
+        late = [(1, 2, E), (2, 2, E), (3, 1, E)]
+        gated = {}
+        for e in range(1, E):
+            b0 = min(b for b, e0, e1 in late if e0 <= e)
+            bank = psum.tile([P, N], F32, name=f"late{e}", tag=f"late{e % 2}")
+            for b in range(b0, NB):
+                multiply(e, b, bank[:, b * P : (b + 1) * P], False)
+            tile = keep.tile([P, (NB - b0) * P], F32, name=f"gated{e}")
+            nc.scalar.activation(tile[:], bank[:, b0 * P : N], COPY, scale=gate_cols[:, e : e + 1])
+            for b in range(b0, NB):
+                gated[e, b] = tile[:, (b - b0) * P : (b - b0 + 1) * P]
+        for b, e0, e1 in late:
+            turned = psum.tile([P, N], F32, name=f"turned{b}", tag="turned", bufs=2)
             for e in range(e0, e1):
                 nc.tensor.transpose(turned[:, (e - e0) * C : (e - e0 + 1) * C], gated[e, b], ident[:])
             nc.scalar.copy(slot_y[b][:, e0 * C : e1 * C], turned[:, 0 : (e1 - e0) * C])
-
-        def scatter_times_gate(b, e0, e1):
-            cols = slice(e0 * C, e1 * C)
-            nc.vector.tensor_tensor(windows[b][:].indirect(listed(e0, e1)), slot_y[b][:, cols], gate_wide[:, cols], MULT)
-
-        def scatter(b, e0, e1):
-            nc.vector.tensor_copy(windows[b][:].indirect(listed(e0, e1)), slot_y[b][:, e0 * C : e1 * C])
 
         def finish(b, engine, parts):
             for i in range(parts):
@@ -222,41 +240,12 @@ def tile_moe_res_lin_none_kernel(tc, xT, xr, w8_words, w8_scales, w4_words, w4_s
                 engine.tensor_tensor(results[b][:, cols], windows[b][:, cols], residual[:, b, cols], ADD)
                 nc.sync.dma_start(out[b * P : (b + 1) * P, cols], results[b][:, cols])
 
-        quantise_pass(1)
-        gather_words(1, 0, E)
-        gather_scales(0, 0, E)
-        quantise_pass(0)
-        gather_words(0, 0, E)
-        quantise_pass(2)
-        spread_gate()
-        for e0, e1 in ((0, 1), (1, E)):
-            gather_scales(1, e0, e1)
-            gather_words(2, e0, e1)
-        for b, tag in ((2, "scales1"), (3, "words2")):
-            window = keep.tile([P, T], F32, name=f"window{b}", tag=tag, align_bytes=64)
-            nc.gpsimd.memset(window[:], 0.0)
-            windows.append(window)
-        first_units = [(b, 0, 1) for b in range(NB)] + [(b, 1, 2) for b in range(3)] + [(0, 2, 4)]
-        for i, (b, e0, e1) in enumerate(first_units):
-            bank = psum.tile([P, N], F32, name=f"direct{i}", tag=f"bank{i % 4}")
-            for e in range(e0, e1):
-                multiply(e, b, b + 1, bank[:, (e - e0) * C : (e - e0 + 1) * C], True)
-            nc.scalar.copy(slot_y[b][:, e0 * C : e1 * C], bank[:, 0 : (e1 - e0) * C])
-        banks = {}
-        for e, b0 in ((1, 3), (2, 1), (3, 1)):
-            banks[e] = psum.tile([P, N], F32, name=f"late{e}", tag=f"late{e % 2}")
-            for b in range(b0, NB):
-                multiply(e, b, b + 1, banks[e][:, b * P : (b + 1) * P], False)
-            weigh(e, banks[e], b0, NB)
-        turn(1, 2, 4)
-        turn(2, 2, 4)
-        turn(3, 1, 4)
-
-        for unit in first_units:
-            scatter_times_gate(*unit)
+        for b, e0, e1 in early:
+            cols = slice(e0 * C, e1 * C)
+            nc.vector.tensor_tensor(windows[b][:].indirect(listed(e0, e1)), slot_y[b][:, cols], gate_wide[:, cols], MULT)
         finish(0, nc.gpsimd, 1)
-        for b in range(1, NB - 1):
-            scatter(b, 2, 4)
-            finish(b, nc.gpsimd, 1)
-        scatter(3, 1, 4)
-        finish(3, nc.vector, 2)
+        for b, e0, e1 in late:
+            nc.vector.tensor_copy(windows[b][:].indirect(listed(e0, e1)), slot_y[b][:, e0 * C : e1 * C])
+            if b < NB - 1:
+                finish(b, nc.gpsimd, 1)
+        finish(NB - 1, nc.vector, 2)

@@ -25,12 +25,7 @@ MULT = mybir.AluOpType.mult
 FLOPS = 2 * K * N * S
 BYTES = 4 * K * T + 2 * 4 * N * T + E * 512 * N * 4 + E * 1024 * N // 2 + E * 48 * N + 4 * S + 2 * 128 * S // 16
 
-FIRST, SECOND, LAST = 1, 0, 2
-ORDER = (FIRST, SECOND, LAST)
-SCALE_PLACE = {FIRST: (0, 0), SECOND: (1, 4), LAST: (1, 0)}
-
-RUNS = ((0, 256), (256, 128), (384, 256))
-LOW, HIGH, BOTH = (0, 2), (2, 4), (0, 4)
+VECTOR_TOKENS = (320, 176, 0, 0)
 
 
 def tile_moe_res_lin_none_kernel(tc, xT, xr, w8_words, w8_scales, w4_words, w4_scales, gate, offs, out):
@@ -40,40 +35,44 @@ def tile_moe_res_lin_none_kernel(tc, xT, xr, w8_words, w8_scales, w4_words, w4_s
         psum = ctx.enter_context(tc.psum_pool(name="psum", bufs=1))
 
         offsets = keep.tile([P, S // 16], U16, name="offsets")
-        w_scales = [keep.tile([P, n, 2, N], U8, name=f"w_scales{n}", align_bytes=64) for n in (1, E - 1)]
+        w4_planes = [keep.tile([P, n, 2, N], U8, name=f"w4_planes{n}", align_bytes=64) for n in (1, E - 1)]
+        w8_planes = keep.tile([P, N], U8, name="w8_planes", align_bytes=64)
         residual = keep.tile([P, NB, T], F32, name="residual")
         gate_rows = keep.tile([P, P], F32, name="gate_rows")
         gate_wide = keep.tile([P, S], F32, name="gate_wide")
         ident = keep.tile([P, P], F32, name="ident")
-        windows = [keep.tile([P, T], F32, name=f"window{b}") for b in range(2)]
+        windows = [keep.tile([P, T], F32, name=f"window{b}") for b in range(NB)]
         slot_y = [keep.tile([P, S], F32, name=f"slot_y{b}") for b in range(NB)]
         results = [keep.tile([P, T], F32, name=f"result{b}") for b in range(NB)]
-        words = [keep.tile([P, T if a == LAST else WIDE], U32, name=f"words{a}", align_bytes=64) for a in range(PASSES)]
-        scales = [keep.tile([P, width], U8, name=f"scales{i}", align_bytes=64) for i, width in enumerate((WIDE, T))]
+        pairs = [keep.tile([P, WIDE, 2], BF16, name=f"pairs{i}") for i in range(4)]
+        rounded = [keep.tile([P, 2 * T], BF16, name=f"rounded{u}") for u in range(2)]
+
+        def as_words(tile, dtype):
+            return tile[:].rearrange("p t j -> p (t j)").bitcast(dtype)
 
         nc.vector.memset(windows[0][:], 0.0)
-        nc.scalar.copy(windows[1][:], windows[0][:])
+        for b in (1, 2):
+            nc.scalar.copy(windows[b][:], windows[0][:])
+        nc.gpsimd.memset(windows[3][:], 0.0)
+        nc.vector.memset(w8_planes[:].bitcast(I32), 0)
+        for tile in w4_planes:
+            nc.vector.memset(tile[:].rearrange("p e a n -> p (e a n)").bitcast(I32), 0)
+        for i in range(4):
+            nc.vector.memset(as_words(pairs[i], I32)[:, T:WIDE], 0)
         nc.gpsimd.memset(gate_rows[:], 0.0)
         make_identity(nc, ident[:])
-        for tile in scales:
-            nc.vector.memset(tile[:].bitcast(I32), 0)
-        for a in (SECOND, FIRST):
-            nc.vector.memset(words[a][:, T:WIDE].bitcast(I32), 0)
-        for tile in w_scales:
-            nc.vector.memset(tile[:].rearrange("p e a n -> p (e a n)").bitcast(I32), 0)
 
         x_src = xT.rearrange("(a p u j) t -> a u p (j t)", a=PASSES, u=2, j=2)
         w8_src = w8_words.rearrange("e a p n r -> p (e a) (n r)").bitcast(I32)
         w4_src = w4_words.rearrange("e a p b -> p (e a) b").bitcast(I32)
-        w8s_src = w8_scales.rearrange("e a (q r) n -> r q (e a) n", r=4).bitcast(I32)
+        w8s_src = w8_scales.rearrange("e a (q r) n -> q (e a) r n", r=4).bitcast(I32)
         w4s_src = w4_scales.rearrange("e a (q r) n -> r q (e a) n", r=4).bitcast(I32)
         xr_src = xr.rearrange("(b p) t -> p b t", p=P)
-        raw = [keep.tile([P, 4 * T], F32, name=f"raw{a}") for a in range(PASSES)]
+        raw = [keep.tile([P, 2 * T], F32, name=f"raw{i}", align_bytes=64) for i in range(6)]
         w8, w4 = {}, {}
 
-        def load_tokens(a):
-            for u in range(2):
-                nc.sync.dma_start(raw[a][:, 2 * T * u : 2 * T * (u + 1)], x_src[a, u])
+        def load_tokens(i):
+            nc.sync.dma_start(raw[i][:], x_src[i // 2, i % 2])
 
         def load_weights(e):
             w4[e] = keep.tile([P, 2, 2 * N], U8, name=f"w4_{e}", align_bytes=64)
@@ -81,145 +80,128 @@ def tile_moe_res_lin_none_kernel(tc, xT, xr, w8_words, w8_scales, w4_words, w4_s
             w8[e] = keep.tile([P, 1, 4 * N], U8, name=f"w8_{e}", align_bytes=64)
             nc.sync.dma_start(w8[e][:].bitcast(I32), w8_src[:, e : e + 1, :])
 
-        def load_w8_scales(tile, e0, e1):
-            for r in range(4):
-                nc.sync.dma_start(tile[4 + r : P : 32, :, 0, :].bitcast(I32), w8s_src[r, :, e0:e1, :])
-
         def load_w4_scales(tile, e0, e1):
             for r in range(4):
                 dst = tile[r:P:32, :, :, :].rearrange("q e a n -> q (e a) n")
                 nc.sync.dma_start(dst.bitcast(I32), w4s_src[r, :, 2 * e0 : 2 * e1, :])
 
-        load_tokens(FIRST)
+        load_tokens(0)
         nc.sync.dma_start(offsets[:], offs)
-        load_tokens(SECOND)
-        load_tokens(LAST)
-        nc.sync.dma_start(gate_rows[0:E, :], gate[0:1, :].rearrange("o (e c) -> (o e) c", c=C))
-        load_w4_scales(w_scales[0], 0, 1)
+        for i in range(1, 5):
+            load_tokens(i)
+        for q in range(4):
+            nc.sync.dma_start(w8_planes[32 * q : 32 * q + 16, :].bitcast(I32), w8s_src[q])
+        load_tokens(5)
+        load_w4_scales(w4_planes[0], 0, 1)
         load_weights(0)
-        load_w8_scales(w_scales[0], 0, 1)
-        load_w4_scales(w_scales[1], 1, E)
+        nc.sync.dma_start(gate_wide[:, 0:C], gate[0:P, 0:C])
+        load_w4_scales(w4_planes[1], 1, E)
         load_weights(1)
-        load_w8_scales(w_scales[1], 1, E)
+        nc.sync.dma_start(gate_wide[:, C:S], gate[0:P, C:S])
+        nc.sync.dma_start(gate_rows[0:E, :], gate[0:1, :].rearrange("o (e c) -> (o e) c", c=C))
         load_weights(2)
         load_weights(3)
         for b0 in (0, 2):
             nc.sync.dma_start(residual[:, b0 : b0 + 2, :], xr_src[:, b0 : b0 + 2, :])
 
-        grouped = {
-            (a, run): keep.tile([P, count, 4], BF16, name=f"grouped{a}_{run}", align_bytes=64)
-            for a in ORDER
-            for run, (first, count) in enumerate(RUNS)
-        }
-
-        def cast(copy, a, pair, run, part=None):
-            first, count = RUNS[run]
-            u0, u1 = part or (0, count)
-            rows = raw[a][:].rearrange("p (j t) -> p j t", j=4)
-            src = rows[:, pair[0] : pair[1], first + u0 : first + u1].rearrange("p j (c i) -> p c j i", i=4)
-            dst = grouped[a, run][:, u0:u1, pair[0] : pair[1]].rearrange("p (c i) j -> p c j i", i=4)
-            copy(dst, src)
-
-        def quantise(a, run):
-            i, row = SCALE_PLACE[a]
-            first, count = RUNS[run]
-            nc.vector.quantize_mx(
-                out=words[a][:, first : first + count].bitcast(FP8X4),
-                scales=scales[i][row:P, first : first + count],
-                in_=grouped[a, run][:].rearrange("p t j -> p (t j)"),
-            )
+        def cast(i):
+            rows = raw[i][:].rearrange("p (j t) -> p j t", j=2)
+            cut = VECTOR_TOKENS[i]
+            for copy, t0, t1 in ((nc.vector.tensor_copy, 0, cut), (nc.scalar.copy, cut, T)):
+                if t1 > t0:
+                    src = rows[:, :, t0:t1].rearrange("p j (c i) -> p c j i", i=4)
+                    dst = pairs[i][:, t0:t1, :].rearrange("p (c i) j -> p c j i", i=4)
+                    copy(dst, src)
 
         def listed(e0, e1):
             return offsets[:, e0 * C // 16 : e1 * C // 16]
 
-        slot_words, slot_scales = {}, {}
+        gathered = [keep.tile([P, 2, S], U32, name=f"gathered{a}") for a in range(2)]
+        codes = {}
 
-        def gather(into, key, table, dtype, e0, e1):
-            sort = "words" if into is slot_words else "scales"
-            tile = keep.tile([P, (e1 - e0) * C], dtype, name=f"slot_{sort}{key}_{e0}", align_bytes=64)
-            nc.vector.tensor_copy(tile[:], table[:].indirect(listed(e0, e1)))
-            for e in range(e0, e1):
-                into[key, e] = (tile, slice((e - e0) * C, (e - e0 + 1) * C))
+        def gather(a, u):
+            nc.vector.tensor_copy(gathered[a][:, u, :], as_words(pairs[2 * a + u], U32).indirect(listed(0, E)))
 
-        on_vector, on_scalar = nc.vector.tensor_copy, nc.scalar.copy
+        def weave(a, e0, e1):
+            width = 4 * C * (e1 - e0)
+            dst = woven[e0][:, a * width : (a + 1) * width].bitcast(U32).rearrange("p (c i u) -> p c u i", i=4, u=2)
+            nc.scalar.copy(dst, gathered[a][:, :, e0 * C : e1 * C].rearrange("p u (c i) -> p c u i", i=4))
 
-        for pair in (LOW, HIGH):
-            cast(on_vector, FIRST, pair, 0)
-            cast(on_scalar, FIRST, pair, 2)
-            cast(on_vector, FIRST, pair, 1)
-        for run in range(3):
-            quantise(FIRST, run)
-        gather(slot_words, FIRST, words[FIRST], U32, 0, E)
-        gather(slot_scales, 0, scales[0], U8, 0, E)
+        def quantise(a0, a1, e0, e1, values, words=None):
+            n = (e1 - e0) * C
+            if words is None:
+                words = keep.tile([P, (a1 - a0) * n], U32, name=f"words{a0}_{e0}", align_bytes=64)
+                words = words[:]
+            plane = keep.tile([P, (a1 - a0) * n], U8, name=f"plane{a0}_{e0}", align_bytes=64)
+            nc.vector.quantize_mx(out=words.bitcast(FP8X4), scales=plane[:], in_=values)
+            for a in range(a0, a1):
+                for e in range(e0, e1):
+                    first = (a - a0) * n + (e - e0) * C
+                    codes[a, e] = (words[:, first : first + C].bitcast(FP8X4), plane[:, first : first + C])
 
-        for pair in (LOW, HIGH):
-            cast(on_scalar, SECOND, pair, 0)
-            cast(on_scalar, SECOND, pair, 1)
-        cast(on_vector, SECOND, BOTH, 2)
-        for run in range(3):
-            quantise(SECOND, run)
-        gather(slot_words, SECOND, words[SECOND], U32, 0, E)
+        def gather_last_on_scalar(e, tag):
+            values = keep.tile([P, C, 4], BF16, name=f"last{e}", tag=tag, align_bytes=64)
+            for j in range(4):
+                row = rounded[j // 2][:, j % 2 * T : (j % 2 + 1) * T]
+                nc.scalar.activation(values[:, :, j], row.indirect(listed(e, e + 1)), COPY)
+            quantise(2, 3, e, e + 1, values[:].rearrange("p s j -> p (s j)"))
 
-        cast(on_scalar, LAST, LOW, 0)
-        cast(on_scalar, LAST, LOW, 2)
-        cast(on_scalar, LAST, HIGH, 0)
-        cast(on_vector, LAST, BOTH, 1)
-        cast(on_scalar, LAST, HIGH, 2, (0, 128))
-        cast(on_vector, LAST, HIGH, 2, (128, 256))
-        for run in (1, 0, 2):
-            quantise(LAST, run)
+        groups = ((0, 1), (1, 2), (2, E))
+        cast(0)
+        gather(0, 0)
+        cast(1)
+        gather(0, 1)
+        cast(2)
+        gather(1, 0)
+        cast(3)
+        gather(1, 1)
+        woven_all = keep.tile([P, 2 * S * 4], BF16, name="woven", tag="raw3", align_bytes=64)
+        woven = {e0: woven_all[:, 8 * C * e0 : 8 * C * e1] for e0, e1 in groups}
+        for u in range(2):
+            nc.gpsimd.tensor_copy(rounded[u][:], raw[4 + u][:])
+        for a in range(2):
+            for e0, e1 in groups:
+                weave(a, e0, e1)
+        last0 = keep.tile([P, C, 4], BF16, name="last0", align_bytes=64)
+        for j in range(4):
+            row = raw[4 + j // 2][:, j % 2 * T : (j % 2 + 1) * T]
+            nc.vector.tensor_copy(last0[:, :, j], row.indirect(listed(0, 1)))
+        early_words = keep.tile([P, 2 * S], U32, name="early_words", tag="raw5", align_bytes=64)
+        quantise(0, 2, 0, 1, woven[0], early_words[:, 0 : 2 * C])
+        quantise(2, 3, 0, 1, last0[:].rearrange("p s j -> p (s j)"))
+        for e0, e1 in groups[1:]:
+            quantise(0, 2, e0, e1, woven[e0], early_words[:, 2 * C * e0 : 2 * C * e1])
+        gather_last_on_scalar(1, "last1")
 
         turned_gate = psum.tile([P, N], F32, name="turned_gate", tag="turned", bufs=2)
         nc.tensor.transpose(turned_gate[:, 0:P], gate_rows[:], ident[:])
-        gate_cols = keep.tile([P, E], F32, name="gate_cols", tag=f"raw{LAST}")
+        gate_cols = keep.tile([P, E], F32, name="gate_cols")
         nc.scalar.copy(gate_cols[:], turned_gate[:, 0:E])
-        spread_gate = psum.tile([P, S], F32, name="spread_gate", tag="turned", bufs=2)
-        for e in range(E):
-            nc.tensor.transpose(spread_gate[:, e * C : (e + 1) * C], gate_cols[:, e : e + 1].to_broadcast([P, P]), ident[:])
-        nc.scalar.copy(gate_wide[:], spread_gate[:])
-
-        for e0, e1 in ((0, 1), (1, E)):
-            gather(slot_scales, 1, scales[1], U8, e0, e1)
-            gather(slot_words, LAST, words[LAST], U32, e0, e1)
-
-        for b, tag in ((2, "scales1"), (3, f"words{LAST}")):
-            window = keep.tile([P, T], F32, name=f"window{b}", tag=tag, align_bytes=64)
-            nc.gpsimd.memset(window[:], 0.0)
-            windows.append(window)
 
         def multiply(e, b, sums, tokens_move):
             n0, n1 = b * P, (b + 1) * P
-            scale_tile, place = (w_scales[0], 0) if e == 0 else (w_scales[1], e - 1)
-            for a in ORDER:
-                i, row = SCALE_PLACE[a]
-                if a == SECOND:
-                    matrix = w8[e][:, 0, 4 * n0 : 4 * n1].bitcast(FP8X4), scale_tile[row:P, place, 0, n0:n1]
+            plane, place = (w4_planes[0], 0) if e == 0 else (w4_planes[1], e - 1)
+            for a in range(PASSES):
+                if a == 0:
+                    matrix = w8[e][:, 0, 4 * n0 : 4 * n1].bitcast(FP8X4), w8_planes[4 * e : P, n0:n1]
                 else:
-                    matrix = w4[e][:, a - 1, 2 * n0 : 2 * n1].bitcast(FP4X4), scale_tile[row:P, place, a - 1, n0:n1]
-                word_tile, word_cols = slot_words[a, e]
-                byte_tile, byte_cols = slot_scales[i, e]
-                tokens = word_tile[:, word_cols].bitcast(FP8X4), byte_tile[row:P, byte_cols]
-                still, moving = (matrix, tokens) if tokens_move else (tokens, matrix)
+                    matrix = w4[e][:, a - 1, 2 * n0 : 2 * n1].bitcast(FP4X4), plane[:, place, a - 1, n0:n1]
+                still, moving = (matrix, codes[a, e]) if tokens_move else (codes[a, e], matrix)
                 nc.tensor.matmul_mx(
                     out=sums,
                     lhsT=still[0],
                     lhsT_scale=still[1],
                     rhs=moving[0],
                     rhs_scale=moving[1],
-                    start=(a == FIRST),
-                    stop=(a == LAST),
+                    start=(a == 0),
+                    stop=(a == PASSES - 1),
                 )
 
-        early = [(b, 0, 1) for b in range(NB)] + [(b, 1, 2) for b in range(NB - 1)] + [(0, 2, E)]
-        for i, (b, e0, e1) in enumerate(early):
-            bank = psum.tile([P, N], F32, name=f"early{i}", tag=f"early{i % 4}")
-            for e in range(e0, e1):
-                multiply(e, b, bank[:, (e - e0) * C : (e - e0 + 1) * C], True)
-            nc.scalar.copy(slot_y[b][:, e0 * C : e1 * C], bank[:, 0 : (e1 - e0) * C])
-
-        late = [(1, 2, E), (2, 2, E), (3, 1, E)]
+        early = [(b, 0, 1) for b in range(NB)] + [(b, 1, 2) for b in range(NB - 1)] + [(0, 2, 3), (1, 2, 3), (0, 3, 4)]
+        late = [(1, 3, E), (2, 2, E), (3, 1, E)]
         gated = {}
-        for e in range(1, E):
+
+        def multiply_late(e):
             b0 = min(b for b, e0, e1 in late if e0 <= e)
             bank = psum.tile([P, N], F32, name=f"late{e}", tag=f"late{e % 2}")
             for b in range(b0, NB):
@@ -228,6 +210,20 @@ def tile_moe_res_lin_none_kernel(tc, xT, xr, w8_words, w8_scales, w4_words, w4_s
             nc.scalar.activation(tile[:], bank[:, b0 * P : N], COPY, scale=gate_cols[:, e : e + 1])
             for b in range(b0, NB):
                 gated[e, b] = tile[:, (b - b0) * P : (b - b0 + 1) * P]
+
+        for i, (b, e0, e1) in enumerate(early):
+            if (b, e0) == (0, 1):
+                gather_last_on_scalar(2, "words2_0")
+            if (b, e0) == (0, 2):
+                multiply_late(1)
+                gather_last_on_scalar(3, "words2_1")
+            bank = psum.tile([P, N], F32, name=f"early{i}", tag=f"early{i % 4}")
+            for e in range(e0, e1):
+                multiply(e, b, bank[:, (e - e0) * C : (e - e0 + 1) * C], True)
+            nc.scalar.copy(slot_y[b][:, e0 * C : e1 * C], bank[:, 0 : (e1 - e0) * C])
+
+        for e in range(2, E):
+            multiply_late(e)
         for b, e0, e1 in late:
             turned = psum.tile([P, N], F32, name=f"turned{b}", tag="turned", bufs=2)
             for e in range(e0, e1):

@@ -45,7 +45,7 @@ def tile_moe_res_lin_none_kernel(tc, xT, xr, w8_words, w8_scales, w4_words, w4_s
         slot_y = [keep.tile([P, S], F32, name=f"slot_y{b}") for b in range(NB)]
         results = [keep.tile([P, T], F32, name=f"result{b}") for b in range(NB)]
         pairs = [keep.tile([P, WIDE, 2], BF16, name=f"pairs{i}") for i in range(4)]
-        rounded = [keep.tile([P, 2 * T], BF16, name=f"rounded{u}") for u in range(2)]
+        rounded = [keep.tile([P, T], BF16, name=f"rounded{j}") for j in range(4)]
 
         def as_words(tile, dtype):
             return tile[:].rearrange("p t j -> p (t j)").bitcast(dtype)
@@ -68,7 +68,8 @@ def tile_moe_res_lin_none_kernel(tc, xT, xr, w8_words, w8_scales, w4_words, w4_s
         w8s_src = w8_scales.rearrange("e a (q r) n -> q (e a) r n", r=4).bitcast(I32)
         w4s_src = w4_scales.rearrange("e a (q r) n -> r q (e a) n", r=4).bitcast(I32)
         xr_src = xr.rearrange("(b p) t -> p b t", p=P)
-        raw = [keep.tile([P, 2 * T], F32, name=f"raw{i}", align_bytes=64) for i in range(6)]
+        raw = [keep.tile([P, 2 * T], F32, name=f"raw{i}", align_bytes=64) for i in range(5)]
+        last_rows = [keep.tile([P, T], F32, name=f"last_row{j}", align_bytes=64) for j in range(2)]
         w8, w4 = {}, {}
 
         def load_tokens(i):
@@ -91,7 +92,8 @@ def tile_moe_res_lin_none_kernel(tc, xT, xr, w8_words, w8_scales, w4_words, w4_s
             load_tokens(i)
         for q in range(4):
             nc.sync.dma_start(w8_planes[32 * q : 32 * q + 16, :].bitcast(I32), w8s_src[q])
-        load_tokens(5)
+        for j in range(2):
+            nc.sync.dma_start(last_rows[j][:], x_src[2, 1][:, j * T : (j + 1) * T])
         load_w4_scales(w4_planes[0], 0, 1)
         load_weights(0)
         nc.sync.dma_start(gate_wide[:, 0:C], gate[0:P, 0:C])
@@ -122,56 +124,55 @@ def tile_moe_res_lin_none_kernel(tc, xT, xr, w8_words, w8_scales, w4_words, w4_s
         def gather(a, u):
             nc.vector.tensor_copy(gathered[a][:, u, :], as_words(pairs[2 * a + u], U32).indirect(listed(0, E)))
 
-        def weave(a, e0, e1):
-            width = 4 * C * (e1 - e0)
-            dst = woven[e0][:, a * width : (a + 1) * width].bitcast(U32).rearrange("p (c i u) -> p c u i", i=4, u=2)
-            nc.scalar.copy(dst, gathered[a][:, :, e0 * C : e1 * C].rearrange("p u (c i) -> p c u i", i=4))
+        def weave(copy, dtype, a, e0, e1, into):
+            dst = into.bitcast(dtype).rearrange("p (c i u) -> p c u i", i=4, u=2)
+            copy(dst, gathered[a][:, :, e0 * C : e1 * C].bitcast(dtype).rearrange("p u (c i) -> p c u i", i=4))
 
-        def quantise(a0, a1, e0, e1, values, words=None):
-            n = (e1 - e0) * C
-            if words is None:
-                words = keep.tile([P, (a1 - a0) * n], U32, name=f"words{a0}_{e0}", align_bytes=64)
-                words = words[:]
-            plane = keep.tile([P, (a1 - a0) * n], U8, name=f"plane{a0}_{e0}", align_bytes=64)
+        def quantise(a, e0, e1, values, words):
+            plane = keep.tile([P, (e1 - e0) * C], U8, name=f"plane{a}_{e0}", align_bytes=64)
             nc.vector.quantize_mx(out=words.bitcast(FP8X4), scales=plane[:], in_=values)
-            for a in range(a0, a1):
-                for e in range(e0, e1):
-                    first = (a - a0) * n + (e - e0) * C
-                    codes[a, e] = (words[:, first : first + C].bitcast(FP8X4), plane[:, first : first + C])
+            for e in range(e0, e1):
+                cols = slice((e - e0) * C, (e - e0 + 1) * C)
+                codes[a, e] = (words[:, cols].bitcast(FP8X4), plane[:, cols])
 
-        def gather_last_on_scalar(e, tag):
+        def gather_last(e, tag):
             values = keep.tile([P, C, 4], BF16, name=f"last{e}", tag=tag, align_bytes=64)
             for j in range(4):
-                row = rounded[j // 2][:, j % 2 * T : (j % 2 + 1) * T]
-                nc.scalar.activation(values[:, :, j], row.indirect(listed(e, e + 1)), COPY)
-            quantise(2, 3, e, e + 1, values[:].rearrange("p s j -> p (s j)"))
+                nc.scalar.activation(values[:, :, j], rounded[j][:].indirect(listed(e, e + 1)), COPY)
+            return values
 
-        groups = ((0, 1), (1, 2), (2, E))
-        cast(0)
-        gather(0, 0)
-        cast(1)
-        gather(0, 1)
-        cast(2)
-        gather(1, 0)
-        cast(3)
-        gather(1, 1)
-        woven_all = keep.tile([P, 2 * S * 4], BF16, name="woven", tag="raw3", align_bytes=64)
-        woven = {e0: woven_all[:, 8 * C * e0 : 8 * C * e1] for e0, e1 in groups}
-        for u in range(2):
-            nc.gpsimd.tensor_copy(rounded[u][:], raw[4 + u][:])
-        for a in range(2):
-            for e0, e1 in groups:
-                weave(a, e0, e1)
+        def quantise_last(e, values):
+            words = keep.tile([P, C], U32, name=f"words2_{e}", align_bytes=64)
+            quantise(2, e, e + 1, values[:].rearrange("p s j -> p (s j)"), words[:])
+
+        woven = [keep.tile([P, 4 * S], BF16, name="woven0", align_bytes=64)]
+        for i in range(4):
+            cast(i)
+            gather(i // 2, i % 2)
+            if i == 1:
+                weave(nc.vector.tensor_copy, I32, 0, 0, E, woven[0][:])
+        nc.gpsimd.tensor_copy(rounded[0][:], raw[4][:, 0:T])
+        nc.scalar.copy(rounded[1][:], raw[4][:, T : 2 * T])
         last0 = keep.tile([P, C, 4], BF16, name="last0", align_bytes=64)
-        for j in range(4):
-            row = raw[4 + j // 2][:, j % 2 * T : (j % 2 + 1) * T]
-            nc.vector.tensor_copy(last0[:, :, j], row.indirect(listed(0, 1)))
-        early_words = keep.tile([P, 2 * S], U32, name="early_words", tag="raw5", align_bytes=64)
-        quantise(0, 2, 0, 1, woven[0], early_words[:, 0 : 2 * C])
-        quantise(2, 3, 0, 1, last0[:].rearrange("p s j -> p (s j)"))
-        for e0, e1 in groups[1:]:
-            quantise(0, 2, e0, e1, woven[e0], early_words[:, 2 * C * e0 : 2 * C * e1])
-        gather_last_on_scalar(1, "last1")
+        for j in range(2):
+            nc.scalar.activation(last0[:, :, j], rounded[j][:].indirect(listed(0, 1)), COPY)
+        groups = ((0, 1), (1, 2), (2, E))
+        woven.append(keep.tile([P, 8 * C], BF16, name="woven1", tag="raw4", align_bytes=64))
+        for e in range(2):
+            weave(nc.scalar.copy, U32, 1, e, e + 1, woven[1][:, 4 * C * e : 4 * C * (e + 1)])
+        for j in range(2):
+            nc.vector.tensor_copy(last0[:, :, 2 + j], last_rows[j][:].indirect(listed(0, 1)))
+            nc.gpsimd.tensor_copy(rounded[2 + j][:], last_rows[j][:])
+        quantise_last(0, last0)
+        early_words = keep.tile([P, 2, S], U32, name="early_words", tag="last_row1", align_bytes=64)
+        for e in range(2):
+            for a in range(2):
+                quantise(a, e, e + 1, woven[a][:, 4 * C * e : 4 * C * (e + 1)], early_words[:, a, C * e : C * (e + 1)])
+        woven_late = keep.tile([P, 8 * C], BF16, name="woven_late", tag="last0", align_bytes=64)
+        weave(nc.vector.tensor_copy, I32, 1, 2, E, woven_late[:])
+        quantise(0, 2, E, woven[0][:, 8 * C : 16 * C], early_words[:, 0, 2 * C : S])
+        quantise(1, 2, E, woven_late[:], early_words[:, 1, 2 * C : S])
+        quantise_last(1, gather_last(1, "last1"))
 
         turned_gate = psum.tile([P, N], F32, name="turned_gate", tag="turned", bufs=2)
         nc.tensor.transpose(turned_gate[:, 0:P], gate_rows[:], ident[:])
@@ -213,10 +214,10 @@ def tile_moe_res_lin_none_kernel(tc, xT, xr, w8_words, w8_scales, w4_words, w4_s
 
         for i, (b, e0, e1) in enumerate(early):
             if (b, e0) == (0, 1):
-                gather_last_on_scalar(2, "words2_0")
+                quantise_last(2, gather_last(2, "words2_0"))
             if (b, e0) == (0, 2):
                 multiply_late(1)
-                gather_last_on_scalar(3, "words2_1")
+                quantise_last(3, gather_last(3, "words2_1"))
             bank = psum.tile([P, N], F32, name=f"early{i}", tag=f"early{i % 4}")
             for e in range(e0, e1):
                 multiply(e, b, bank[:, (e - e0) * C : (e - e0 + 1) * C], True)

@@ -41,7 +41,7 @@ def tile_moe_res_lin_none_kernel(tc, xT, xr, w8_words, w8_scales, w4_words, w4_s
         gate_rows = keep.tile([P, P], F32, name="gate_rows")
         gate_wide = keep.tile([P, S], F32, name="gate_wide")
         ident = keep.tile([P, P], F32, name="ident")
-        windows = [keep.tile([P, T], F32, name=f"window{b}") for b in range(NB)]
+        windows = [keep.tile([P, T], F32, name=f"window{b}") for b in range(2)]
         slot_y = [keep.tile([P, S], F32, name=f"slot_y{b}") for b in range(NB)]
         results = [keep.tile([P, T], F32, name=f"result{b}") for b in range(NB)]
         pairs = [keep.tile([P, WIDE, 2], BF16, name=f"pairs{i}") for i in range(4)]
@@ -51,9 +51,7 @@ def tile_moe_res_lin_none_kernel(tc, xT, xr, w8_words, w8_scales, w4_words, w4_s
             return tile[:].rearrange("p t j -> p (t j)").bitcast(dtype)
 
         nc.vector.memset(windows[0][:], 0.0)
-        for b in (1, 2):
-            nc.scalar.copy(windows[b][:], windows[0][:])
-        nc.gpsimd.memset(windows[3][:], 0.0)
+        nc.scalar.copy(windows[1][:], windows[0][:])
         nc.vector.memset(w8_planes[:].bitcast(I32), 0)
         for tile in w4_planes:
             nc.vector.memset(tile[:].rearrange("p e a n -> p (e a n)").bitcast(I32), 0)
@@ -75,11 +73,16 @@ def tile_moe_res_lin_none_kernel(tc, xT, xr, w8_words, w8_scales, w4_words, w4_s
         def load_tokens(i):
             nc.sync.dma_start(raw[i][:], x_src[i // 2, i % 2])
 
-        def load_weights(e):
-            w4[e] = keep.tile([P, 2, 2 * N], U8, name=f"w4_{e}", align_bytes=64)
-            nc.sync.dma_start(w4[e][:].bitcast(I32), w4_src[:, 2 * e : 2 * e + 2, :])
-            w8[e] = keep.tile([P, 1, 4 * N], U8, name=f"w8_{e}", align_bytes=64)
-            nc.sync.dma_start(w8[e][:].bitcast(I32), w8_src[:, e : e + 1, :])
+        def load_weights(e, n0, n1):
+            tile4 = keep.tile([P, 2, 2 * (n1 - n0)], U8, name=f"w4_{e}_{n0}", align_bytes=64)
+            nc.sync.dma_start(tile4[:].bitcast(I32), w4_src[:, 2 * e : 2 * e + 2, n0 // 2 : n1 // 2])
+            tile8 = keep.tile([P, 4 * (n1 - n0)], U8, name=f"w8_{e}_{n0}", align_bytes=64)
+            nc.sync.dma_start(tile8[:].bitcast(I32), w8_src[:, e, n0:n1])
+            for b in range(n0 // P, n1 // P):
+                first = b * P - n0
+                w8[e, b] = tile8[:, 4 * first : 4 * (first + P)].bitcast(FP8X4)
+                for a in (1, 2):
+                    w4[e, a, b] = tile4[:, a - 1, 2 * first : 2 * (first + P)].bitcast(FP4X4)
 
         def load_w4_scales(tile, e0, e1):
             for r in range(4):
@@ -95,14 +98,15 @@ def tile_moe_res_lin_none_kernel(tc, xT, xr, w8_words, w8_scales, w4_words, w4_s
         for j in range(2):
             nc.sync.dma_start(last_rows[j][:], x_src[2, 1][:, j * T : (j + 1) * T])
         load_w4_scales(w4_planes[0], 0, 1)
-        load_weights(0)
+        load_weights(0, 0, N // 2)
         nc.sync.dma_start(gate_wide[:, 0:C], gate[0:P, 0:C])
+        load_weights(0, N // 2, N)
         load_w4_scales(w4_planes[1], 1, E)
-        load_weights(1)
+        load_weights(2, 0, N)
         nc.sync.dma_start(gate_wide[:, C:S], gate[0:P, C:S])
         nc.sync.dma_start(gate_rows[0:E, :], gate[0:1, :].rearrange("o (e c) -> (o e) c", c=C))
-        load_weights(2)
-        load_weights(3)
+        load_weights(1, 0, N)
+        load_weights(3, 0, N)
         for b0 in (0, 2):
             nc.sync.dma_start(residual[:, b0 : b0 + 2, :], xr_src[:, b0 : b0 + 2, :])
 
@@ -145,34 +149,41 @@ def tile_moe_res_lin_none_kernel(tc, xT, xr, w8_words, w8_scales, w4_words, w4_s
             words = keep.tile([P, C], U32, name=f"words2_{e}", align_bytes=64)
             quantise(2, e, e + 1, values[:].rearrange("p s j -> p (s j)"), words[:])
 
-        woven = [keep.tile([P, 4 * S], BF16, name="woven0", align_bytes=64)]
+        woven = [keep.tile([P, 12 * C], BF16, name="woven0", align_bytes=64)]
         for i in range(4):
             cast(i)
             gather(i // 2, i % 2)
+            if i < 2:
+                window = keep.tile([P, T], F32, name=f"window{2 + i}", tag=f"raw{i}", align_bytes=64)
+                nc.gpsimd.memset(window[:], 0.0)
+                windows.append(window)
             if i == 1:
-                weave(nc.vector.tensor_copy, I32, 0, 0, E, woven[0][:])
+                weave(nc.vector.tensor_copy, I32, 0, 0, 3, woven[0][:])
+            if i == 2:
+                woven0_late = keep.tile([P, 4 * C], BF16, name="woven0_late", tag="raw2", align_bytes=64)
+                weave(nc.gpsimd.tensor_copy, I32, 0, 3, E, woven0_late[:])
         nc.gpsimd.tensor_copy(rounded[0][:], raw[4][:, 0:T])
         nc.scalar.copy(rounded[1][:], raw[4][:, T : 2 * T])
         last0 = keep.tile([P, C, 4], BF16, name="last0", align_bytes=64)
         for j in range(2):
             nc.scalar.activation(last0[:, :, j], rounded[j][:].indirect(listed(0, 1)), COPY)
         groups = ((0, 1), (1, 2), (2, E))
-        woven.append(keep.tile([P, 8 * C], BF16, name="woven1", tag="raw4", align_bytes=64))
-        for e in range(2):
-            weave(nc.scalar.copy, U32, 1, e, e + 1, woven[1][:, 4 * C * e : 4 * C * (e + 1)])
+        woven.append(keep.tile([P, 4 * C], BF16, name="woven1", tag="raw4", align_bytes=64))
+        weave(nc.scalar.copy, U32, 1, 0, 1, woven[1][:])
         for j in range(2):
             nc.vector.tensor_copy(last0[:, :, 2 + j], last_rows[j][:].indirect(listed(0, 1)))
             nc.gpsimd.tensor_copy(rounded[2 + j][:], last_rows[j][:])
         quantise_last(0, last0)
         early_words = keep.tile([P, 2, S], U32, name="early_words", tag="last_row1", align_bytes=64)
-        for e in range(2):
-            for a in range(2):
-                quantise(a, e, e + 1, woven[a][:, 4 * C * e : 4 * C * (e + 1)], early_words[:, a, C * e : C * (e + 1)])
-        woven_late = keep.tile([P, 8 * C], BF16, name="woven_late", tag="last0", align_bytes=64)
-        weave(nc.vector.tensor_copy, I32, 1, 2, E, woven_late[:])
-        quantise(0, 2, E, woven[0][:, 8 * C : 16 * C], early_words[:, 0, 2 * C : S])
-        quantise(1, 2, E, woven_late[:], early_words[:, 1, 2 * C : S])
-        quantise_last(1, gather_last(1, "last1"))
+        quantise(1, 0, 1, woven[1][:, 0 : 4 * C], early_words[:, 1, 0:C])
+        quantise(0, 0, 1, woven[0][:, 0 : 4 * C], early_words[:, 0, 0:C])
+        quantise(0, 1, 3, woven[0][:, 4 * C : 12 * C], early_words[:, 0, C : 3 * C])
+        woven_late = keep.tile([P, 12 * C], BF16, name="woven_late", tag="raw4", align_bytes=64)
+        weave(nc.vector.tensor_copy, I32, 1, 1, E, woven_late[:])
+        quantise(0, 3, E, woven0_late[:], early_words[:, 0, 3 * C : S])
+        quantise(1, 1, 3, woven_late[:, 0 : 8 * C], early_words[:, 1, C : 3 * C])
+        quantise(1, 3, E, woven_late[:, 8 * C : 12 * C], early_words[:, 1, 3 * C : S])
+        quantise_last(2, gather_last(2, "last2"))
 
         turned_gate = psum.tile([P, N], F32, name="turned_gate", tag="turned", bufs=2)
         nc.tensor.transpose(turned_gate[:, 0:P], gate_rows[:], ident[:])
@@ -182,11 +193,11 @@ def tile_moe_res_lin_none_kernel(tc, xT, xr, w8_words, w8_scales, w4_words, w4_s
         def multiply(e, b, sums, tokens_move):
             n0, n1 = b * P, (b + 1) * P
             plane, place = (w4_planes[0], 0) if e == 0 else (w4_planes[1], e - 1)
-            for a in range(PASSES):
+            for a in (2, 1, 0):
                 if a == 0:
-                    matrix = w8[e][:, 0, 4 * n0 : 4 * n1].bitcast(FP8X4), w8_planes[4 * e : P, n0:n1]
+                    matrix = w8[e, b], w8_planes[4 * e : P, n0:n1]
                 else:
-                    matrix = w4[e][:, a - 1, 2 * n0 : 2 * n1].bitcast(FP4X4), plane[:, place, a - 1, n0:n1]
+                    matrix = w4[e, a, b], plane[:, place, a - 1, n0:n1]
                 still, moving = (matrix, codes[a, e]) if tokens_move else (codes[a, e], matrix)
                 nc.tensor.matmul_mx(
                     out=sums,
@@ -194,11 +205,11 @@ def tile_moe_res_lin_none_kernel(tc, xT, xr, w8_words, w8_scales, w4_words, w4_s
                     lhsT_scale=still[1],
                     rhs=moving[0],
                     rhs_scale=moving[1],
-                    start=(a == 0),
-                    stop=(a == PASSES - 1),
+                    start=(a == 2),
+                    stop=(a == 0),
                 )
 
-        early = [(b, 0, 1) for b in range(NB)] + [(b, 1, 2) for b in range(NB - 1)] + [(0, 2, 3), (1, 2, 3), (0, 3, 4)]
+        early = [(b, 0, 1) for b in range(NB)] + [(b, 2, 3) for b in range(2)] + [(b, 1, 2) for b in range(3)] + [(0, 3, 4)]
         late = [(1, 3, E), (2, 2, E), (3, 1, E)]
         gated = {}
 
@@ -213,17 +224,17 @@ def tile_moe_res_lin_none_kernel(tc, xT, xr, w8_words, w8_scales, w4_words, w4_s
                 gated[e, b] = tile[:, (b - b0) * P : (b - b0 + 1) * P]
 
         for i, (b, e0, e1) in enumerate(early):
-            if (b, e0) == (0, 1):
-                quantise_last(2, gather_last(2, "words2_0"))
             if (b, e0) == (0, 2):
-                multiply_late(1)
-                quantise_last(3, gather_last(3, "words2_1"))
+                quantise_last(1, gather_last(1, "w8_0_256"))
+            if (b, e0) == (0, 1):
+                multiply_late(2)
+                quantise_last(3, gather_last(3, "w8_2_0"))
             bank = psum.tile([P, N], F32, name=f"early{i}", tag=f"early{i % 4}")
             for e in range(e0, e1):
                 multiply(e, b, bank[:, (e - e0) * C : (e - e0 + 1) * C], True)
             nc.scalar.copy(slot_y[b][:, e0 * C : e1 * C], bank[:, 0 : (e1 - e0) * C])
 
-        for e in range(2, E):
+        for e in (1, 3):
             multiply_late(e)
         for b, e0, e1 in late:
             turned = psum.tile([P, N], F32, name=f"turned{b}", tag="turned", bufs=2)
@@ -231,18 +242,18 @@ def tile_moe_res_lin_none_kernel(tc, xT, xr, w8_words, w8_scales, w4_words, w4_s
                 nc.tensor.transpose(turned[:, (e - e0) * C : (e - e0 + 1) * C], gated[e, b], ident[:])
             nc.scalar.copy(slot_y[b][:, e0 * C : e1 * C], turned[:, 0 : (e1 - e0) * C])
 
-        def finish(b, engine, parts):
-            for i in range(parts):
-                cols = slice(i * T // parts, (i + 1) * T // parts)
+        def finish(b, engine, cuts):
+            for t0, t1 in zip(cuts, cuts[1:]):
+                cols = slice(t0, t1)
                 engine.tensor_tensor(results[b][:, cols], windows[b][:, cols], residual[:, b, cols], ADD)
                 nc.sync.dma_start(out[b * P : (b + 1) * P, cols], results[b][:, cols])
 
         for b, e0, e1 in early:
             cols = slice(e0 * C, e1 * C)
             nc.vector.tensor_tensor(windows[b][:].indirect(listed(e0, e1)), slot_y[b][:, cols], gate_wide[:, cols], MULT)
-        finish(0, nc.gpsimd, 1)
+        finish(0, nc.gpsimd, (0, T))
         for b, e0, e1 in late:
             nc.vector.tensor_copy(windows[b][:].indirect(listed(e0, e1)), slot_y[b][:, e0 * C : e1 * C])
             if b < NB - 1:
-                finish(b, nc.gpsimd, 1)
-        finish(NB - 1, nc.vector, 2)
+                finish(b, nc.gpsimd, (0, T))
+        finish(NB - 1, nc.vector, (0, T // 2, T))

@@ -6,7 +6,6 @@ from concourse.masks import make_identity
 K, T, E, C, N = 1536, 640, 4, 128, 512
 P = 128
 S = E * C
-PASSES = 3
 NB = N // P
 WIDE = 704
 
@@ -25,7 +24,7 @@ MULT = mybir.AluOpType.mult
 FLOPS = 2 * K * N * S
 BYTES = 4 * K * T + 2 * 4 * N * T + E * 512 * N * 4 + E * 1024 * N // 2 + E * 48 * N + 4 * S + 2 * 128 * S // 16
 
-VECTOR_TOKENS = (320, 176, 0, 0)
+VECTOR_TOKENS = (320, 176)
 
 
 def tile_moe_res_lin_none_kernel(tc, xT, xr, w8_words, w8_scales, w4_words, w4_scales, gate, offs, out):
@@ -47,8 +46,8 @@ def tile_moe_res_lin_none_kernel(tc, xT, xr, w8_words, w8_scales, w4_words, w4_s
         pairs = [keep.tile([P, WIDE, 2], BF16, name=f"pairs{i}") for i in range(4)]
         rounded = [keep.tile([P, T], BF16, name=f"rounded{j}") for j in range(4)]
 
-        def as_words(tile, dtype):
-            return tile[:].rearrange("p t j -> p (t j)").bitcast(dtype)
+        def pair_words(i, dtype):
+            return pairs[i][:].rearrange("p t j -> p (t j)").bitcast(dtype)
 
         nc.vector.memset(windows[0][:], 0.0)
         nc.scalar.copy(windows[1][:], windows[0][:])
@@ -56,11 +55,11 @@ def tile_moe_res_lin_none_kernel(tc, xT, xr, w8_words, w8_scales, w4_words, w4_s
         for tile in w4_planes:
             nc.vector.memset(tile[:].rearrange("p e a n -> p (e a n)").bitcast(I32), 0)
         for i in range(4):
-            nc.vector.memset(as_words(pairs[i], I32)[:, T:WIDE], 0)
+            nc.vector.memset(pair_words(i, I32)[:, T:WIDE], 0)
         nc.gpsimd.memset(gate_rows[:], 0.0)
         make_identity(nc, ident[:])
 
-        x_src = xT.rearrange("(a p u j) t -> a u p (j t)", a=PASSES, u=2, j=2)
+        x_src = xT.rearrange("(a p u j) t -> a u p (j t)", a=3, u=2, j=2)
         w8_src = w8_words.rearrange("e a p n r -> p (e a) (n r)").bitcast(I32)
         w4_src = w4_words.rearrange("e a p b -> p (e a) b").bitcast(I32)
         w8s_src = w8_scales.rearrange("e a (q r) n -> q (e a) r n", r=4).bitcast(I32)
@@ -70,7 +69,7 @@ def tile_moe_res_lin_none_kernel(tc, xT, xr, w8_words, w8_scales, w4_words, w4_s
         last_rows = [keep.tile([P, T], F32, name=f"last_row{j}", align_bytes=64) for j in range(2)]
         w8, w4 = {}, {}
 
-        def load_tokens(i):
+        def load_two_rows(i):
             nc.sync.dma_start(raw[i][:], x_src[i // 2, i % 2])
 
         def load_weights(e, n0, n1):
@@ -89,10 +88,10 @@ def tile_moe_res_lin_none_kernel(tc, xT, xr, w8_words, w8_scales, w4_words, w4_s
                 dst = tile[r:P:32, :, :, :].rearrange("q e a n -> q (e a) n")
                 nc.sync.dma_start(dst.bitcast(I32), w4s_src[r, :, 2 * e0 : 2 * e1, :])
 
-        load_tokens(0)
+        load_two_rows(0)
         nc.sync.dma_start(offsets[:], offs)
         for i in range(1, 5):
-            load_tokens(i)
+            load_two_rows(i)
         for q in range(4):
             nc.sync.dma_start(w8_planes[32 * q : 32 * q + 16, :].bitcast(I32), w8s_src[q])
         for j in range(2):
@@ -110,23 +109,19 @@ def tile_moe_res_lin_none_kernel(tc, xT, xr, w8_words, w8_scales, w4_words, w4_s
         for b0 in (0, 2):
             nc.sync.dma_start(residual[:, b0 : b0 + 2, :], xr_src[:, b0 : b0 + 2, :])
 
-        def cast(i):
-            rows = raw[i][:].rearrange("p (j t) -> p j t", j=2)
-            cut = VECTOR_TOKENS[i]
-            for copy, t0, t1 in ((nc.vector.tensor_copy, 0, cut), (nc.scalar.copy, cut, T)):
-                if t1 > t0:
-                    src = rows[:, :, t0:t1].rearrange("p j (c i) -> p c j i", i=4)
-                    dst = pairs[i][:, t0:t1, :].rearrange("p (c i) j -> p c j i", i=4)
-                    copy(dst, src)
+        gathered = [keep.tile([P, 2, S], U32, name=f"gathered{a}") for a in range(2)]
+        codes = {}
 
         def listed(e0, e1):
             return offsets[:, e0 * C // 16 : e1 * C // 16]
 
-        gathered = [keep.tile([P, 2, S], U32, name=f"gathered{a}") for a in range(2)]
-        codes = {}
+        def round_pairs(copy, i, t0, t1):
+            rows = raw[i][:].rearrange("p (j t) -> p j t", j=2)
+            src = rows[:, :, t0:t1].rearrange("p j (c i) -> p c j i", i=4)
+            copy(pairs[i][:, t0:t1, :].rearrange("p (c i) j -> p c j i", i=4), src)
 
-        def gather(a, u):
-            nc.vector.tensor_copy(gathered[a][:, u, :], as_words(pairs[2 * a + u], U32).indirect(listed(0, E)))
+        def gather_pairs(i):
+            nc.vector.tensor_copy(gathered[i // 2][:, i % 2, :], pair_words(i, U32).indirect(listed(0, E)))
 
         def weave(copy, dtype, a, e0, e1, into):
             dst = into.bitcast(dtype).rearrange("p (c i u) -> p c u i", i=4, u=2)
@@ -139,51 +134,54 @@ def tile_moe_res_lin_none_kernel(tc, xT, xr, w8_words, w8_scales, w4_words, w4_s
                 cols = slice((e - e0) * C, (e - e0 + 1) * C)
                 codes[a, e] = (words[:, cols].bitcast(FP8X4), plane[:, cols])
 
-        def gather_last(e, tag):
-            values = keep.tile([P, C, 4], BF16, name=f"last{e}", tag=tag, align_bytes=64)
-            for j in range(4):
+        def gather_rows(values, e, rows):
+            for j in rows:
                 nc.scalar.activation(values[:, :, j], rounded[j][:].indirect(listed(e, e + 1)), COPY)
-            return values
 
-        def quantise_last(e, values):
+        def quantise_pass2(e, values):
             words = keep.tile([P, C], U32, name=f"words2_{e}", align_bytes=64)
             quantise(2, e, e + 1, values[:].rearrange("p s j -> p (s j)"), words[:])
 
-        woven = [keep.tile([P, 12 * C], BF16, name="woven0", align_bytes=64)]
-        for i in range(4):
-            cast(i)
-            gather(i // 2, i % 2)
-            if i < 2:
-                window = keep.tile([P, T], F32, name=f"window{2 + i}", tag=f"raw{i}", align_bytes=64)
-                nc.gpsimd.memset(window[:], 0.0)
-                windows.append(window)
-            if i == 1:
-                weave(nc.vector.tensor_copy, I32, 0, 0, 3, woven[0][:])
-            if i == 2:
-                woven0_late = keep.tile([P, 4 * C], BF16, name="woven0_late", tag="raw2", align_bytes=64)
-                weave(nc.gpsimd.tensor_copy, I32, 0, 3, E, woven0_late[:])
+        def pass2_on_scalar(e, tag):
+            values = keep.tile([P, C, 4], BF16, name=f"last{e}", tag=tag, align_bytes=64)
+            gather_rows(values, e, range(4))
+            quantise_pass2(e, values)
+
+        woven0 = keep.tile([P, 4 * S], BF16, name="woven0", align_bytes=64)
+        for i in range(2):
+            round_pairs(nc.vector.tensor_copy, i, 0, VECTOR_TOKENS[i])
+            round_pairs(nc.scalar.copy, i, VECTOR_TOKENS[i], T)
+            gather_pairs(i)
+            window = keep.tile([P, T], F32, name=f"window{2 + i}", tag=f"raw{i}", align_bytes=64)
+            nc.gpsimd.memset(window[:], 0.0)
+            windows.append(window)
+        weave(nc.vector.tensor_copy, I32, 0, 0, E, woven0[:])
+
+        for i in range(2, 4):
+            round_pairs(nc.scalar.copy, i, 0, T)
+            gather_pairs(i)
+
         nc.gpsimd.tensor_copy(rounded[0][:], raw[4][:, 0:T])
         nc.scalar.copy(rounded[1][:], raw[4][:, T : 2 * T])
         last0 = keep.tile([P, C, 4], BF16, name="last0", align_bytes=64)
-        for j in range(2):
-            nc.scalar.activation(last0[:, :, j], rounded[j][:].indirect(listed(0, 1)), COPY)
-        groups = ((0, 1), (1, 2), (2, E))
-        woven.append(keep.tile([P, 4 * C], BF16, name="woven1", tag="raw4", align_bytes=64))
-        weave(nc.scalar.copy, U32, 1, 0, 1, woven[1][:])
+        gather_rows(last0, 0, range(2))
+        woven1_first = keep.tile([P, 4 * C], BF16, name="woven1_first", tag="raw4", align_bytes=64)
+        weave(nc.scalar.copy, U32, 1, 0, 1, woven1_first[:])
         for j in range(2):
             nc.vector.tensor_copy(last0[:, :, 2 + j], last_rows[j][:].indirect(listed(0, 1)))
             nc.gpsimd.tensor_copy(rounded[2 + j][:], last_rows[j][:])
-        quantise_last(0, last0)
-        early_words = keep.tile([P, 2, S], U32, name="early_words", tag="last_row1", align_bytes=64)
-        quantise(1, 0, 1, woven[1][:, 0 : 4 * C], early_words[:, 1, 0:C])
-        quantise(0, 0, 1, woven[0][:, 0 : 4 * C], early_words[:, 0, 0:C])
-        quantise(0, 1, 3, woven[0][:, 4 * C : 12 * C], early_words[:, 0, C : 3 * C])
-        woven_late = keep.tile([P, 12 * C], BF16, name="woven_late", tag="raw4", align_bytes=64)
-        weave(nc.vector.tensor_copy, I32, 1, 1, E, woven_late[:])
-        quantise(0, 3, E, woven0_late[:], early_words[:, 0, 3 * C : S])
-        quantise(1, 1, 3, woven_late[:, 0 : 8 * C], early_words[:, 1, C : 3 * C])
-        quantise(1, 3, E, woven_late[:, 8 * C : 12 * C], early_words[:, 1, 3 * C : S])
-        quantise_last(2, gather_last(2, "last2"))
+        quantise_pass2(0, last0)
+
+        words01 = keep.tile([P, 2, S], U32, name="words01", tag="last_row1", align_bytes=64)
+        quantise(1, 0, 1, woven1_first[:], words01[:, 1, 0:C])
+        quantise(0, 0, 1, woven0[:, 0 : 4 * C], words01[:, 0, 0:C])
+        quantise(0, 1, 3, woven0[:, 4 * C : 12 * C], words01[:, 0, C : 3 * C])
+        woven1_rest = keep.tile([P, 12 * C], BF16, name="woven1_rest", tag="raw4", align_bytes=64)
+        weave(nc.vector.tensor_copy, I32, 1, 1, E, woven1_rest[:])
+        quantise(0, 3, E, woven0[:, 12 * C : 16 * C], words01[:, 0, 3 * C : S])
+        quantise(1, 1, 3, woven1_rest[:, 0 : 8 * C], words01[:, 1, C : 3 * C])
+        quantise(1, 3, E, woven1_rest[:, 8 * C : 12 * C], words01[:, 1, 3 * C : S])
+        pass2_on_scalar(2, "last2")
 
         turned_gate = psum.tile([P, N], F32, name="turned_gate", tag="turned", bufs=2)
         nc.tensor.transpose(turned_gate[:, 0:P], gate_rows[:], ident[:])
@@ -192,12 +190,12 @@ def tile_moe_res_lin_none_kernel(tc, xT, xr, w8_words, w8_scales, w4_words, w4_s
 
         def multiply(e, b, sums, tokens_move):
             n0, n1 = b * P, (b + 1) * P
-            plane, place = (w4_planes[0], 0) if e == 0 else (w4_planes[1], e - 1)
+            planes, place = (w4_planes[0], 0) if e == 0 else (w4_planes[1], e - 1)
             for a in (2, 1, 0):
                 if a == 0:
                     matrix = w8[e, b], w8_planes[4 * e : P, n0:n1]
                 else:
-                    matrix = w4[e, a, b], plane[:, place, a - 1, n0:n1]
+                    matrix = w4[e, a, b], planes[:, place, a - 1, n0:n1]
                 still, moving = (matrix, codes[a, e]) if tokens_move else (codes[a, e], matrix)
                 nc.tensor.matmul_mx(
                     out=sums,
@@ -209,7 +207,7 @@ def tile_moe_res_lin_none_kernel(tc, xT, xr, w8_words, w8_scales, w4_words, w4_s
                     stop=(a == 0),
                 )
 
-        early = [(b, 0, 1) for b in range(NB)] + [(b, 2, 3) for b in range(2)] + [(b, 1, 2) for b in range(3)] + [(0, 3, 4)]
+        early = [(b, e) for e, blocks in ((0, 4), (2, 2), (1, 3), (3, 1)) for b in range(blocks)]
         late = [(1, 3, E), (2, 2, E), (3, 1, E)]
         gated = {}
 
@@ -223,16 +221,15 @@ def tile_moe_res_lin_none_kernel(tc, xT, xr, w8_words, w8_scales, w4_words, w4_s
             for b in range(b0, NB):
                 gated[e, b] = tile[:, (b - b0) * P : (b - b0 + 1) * P]
 
-        for i, (b, e0, e1) in enumerate(early):
-            if (b, e0) == (0, 2):
-                quantise_last(1, gather_last(1, "w8_0_256"))
-            if (b, e0) == (0, 1):
+        for i, (b, e) in enumerate(early):
+            if (b, e) == (0, 2):
+                pass2_on_scalar(1, f"w8_0_{N // 2}")
+            if (b, e) == (0, 1):
                 multiply_late(2)
-                quantise_last(3, gather_last(3, "w8_2_0"))
+                pass2_on_scalar(3, "w8_2_0")
             bank = psum.tile([P, N], F32, name=f"early{i}", tag=f"early{i % 4}")
-            for e in range(e0, e1):
-                multiply(e, b, bank[:, (e - e0) * C : (e - e0 + 1) * C], True)
-            nc.scalar.copy(slot_y[b][:, e0 * C : e1 * C], bank[:, 0 : (e1 - e0) * C])
+            multiply(e, b, bank[:, 0:C], True)
+            nc.scalar.copy(slot_y[b][:, e * C : (e + 1) * C], bank[:, 0:C])
 
         for e in (1, 3):
             multiply_late(e)
@@ -242,18 +239,18 @@ def tile_moe_res_lin_none_kernel(tc, xT, xr, w8_words, w8_scales, w4_words, w4_s
                 nc.tensor.transpose(turned[:, (e - e0) * C : (e - e0 + 1) * C], gated[e, b], ident[:])
             nc.scalar.copy(slot_y[b][:, e0 * C : e1 * C], turned[:, 0 : (e1 - e0) * C])
 
-        def finish(b, engine, cuts):
-            for t0, t1 in zip(cuts, cuts[1:]):
-                cols = slice(t0, t1)
+        def finish(b, engine, parts):
+            for i in range(parts):
+                cols = slice(i * T // parts, (i + 1) * T // parts)
                 engine.tensor_tensor(results[b][:, cols], windows[b][:, cols], residual[:, b, cols], ADD)
                 nc.sync.dma_start(out[b * P : (b + 1) * P, cols], results[b][:, cols])
 
-        for b, e0, e1 in early:
-            cols = slice(e0 * C, e1 * C)
-            nc.vector.tensor_tensor(windows[b][:].indirect(listed(e0, e1)), slot_y[b][:, cols], gate_wide[:, cols], MULT)
-        finish(0, nc.gpsimd, (0, T))
+        for b, e in early:
+            cols = slice(e * C, (e + 1) * C)
+            nc.vector.tensor_tensor(windows[b][:].indirect(listed(e, e + 1)), slot_y[b][:, cols], gate_wide[:, cols], MULT)
+        finish(0, nc.gpsimd, 1)
         for b, e0, e1 in late:
             nc.vector.tensor_copy(windows[b][:].indirect(listed(e0, e1)), slot_y[b][:, e0 * C : e1 * C])
             if b < NB - 1:
-                finish(b, nc.gpsimd, (0, T))
-        finish(NB - 1, nc.vector, (0, T // 2, T))
+                finish(b, nc.gpsimd, 1)
+        finish(NB - 1, nc.vector, 2)

@@ -116,16 +116,15 @@ def tile_moe_res_lin_none_kernel(tc, xT, xr, w8_words, w8_scales, w4_words, w4_s
             return offsets[:, e0 * C // 16 : e1 * C // 16]
 
         def round_pairs(copy, i, t0, t1):
-            rows = raw[i][:].rearrange("p (j t) -> p j t", j=2)
-            src = rows[:, :, t0:t1].rearrange("p j (c i) -> p c j i", i=4)
-            copy(pairs[i][:, t0:t1, :].rearrange("p (c i) j -> p c j i", i=4), src)
+            rows = raw[i][:].rearrange("p (j t) -> p t j", j=2)
+            copy(pairs[i][:, t0:t1, :], rows[:, t0:t1, :])
 
         def gather_pairs(i):
             nc.vector.tensor_copy(gathered[i // 2][:, i % 2, :], pair_words(i, U32).indirect(listed(0, E)))
 
         def weave(copy, dtype, a, e0, e1, into):
-            dst = into.bitcast(dtype).rearrange("p (c i u) -> p c u i", i=4, u=2)
-            copy(dst, gathered[a][:, :, e0 * C : e1 * C].bitcast(dtype).rearrange("p u (c i) -> p c u i", i=4))
+            dst = into.bitcast(dtype).rearrange("p (s u) -> p s u", u=2)
+            copy(dst, gathered[a][:, :, e0 * C : e1 * C].bitcast(dtype).rearrange("p u s -> p s u"))
 
         def quantise(a, e0, e1, values, words):
             plane = keep.tile([P, (e1 - e0) * C], U8, name=f"plane{a}_{e0}", align_bytes=64)

@@ -24,7 +24,7 @@ MULT = mybir.AluOpType.mult
 FLOPS = 2 * K * N * S
 BYTES = 4 * K * T + 2 * 4 * N * T + E * 512 * N * 4 + E * 1024 * N // 2 + E * 48 * N + 4 * S + 2 * 128 * S // 16
 
-VECTOR_TOKENS = (320, 176)
+VECTOR_TOKENS = (384, 208)
 
 
 def tile_moe_res_lin_none_kernel(tc, xT, xr, w8_words, w8_scales, w4_words, w4_scales, gate, offs, out):
@@ -106,8 +106,7 @@ def tile_moe_res_lin_none_kernel(tc, xT, xr, w8_words, w8_scales, w4_words, w4_s
         nc.sync.dma_start(gate_rows[0:E, :], gate[0:1, :].rearrange("o (e c) -> (o e) c", c=C))
         load_weights(1, 0, N)
         load_weights(3, 0, N)
-        for b0 in (0, 2):
-            nc.sync.dma_start(residual[:, b0 : b0 + 2, :], xr_src[:, b0 : b0 + 2, :])
+        nc.sync.dma_start(residual[:], xr_src)
 
         gathered = [keep.tile([P, 2, S], U32, name=f"gathered{a}") for a in range(2)]
         codes = {}
@@ -168,7 +167,7 @@ def tile_moe_res_lin_none_kernel(tc, xT, xr, w8_words, w8_scales, w4_words, w4_s
         weave(nc.scalar.copy, U32, 1, 0, 1, woven1_first[:])
         for j in range(2):
             nc.vector.tensor_copy(last0[:, :, 2 + j], last_rows[j][:].indirect(listed(0, 1)))
-            nc.gpsimd.tensor_copy(rounded[2 + j][:], last_rows[j][:])
+            (nc.gpsimd, nc.vector)[j].tensor_copy(rounded[2 + j][:], last_rows[j][:])
         quantise_pass2(0, last0)
 
         words01 = keep.tile([P, 2, S], U32, name="words01", tag="last_row1", align_bytes=64)

@@ -7,7 +7,6 @@ K, T, E, C, N = 1536, 640, 4, 128, 512
 P = 128
 S = E * C
 NB = N // P
-WIDE = 704
 
 F32 = mybir.dt.float32
 BF16 = mybir.dt.bfloat16
@@ -24,7 +23,8 @@ MULT = mybir.AluOpType.mult
 FLOPS = 2 * K * N * S
 BYTES = 4 * K * T + 2 * 4 * N * T + E * 512 * N * 4 + E * 1024 * N // 2 + E * 48 * N + 4 * S + 2 * 128 * S // 16
 
-VECTOR_TOKENS = (384, 208)
+WIDE = 704
+CUT = 384
 
 
 def tile_moe_res_lin_none_kernel(tc, xT, xr, w8_words, w8_scales, w4_words, w4_scales, gate, offs, out):
@@ -35,220 +35,202 @@ def tile_moe_res_lin_none_kernel(tc, xT, xr, w8_words, w8_scales, w4_words, w4_s
 
         offsets = keep.tile([P, S // 16], U16, name="offsets")
         w4_planes = [keep.tile([P, n, 2, N], U8, name=f"w4_planes{n}", align_bytes=64) for n in (1, E - 1)]
-        w8_planes = keep.tile([P, N], U8, name="w8_planes", align_bytes=64)
-        residual = keep.tile([P, NB, T], F32, name="residual")
+        w8_planes = [keep.tile([P, N], U8, name=f"w8_planes{h}", align_bytes=64) for h in range(2)]
+        residual = [keep.tile([P, 2, T], F32, name=f"residual{h}") for h in range(2)]
         gate_rows = keep.tile([P, P], F32, name="gate_rows")
-        gate_wide = keep.tile([P, S], F32, name="gate_wide")
         ident = keep.tile([P, P], F32, name="ident")
-        windows = [keep.tile([P, T], F32, name=f"window{b}") for b in range(2)]
-        slot_y = [keep.tile([P, S], F32, name=f"slot_y{b}") for b in range(NB)]
+        windows = [keep.tile([P, T], F32, name=f"window{b}") for b in range(NB)]
         results = [keep.tile([P, T], F32, name=f"result{b}") for b in range(NB)]
-        pairs = [keep.tile([P, WIDE, 2], BF16, name=f"pairs{i}") for i in range(4)]
-        rounded = [keep.tile([P, T], BF16, name=f"rounded{j}") for j in range(4)]
+        grouped = {a: keep.tile([P, 4 * T], BF16, name=f"grouped{a}", align_bytes=64) for a in range(3)}
+        words = {a: keep.tile([P, WIDE if a == 1 else T], U32, name=f"words{a}", align_bytes=64) for a in range(3)}
+        plane1 = keep.tile([P, WIDE], U8, name="plane1", align_bytes=64)
+        plane02 = keep.tile([P, T], U8, name="plane02", align_bytes=64)
 
-        def pair_words(i, dtype):
-            return pairs[i][:].rearrange("p t j -> p (t j)").bitcast(dtype)
-
-        nc.vector.memset(windows[0][:], 0.0)
-        nc.scalar.copy(windows[1][:], windows[0][:])
-        nc.vector.memset(w8_planes[:].bitcast(I32), 0)
-        for tile in w4_planes:
-            nc.vector.memset(tile[:].rearrange("p e a n -> p (e a n)").bitcast(I32), 0)
-        for i in range(4):
-            nc.vector.memset(pair_words(i, I32)[:, T:WIDE], 0)
         nc.gpsimd.memset(gate_rows[:], 0.0)
         make_identity(nc, ident[:])
+        nc.vector.memset(windows[0][:], 0.0)
+        nc.scalar.activation(windows[1][:], windows[0][:], COPY)
+        for tile in w8_planes + [plane1, plane02]:
+            nc.vector.memset(tile[:].bitcast(I32), 0)
+        for tile in w4_planes:
+            nc.vector.memset(tile[:].rearrange("p e a n -> p (e a n)").bitcast(I32), 0)
+        nc.vector.memset(words[1][:].bitcast(I32)[:, T:WIDE], 0)
+        for b in (2, 3):
+            nc.gpsimd.memset(windows[b][:], 0.0)
 
-        x_src = xT.rearrange("(a p u j) t -> a u p (j t)", a=3, u=2, j=2)
+        x_src = xT.rearrange("(a p u j) t -> a u p j t", a=3, u=2, j=2)
         w8_src = w8_words.rearrange("e a p n r -> p (e a) (n r)").bitcast(I32)
         w4_src = w4_words.rearrange("e a p b -> p (e a) b").bitcast(I32)
         w8s_src = w8_scales.rearrange("e a (q r) n -> q (e a) r n", r=4).bitcast(I32)
         w4s_src = w4_scales.rearrange("e a (q r) n -> r q (e a) n", r=4).bitcast(I32)
         xr_src = xr.rearrange("(b p) t -> p b t", p=P)
-        raw = [keep.tile([P, 2 * T], F32, name=f"raw{i}", align_bytes=64) for i in range(5)]
-        last_rows = [keep.tile([P, T], F32, name=f"last_row{j}", align_bytes=64) for j in range(2)]
-        w8, w4 = {}, {}
+        raw, w8, w4 = {}, {}, {}
 
-        def load_two_rows(i):
-            nc.sync.dma_start(raw[i][:], x_src[i // 2, i % 2])
+        for a in range(3):
+            raw[a] = keep.tile([P, 4 * T], F32, name=f"raw{a}", align_bytes=64)[:].rearrange("p (j t) -> p j t", j=4)
+        early_rows = keep.tile([P, 2, CUT], F32, name="early_rows", align_bytes=64)
 
-        def load_weights(e, n0, n1):
-            tile4 = keep.tile([P, 2, 2 * (n1 - n0)], U8, name=f"w4_{e}_{n0}", align_bytes=64)
-            nc.sync.dma_start(tile4[:].bitcast(I32), w4_src[:, 2 * e : 2 * e + 2, n0 // 2 : n1 // 2])
-            tile8 = keep.tile([P, 4 * (n1 - n0)], U8, name=f"w8_{e}_{n0}", align_bytes=64)
-            nc.sync.dma_start(tile8[:].bitcast(I32), w8_src[:, e, n0:n1])
-            for b in range(n0 // P, n1 // P):
-                first = b * P - n0
-                w8[e, b] = tile8[:, 4 * first : 4 * (first + P)].bitcast(FP8X4)
-                for a in (1, 2):
-                    w4[e, a, b] = tile4[:, a - 1, 2 * first : 2 * (first + P)].bitcast(FP4X4)
+        def load_rows(a, u, t0, t1):
+            nc.sync.dma_start(raw[a][:, 2 * u : 2 * u + 2, t0:t1], x_src[a, u][:, :, t0:t1])
+
+        def load_weights(e):
+            w4[e] = keep.tile([P, 2, 2 * N], U8, name=f"w4_{e}", align_bytes=64)
+            nc.sync.dma_start(w4[e][:].bitcast(I32), w4_src[:, 2 * e : 2 * e + 2, :])
+            w8[e] = keep.tile([P, 4 * N], U8, name=f"w8_{e}", align_bytes=64)
+            nc.sync.dma_start(w8[e][:].bitcast(I32), w8_src[:, e, :])
 
         def load_w4_scales(tile, e0, e1):
             for r in range(4):
                 dst = tile[r:P:32, :, :, :].rearrange("q e a n -> q (e a) n")
                 nc.sync.dma_start(dst.bitcast(I32), w4s_src[r, :, 2 * e0 : 2 * e1, :])
 
-        load_two_rows(0)
-        nc.sync.dma_start(offsets[:], offs)
-        for i in range(1, 5):
-            load_two_rows(i)
-        for q in range(4):
-            nc.sync.dma_start(w8_planes[32 * q : 32 * q + 16, :].bitcast(I32), w8s_src[q])
-        for j in range(2):
-            nc.sync.dma_start(last_rows[j][:], x_src[2, 1][:, j * T : (j + 1) * T])
-        load_w4_scales(w4_planes[0], 0, 1)
-        load_weights(0, 0, N // 2)
-        nc.sync.dma_start(gate_wide[:, 0:C], gate[0:P, 0:C])
-        load_weights(0, N // 2, N)
-        load_w4_scales(w4_planes[1], 1, E)
-        load_weights(2, 0, N)
-        nc.sync.dma_start(gate_wide[:, C:S], gate[0:P, C:S])
-        nc.sync.dma_start(gate_rows[0:E, :], gate[0:1, :].rearrange("o (e c) -> (o e) c", c=C))
-        load_weights(1, 0, N)
-        load_weights(3, 0, N)
-        nc.sync.dma_start(residual[:], xr_src)
+        def load_w8_scales(h):
+            for q in range(4):
+                nc.sync.dma_start(w8_planes[h][32 * q : 32 * q + 8, :].bitcast(I32), w8s_src[q, 2 * h : 2 * h + 2])
 
-        gathered = [keep.tile([P, 2, S], U32, name=f"gathered{a}") for a in range(2)]
-        codes = {}
+        nc.sync.dma_start(gate_rows[0:E, :], gate[0:1, :].rearrange("o (e c) -> (o e) c", c=C))
+        load_rows(1, 0, 0, T)
+        load_rows(1, 1, 0, T)
+        nc.sync.dma_start(offsets[:], offs)
+        load_rows(0, 0, 0, T)
+        load_w8_scales(0)
+        load_rows(0, 1, 0, T)
+        load_rows(2, 0, 0, T)
+        nc.sync.dma_start(early_rows[:], x_src[2, 1][:, :, 0:CUT])
+        load_rows(2, 1, CUT, T)
+        load_w4_scales(w4_planes[0], 0, 1)
+        load_weights(0)
+        load_w4_scales(w4_planes[1], 1, E)
+        load_weights(1)
+        load_w8_scales(1)
+        load_weights(2)
+        load_weights(3)
+        for h in range(2):
+            nc.sync.dma_start(residual[h][:], xr_src[:, 2 * h : 2 * h + 2, :])
+
+        bank = psum.tile([P, N], F32, name="gate_turned", tag="bank6")
+        nc.tensor.transpose(bank[:, 0:P], gate_rows[:], ident[:])
+        gate_cols = keep.tile([P, E], F32, name="gate_cols")
+        nc.scalar.copy(gate_cols[:], bank[:, 0:E])
+        bank = psum.tile([P, N], F32, name="gate_spread", tag="bank7")
+        for e in range(E):
+            nc.tensor.transpose(bank[:, e * C : (e + 1) * C], gate_cols[:, e : e + 1].to_broadcast([P, P]), ident[:])
+        gate_bank = bank
 
         def listed(e0, e1):
             return offsets[:, e0 * C // 16 : e1 * C // 16]
 
-        def round_pairs(copy, i, t0, t1):
-            rows = raw[i][:].rearrange("p (j t) -> p t j", j=2)
-            copy(pairs[i][:, t0:t1, :], rows[:, t0:t1, :])
+        def round_pair(a, u, rows, t0, t1):
+            dst = grouped[a][:].rearrange("p (t j) -> p t j", j=4)[:, t0:t1, 2 * u : 2 * u + 2]
+            nc.scalar.copy(dst, rows[:, :, t0:t1].rearrange("p j t -> p t j"))
 
-        def gather_pairs(i):
-            nc.vector.tensor_copy(gathered[i // 2][:, i % 2, :], pair_words(i, U32).indirect(listed(0, E)))
+        def round_four(a, t0, t1, engine=nc.vector):
+            dst = grouped[a][:, 4 * t0 : 4 * t1].rearrange("p (t j) -> p t j", j=4)
+            engine.tensor_copy(dst, raw[a][:, :, t0:t1].rearrange("p j t -> p t j"))
 
-        def weave(copy, dtype, a, e0, e1, into):
-            dst = into.bitcast(dtype).rearrange("p (s u) -> p s u", u=2)
-            copy(dst, gathered[a][:, :, e0 * C : e1 * C].bitcast(dtype).rearrange("p u s -> p s u"))
+        def quantise(a, t0, t1):
+            scales = {0: plane02[4:P, t0:t1], 1: plane1[:, t0:t1], 2: plane02[:, t0:t1]}[a]
+            nc.vector.quantize_mx(out=words[a][:, t0:t1].bitcast(FP8X4), scales=scales, in_=grouped[a][:, 4 * t0 : 4 * t1])
 
-        def quantise(a, e0, e1, values, words):
-            plane = keep.tile([P, (e1 - e0) * C], U8, name=f"plane{a}_{e0}", align_bytes=64)
-            nc.vector.quantize_mx(out=words.bitcast(FP8X4), scales=plane[:], in_=values)
-            for e in range(e0, e1):
-                cols = slice((e - e0) * C, (e - e0 + 1) * C)
-                codes[a, e] = (words[:, cols].bitcast(FP8X4), plane[:, cols])
+        codes, scale_of = {}, {}
 
-        def gather_rows(values, e, rows):
-            for j in rows:
-                nc.scalar.activation(values[:, :, j], rounded[j][:].indirect(listed(e, e + 1)), COPY)
+        def gather_words(passes, e0, e1, tag=None):
+            name = f"slot_words{passes[0]}_{e0}"
+            tile = keep.tile([P, len(passes), (e1 - e0) * C], U32, name=name, tag=tag or name, align_bytes=64)
+            for i, a in enumerate(passes):
+                nc.vector.tensor_copy(tile[:, i, :], words[a][:].indirect(listed(e0, e1)))
+                for e in range(e0, e1):
+                    codes[a, e] = tile[:, i, (e - e0) * C : (e - e0 + 1) * C].bitcast(FP8X4)
 
-        def quantise_pass2(e, values):
-            words = keep.tile([P, C], U32, name=f"words2_{e}", align_bytes=64)
-            quantise(2, e, e + 1, values[:].rearrange("p s j -> p (s j)"), words[:])
+        def gather_bytes(passes, e0, e1, tag=None):
+            name = f"slot_bytes{passes[0]}_{e0}"
+            tile = keep.tile([P, (e1 - e0) * C], U8, name=name, tag=tag or name, align_bytes=64)
+            nc.vector.tensor_copy(tile[:], (plane1 if passes == (1,) else plane02)[:].indirect(listed(e0, e1)))
+            for a in passes:
+                for e in range(e0, e1):
+                    scale_of[a, e] = tile[4 if a == 0 else 0 : P, (e - e0) * C : (e - e0 + 1) * C]
 
-        def pass2_on_scalar(e, tag):
-            values = keep.tile([P, C, 4], BF16, name=f"last{e}", tag=tag, align_bytes=64)
-            gather_rows(values, e, range(4))
-            quantise_pass2(e, values)
+        for u in range(2):
+            round_pair(1, u, raw[1][:, 2 * u : 2 * u + 2, :], 0, 320)
+        round_four(1, 320, T)
+        quantise(1, 0, 256)
+        quantise(1, 256, T)
+        gather_words((1,), 0, E)
+        gather_bytes((1,), 0, E)
+        for u in range(2):
+            round_pair(0, u, raw[0][:, 2 * u : 2 * u + 2, :], 0, 480)
+        round_four(0, 480, T, nc.gpsimd)
+        quantise(0, 0, 128)
+        quantise(0, 128, T)
+        gather_words((0,), 0, 1)
+        round_pair(2, 0, raw[2][:, 0:2, :], 0, CUT)
+        round_pair(2, 1, early_rows[:], 0, CUT)
+        gate_wide = keep.tile([P, S], F32, name="gate_wide", tag="early_rows", align_bytes=64)
+        nc.scalar.copy(gate_wide[:], gate_bank[:])
+        round_four(2, CUT, T)
+        quantise(2, CUT, T)
+        quantise(2, 0, CUT)
+        gather_bytes((0, 2), 0, 1)
+        gather_words((2,), 0, 1)
+        gather_bytes((0, 2), 1, E)
 
-        woven0 = keep.tile([P, 4 * S], BF16, name="woven0", align_bytes=64)
-        for i in range(2):
-            round_pairs(nc.vector.tensor_copy, i, 0, VECTOR_TOKENS[i])
-            round_pairs(nc.scalar.copy, i, VECTOR_TOKENS[i], T)
-            gather_pairs(i)
-            window = keep.tile([P, T], F32, name=f"window{2 + i}", tag=f"raw{i}", align_bytes=64)
-            nc.gpsimd.memset(window[:], 0.0)
-            windows.append(window)
-        weave(nc.vector.tensor_copy, I32, 0, 0, E, woven0[:])
+        slot_y = {}
 
-        for i in range(2, 4):
-            round_pairs(nc.scalar.copy, i, 0, T)
-            gather_pairs(i)
-
-        nc.gpsimd.tensor_copy(rounded[0][:], raw[4][:, 0:T])
-        nc.scalar.copy(rounded[1][:], raw[4][:, T : 2 * T])
-        last0 = keep.tile([P, C, 4], BF16, name="last0", align_bytes=64)
-        gather_rows(last0, 0, range(2))
-        woven1_first = keep.tile([P, 4 * C], BF16, name="woven1_first", tag="raw4", align_bytes=64)
-        weave(nc.scalar.copy, U32, 1, 0, 1, woven1_first[:])
-        for j in range(2):
-            nc.vector.tensor_copy(last0[:, :, 2 + j], last_rows[j][:].indirect(listed(0, 1)))
-            (nc.gpsimd, nc.vector)[j].tensor_copy(rounded[2 + j][:], last_rows[j][:])
-        quantise_pass2(0, last0)
-
-        words01 = keep.tile([P, 2, S], U32, name="words01", tag="last_row1", align_bytes=64)
-        quantise(1, 0, 1, woven1_first[:], words01[:, 1, 0:C])
-        quantise(0, 0, 1, woven0[:, 0 : 4 * C], words01[:, 0, 0:C])
-        quantise(0, 1, 3, woven0[:, 4 * C : 12 * C], words01[:, 0, C : 3 * C])
-        woven1_rest = keep.tile([P, 12 * C], BF16, name="woven1_rest", tag="raw4", align_bytes=64)
-        weave(nc.vector.tensor_copy, I32, 1, 1, E, woven1_rest[:])
-        quantise(0, 3, E, woven0[:, 12 * C : 16 * C], words01[:, 0, 3 * C : S])
-        quantise(1, 1, 3, woven1_rest[:, 0 : 8 * C], words01[:, 1, C : 3 * C])
-        quantise(1, 3, E, woven1_rest[:, 8 * C : 12 * C], words01[:, 1, 3 * C : S])
-        pass2_on_scalar(2, "last2")
-
-        turned_gate = psum.tile([P, N], F32, name="turned_gate", tag="turned", bufs=2)
-        nc.tensor.transpose(turned_gate[:, 0:P], gate_rows[:], ident[:])
-        gate_cols = keep.tile([P, E], F32, name="gate_cols")
-        nc.scalar.copy(gate_cols[:], turned_gate[:, 0:E])
-
-        def multiply(e, b, sums, tokens_move):
-            n0, n1 = b * P, (b + 1) * P
+        def multiply(e, blocks, tag):
+            bank = psum.tile([P, N], F32, name=f"sums{e}_{blocks[0]}", tag=tag)
             planes, place = (w4_planes[0], 0) if e == 0 else (w4_planes[1], e - 1)
-            for a in (2, 1, 0):
-                if a == 0:
-                    matrix = w8[e, b], w8_planes[4 * e : P, n0:n1]
-                else:
-                    matrix = w4[e, a, b], planes[:, place, a - 1, n0:n1]
-                still, moving = (matrix, codes[a, e]) if tokens_move else (codes[a, e], matrix)
-                nc.tensor.matmul_mx(
-                    out=sums,
-                    lhsT=still[0],
-                    lhsT_scale=still[1],
-                    rhs=moving[0],
-                    rhs_scale=moving[1],
-                    start=(a == 2),
-                    stop=(a == 0),
-                )
+            for a in (1, 0, 2):
+                for i, b in enumerate(blocks):
+                    n0, n1 = b * P, (b + 1) * P
+                    if a == 0:
+                        matrix = w8[e][:, 4 * n0 : 4 * n1].bitcast(FP8X4), w8_planes[e // 2][4 * (e % 2) : P, n0:n1]
+                    else:
+                        matrix = w4[e][:, a - 1, 2 * n0 : 2 * n1].bitcast(FP4X4), planes[:, place, a - 1, n0:n1]
+                    nc.tensor.matmul_mx(
+                        out=bank[:, i * C : (i + 1) * C],
+                        lhsT=matrix[0],
+                        lhsT_scale=matrix[1],
+                        rhs=codes[a, e],
+                        rhs_scale=scale_of[a, e],
+                        start=(a == 1 and i == 0),
+                        stop=(a == 2 and i == len(blocks) - 1),
+                    )
+            tile = keep.tile([P, len(blocks), C], F32, name=f"slot_y{e}_{blocks[0]}")
+            weights = gate_wide[:, e * C : (e + 1) * C].unsqueeze(1).to_broadcast([P, len(blocks), C])
+            nc.vector.tensor_tensor(tile[:], bank[:, 0 : len(blocks) * C].rearrange("p (b c) -> p b c", c=C), weights, MULT)
+            for i, b in enumerate(blocks):
+                slot_y[b, e] = tile[:, i, :]
 
-        early = [(b, e) for e, blocks in ((0, 4), (2, 2), (1, 3), (3, 1)) for b in range(blocks)]
-        late = [(1, 3, E), (2, 2, E), (3, 1, E)]
-        gated = {}
+        def scatter_scalar(b, e):
+            nc.scalar.activation(windows[b][:].indirect(listed(e, e + 1)), slot_y[b, e], COPY)
 
-        def multiply_late(e):
-            b0 = min(b for b, e0, e1 in late if e0 <= e)
-            bank = psum.tile([P, N], F32, name=f"late{e}", tag=f"late{e % 2}")
-            for b in range(b0, NB):
-                multiply(e, b, bank[:, b * P : (b + 1) * P], False)
-            tile = keep.tile([P, (NB - b0) * P], F32, name=f"gated{e}")
-            nc.scalar.activation(tile[:], bank[:, b0 * P : N], COPY, scale=gate_cols[:, e : e + 1])
-            for b in range(b0, NB):
-                gated[e, b] = tile[:, (b - b0) * P : (b - b0 + 1) * P]
-
-        for i, (b, e) in enumerate(early):
-            if (b, e) == (0, 2):
-                pass2_on_scalar(1, f"w8_0_{N // 2}")
-            if (b, e) == (0, 1):
-                multiply_late(2)
-                pass2_on_scalar(3, "w8_2_0")
-            bank = psum.tile([P, N], F32, name=f"early{i}", tag=f"early{i % 4}")
-            multiply(e, b, bank[:, 0:C], True)
-            nc.scalar.copy(slot_y[b][:, e * C : (e + 1) * C], bank[:, 0:C])
-
-        for e in (1, 3):
-            multiply_late(e)
-        for b, e0, e1 in late:
-            turned = psum.tile([P, N], F32, name=f"turned{b}", tag="turned", bufs=2)
-            for e in range(e0, e1):
-                nc.tensor.transpose(turned[:, (e - e0) * C : (e - e0 + 1) * C], gated[e, b], ident[:])
-            nc.scalar.copy(slot_y[b][:, e0 * C : e1 * C], turned[:, 0 : (e1 - e0) * C])
+        def scatter_vector(b, e):
+            nc.vector.tensor_copy(windows[b][:].indirect(listed(e, e + 1)), slot_y[b, e])
 
         def finish(b, engine, parts):
             for i in range(parts):
                 cols = slice(i * T // parts, (i + 1) * T // parts)
-                engine.tensor_tensor(results[b][:, cols], windows[b][:, cols], residual[:, b, cols], ADD)
+                engine.tensor_tensor(results[b][:, cols], windows[b][:, cols], residual[b // 2][:, b % 2, cols], ADD)
                 nc.sync.dma_start(out[b * P : (b + 1) * P, cols], results[b][:, cols])
 
-        for b, e in early:
-            cols = slice(e * C, (e + 1) * C)
-            nc.vector.tensor_tensor(windows[b][:].indirect(listed(e, e + 1)), slot_y[b][:, cols], gate_wide[:, cols], MULT)
+        for b in range(NB):
+            multiply(0, (b,), f"bank{b}")
+        for b in range(NB):
+            scatter_scalar(b, 0)
+        gather_words((0, 2), 1, 2, "w4_0")
+        gather_words((0, 2), 2, E, "w8_0")
+        for i in range(6):
+            multiply(1 + i // 2, (2 * (i % 2), 2 * (i % 2) + 1), f"bank{i % 4}")
+        for e in range(1, E):
+            scatter_scalar(0, e)
         finish(0, nc.gpsimd, 1)
-        for b, e0, e1 in late:
-            nc.vector.tensor_copy(windows[b][:].indirect(listed(e0, e1)), slot_y[b][:, e0 * C : e1 * C])
-            if b < NB - 1:
-                finish(b, nc.gpsimd, 1)
-        finish(NB - 1, nc.vector, 2)
+        for e in (3, 1, 2):
+            scatter_vector(1, e)
+        finish(1, nc.gpsimd, 1)
+        scatter_scalar(3, 3)
+        for e in (3, 1, 2):
+            scatter_scalar(2, e)
+        for e in (1, 2):
+            scatter_vector(3, e)
+        finish(3, nc.vector, 1)
+        finish(2, nc.vector, 2)

from contextlib import ExitStack

import concourse.mybir as mybir
from concourse.masks import make_identity

K, T, E, C, N = 1536, 640, 4, 128, 512
P = 128
S = E * C
NB = N // P

F32 = mybir.dt.float32
BF16 = mybir.dt.bfloat16
I32 = mybir.dt.int32
U32 = mybir.dt.uint32
U16 = mybir.dt.uint16
U8 = mybir.dt.uint8
FP8X4 = mybir.dt.float8_e4m3fn_x4
FP4X4 = mybir.dt.float4_e2m1fn_x4
COPY = mybir.ActivationFunctionType.Copy
ADD = mybir.AluOpType.add
MULT = mybir.AluOpType.mult

FLOPS = 2 * K * N * S
BYTES = 4 * K * T + 2 * 4 * N * T + E * 512 * N * 4 + E * 1024 * N // 2 + E * 48 * N + 4 * S + 2 * 128 * S // 16

WIDE = 704
CUT = 384


def tile_moe_res_lin_none_kernel(tc, xT, xr, w8_words, w8_scales, w4_words, w4_scales, gate, offs, out):
    nc = tc.nc
    with ExitStack() as ctx:
        keep = ctx.enter_context(tc.tile_pool(name="keep", bufs=1))
        psum = ctx.enter_context(tc.psum_pool(name="psum", bufs=1))

        offsets = keep.tile([P, S // 16], U16, name="offsets")
        w4_planes = [keep.tile([P, n, 2, N], U8, name=f"w4_planes{n}", align_bytes=64) for n in (1, E - 1)]
        w8_planes = [keep.tile([P, N], U8, name=f"w8_planes{h}", align_bytes=64) for h in range(2)]
        residual = [keep.tile([P, 2, T], F32, name=f"residual{h}") for h in range(2)]
        gate_rows = keep.tile([P, P], F32, name="gate_rows")
        ident = keep.tile([P, P], F32, name="ident")
        windows = [keep.tile([P, T], F32, name=f"window{b}") for b in range(NB)]
        results = [keep.tile([P, T], F32, name=f"result{b}") for b in range(NB)]
        grouped = {a: keep.tile([P, 4 * T], BF16, name=f"grouped{a}", align_bytes=64) for a in range(3)}
        words = {a: keep.tile([P, WIDE if a == 1 else T], U32, name=f"words{a}", align_bytes=64) for a in range(3)}
        plane1 = keep.tile([P, WIDE], U8, name="plane1", align_bytes=64)
        plane02 = keep.tile([P, T], U8, name="plane02", align_bytes=64)

        nc.gpsimd.memset(gate_rows[:], 0.0)
        make_identity(nc, ident[:])
        nc.vector.memset(windows[0][:], 0.0)
        nc.scalar.activation(windows[1][:], windows[0][:], COPY)
        for tile in w8_planes + [plane1, plane02]:
            nc.vector.memset(tile[:].bitcast(I32), 0)
        for tile in w4_planes:
            nc.vector.memset(tile[:].rearrange("p e a n -> p (e a n)").bitcast(I32), 0)
        nc.vector.memset(words[1][:].bitcast(I32)[:, T:WIDE], 0)
        for b in (2, 3):
            nc.gpsimd.memset(windows[b][:], 0.0)

        x_src = xT.rearrange("(a p u j) t -> a u p j t", a=3, u=2, j=2)
        w8_src = w8_words.rearrange("e a p n r -> p (e a) (n r)").bitcast(I32)
        w4_src = w4_words.rearrange("e a p b -> p (e a) b").bitcast(I32)
        w8s_src = w8_scales.rearrange("e a (q r) n -> q (e a) r n", r=4).bitcast(I32)
        w4s_src = w4_scales.rearrange("e a (q r) n -> r q (e a) n", r=4).bitcast(I32)
        xr_src = xr.rearrange("(b p) t -> p b t", p=P)
        raw, w8, w4 = {}, {}, {}

        for a in range(3):
            raw[a] = keep.tile([P, 4 * T], F32, name=f"raw{a}", align_bytes=64)[:].rearrange("p (j t) -> p j t", j=4)
        early_rows = keep.tile([P, 2, CUT], F32, name="early_rows", align_bytes=64)

        def load_rows(a, u, t0, t1):
            nc.sync.dma_start(raw[a][:, 2 * u : 2 * u + 2, t0:t1], x_src[a, u][:, :, t0:t1])

        def load_weights(e):
            w4[e] = keep.tile([P, 2, 2 * N], U8, name=f"w4_{e}", align_bytes=64)
            nc.sync.dma_start(w4[e][:].bitcast(I32), w4_src[:, 2 * e : 2 * e + 2, :])
            w8[e] = keep.tile([P, 4 * N], U8, name=f"w8_{e}", align_bytes=64)
            nc.sync.dma_start(w8[e][:].bitcast(I32), w8_src[:, e, :])

        def load_w4_scales(tile, e0, e1):
            for r in range(4):
                dst = tile[r:P:32, :, :, :].rearrange("q e a n -> q (e a) n")
                nc.sync.dma_start(dst.bitcast(I32), w4s_src[r, :, 2 * e0 : 2 * e1, :])

        def load_w8_scales(h):
            for q in range(4):
                nc.sync.dma_start(w8_planes[h][32 * q : 32 * q + 8, :].bitcast(I32), w8s_src[q, 2 * h : 2 * h + 2])

        nc.sync.dma_start(gate_rows[0:E, :], gate[0:1, :].rearrange("o (e c) -> (o e) c", c=C))
        load_rows(1, 0, 0, T)
        load_rows(1, 1, 0, T)
        nc.sync.dma_start(offsets[:], offs)
        load_rows(0, 0, 0, T)
        load_w8_scales(0)
        load_rows(0, 1, 0, T)
        load_rows(2, 0, 0, T)
        nc.sync.dma_start(early_rows[:], x_src[2, 1][:, :, 0:CUT])
        load_rows(2, 1, CUT, T)
        load_w4_scales(w4_planes[0], 0, 1)
        load_weights(0)
        load_w4_scales(w4_planes[1], 1, E)
        load_weights(1)
        load_w8_scales(1)
        load_weights(2)
        load_weights(3)
        for h in range(2):
            nc.sync.dma_start(residual[h][:], xr_src[:, 2 * h : 2 * h + 2, :])

        bank = psum.tile([P, N], F32, name="gate_turned", tag="bank6")
        nc.tensor.transpose(bank[:, 0:P], gate_rows[:], ident[:])
        gate_cols = keep.tile([P, E], F32, name="gate_cols")
        nc.scalar.copy(gate_cols[:], bank[:, 0:E])
        bank = psum.tile([P, N], F32, name="gate_spread", tag="bank7")
        for e in range(E):
            nc.tensor.transpose(bank[:, e * C : (e + 1) * C], gate_cols[:, e : e + 1].to_broadcast([P, P]), ident[:])
        gate_bank = bank

        def listed(e0, e1):
            return offsets[:, e0 * C // 16 : e1 * C // 16]

        def round_pair(a, u, rows, t0, t1):
            dst = grouped[a][:].rearrange("p (t j) -> p t j", j=4)[:, t0:t1, 2 * u : 2 * u + 2]
            nc.scalar.copy(dst, rows[:, :, t0:t1].rearrange("p j t -> p t j"))

        def round_four(a, t0, t1, engine=nc.vector):
            dst = grouped[a][:, 4 * t0 : 4 * t1].rearrange("p (t j) -> p t j", j=4)
            engine.tensor_copy(dst, raw[a][:, :, t0:t1].rearrange("p j t -> p t j"))

        def quantise(a, t0, t1):
            scales = {0: plane02[4:P, t0:t1], 1: plane1[:, t0:t1], 2: plane02[:, t0:t1]}[a]
            nc.vector.quantize_mx(out=words[a][:, t0:t1].bitcast(FP8X4), scales=scales, in_=grouped[a][:, 4 * t0 : 4 * t1])

        codes, scale_of = {}, {}

        def gather_words(passes, e0, e1, tag=None):
            name = f"slot_words{passes[0]}_{e0}"
            tile = keep.tile([P, len(passes), (e1 - e0) * C], U32, name=name, tag=tag or name, align_bytes=64)
            for i, a in enumerate(passes):
                nc.vector.tensor_copy(tile[:, i, :], words[a][:].indirect(listed(e0, e1)))
                for e in range(e0, e1):
                    codes[a, e] = tile[:, i, (e - e0) * C : (e - e0 + 1) * C].bitcast(FP8X4)

        def gather_bytes(passes, e0, e1, tag=None):
            name = f"slot_bytes{passes[0]}_{e0}"
            tile = keep.tile([P, (e1 - e0) * C], U8, name=name, tag=tag or name, align_bytes=64)
            nc.vector.tensor_copy(tile[:], (plane1 if passes == (1,) else plane02)[:].indirect(listed(e0, e1)))
            for a in passes:
                for e in range(e0, e1):
                    scale_of[a, e] = tile[4 if a == 0 else 0 : P, (e - e0) * C : (e - e0 + 1) * C]

        for u in range(2):
            round_pair(1, u, raw[1][:, 2 * u : 2 * u + 2, :], 0, 320)
        round_four(1, 320, T)
        quantise(1, 0, 256)
        quantise(1, 256, T)
        gather_words((1,), 0, E)
        gather_bytes((1,), 0, E)
        for u in range(2):
            round_pair(0, u, raw[0][:, 2 * u : 2 * u + 2, :], 0, 480)
        round_four(0, 480, T, nc.gpsimd)
        quantise(0, 0, 128)
        quantise(0, 128, T)
        gather_words((0,), 0, 1)
        round_pair(2, 0, raw[2][:, 0:2, :], 0, CUT)
        round_pair(2, 1, early_rows[:], 0, CUT)
        gate_wide = keep.tile([P, S], F32, name="gate_wide", tag="early_rows", align_bytes=64)
        nc.scalar.copy(gate_wide[:], gate_bank[:])
        round_four(2, CUT, T)
        quantise(2, CUT, T)
        quantise(2, 0, CUT)
        gather_bytes((0, 2), 0, 1)
        gather_words((2,), 0, 1)
        gather_bytes((0, 2), 1, E)

        slot_y = {}

        def multiply(e, blocks, tag):
            bank = psum.tile([P, N], F32, name=f"sums{e}_{blocks[0]}", tag=tag)
            planes, place = (w4_planes[0], 0) if e == 0 else (w4_planes[1], e - 1)
            for a in (1, 0, 2):
                for i, b in enumerate(blocks):
                    n0, n1 = b * P, (b + 1) * P
                    if a == 0:
                        matrix = w8[e][:, 4 * n0 : 4 * n1].bitcast(FP8X4), w8_planes[e // 2][4 * (e % 2) : P, n0:n1]
                    else:
                        matrix = w4[e][:, a - 1, 2 * n0 : 2 * n1].bitcast(FP4X4), planes[:, place, a - 1, n0:n1]
                    nc.tensor.matmul_mx(
                        out=bank[:, i * C : (i + 1) * C],
                        lhsT=matrix[0],
                        lhsT_scale=matrix[1],
                        rhs=codes[a, e],
                        rhs_scale=scale_of[a, e],
                        start=(a == 1 and i == 0),
                        stop=(a == 2 and i == len(blocks) - 1),
                    )
            tile = keep.tile([P, len(blocks), C], F32, name=f"slot_y{e}_{blocks[0]}")
            weights = gate_wide[:, e * C : (e + 1) * C].unsqueeze(1).to_broadcast([P, len(blocks), C])
            nc.vector.tensor_tensor(tile[:], bank[:, 0 : len(blocks) * C].rearrange("p (b c) -> p b c", c=C), weights, MULT)
            for i, b in enumerate(blocks):
                slot_y[b, e] = tile[:, i, :]

        def scatter_scalar(b, e):
            nc.scalar.activation(windows[b][:].indirect(listed(e, e + 1)), slot_y[b, e], COPY)

        def scatter_vector(b, e):
            nc.vector.tensor_copy(windows[b][:].indirect(listed(e, e + 1)), slot_y[b, e])

        def finish(b, engine, parts):
            for i in range(parts):
                cols = slice(i * T // parts, (i + 1) * T // parts)
                engine.tensor_tensor(results[b][:, cols], windows[b][:, cols], residual[b // 2][:, b % 2, cols], ADD)
                nc.sync.dma_start(out[b * P : (b + 1) * P, cols], results[b][:, cols])

        for b in range(NB):
            multiply(0, (b,), f"bank{b}")
        for b in range(NB):
            scatter_scalar(b, 0)
        gather_words((0, 2), 1, 2, "w4_0")
        gather_words((0, 2), 2, E, "w8_0")
        for i in range(6):
            multiply(1 + i // 2, (2 * (i % 2), 2 * (i % 2) + 1), f"bank{i % 4}")
        for e in range(1, E):
            scatter_scalar(0, e)
        finish(0, nc.gpsimd, 1)
        for e in (3, 1, 2):
            scatter_vector(1, e)
        finish(1, nc.gpsimd, 1)
        scatter_scalar(3, 3)
        for e in (3, 1, 2):
            scatter_scalar(2, e)
        for e in (1, 2):
            scatter_vector(3, e)
        finish(3, nc.vector, 1)
        finish(2, nc.vector, 2)
